import numpy as np, ml_dtypes
CORES = [3,7,11,15,131,135,139,143]
N = 8
BF = ml_dtypes.bfloat16
def gentries(a):
    return np.ascontiguousarray(a.reshape(8, 16, -1).transpose(0, 2, 1)).reshape(8, -1)
def gtable(e):
    e = np.asarray(e); return np.ascontiguousarray(e.reshape(8, -1, 16).transpose(0, 2, 1)).reshape(128, -1).astype(np.int32)
F, S, T, LV, C, W = 864, 128, 4, 3, 7, 1760
LN, SH = (1, 2, 4), (0, 1, 2)
def parts(rng):
    th = rng.integers(0, 4096, (N, 8, 16, F)); su = rng.integers(0, F, (N, 8, 16, F)); st = rng.integers(0, F, (N, 8, LV, S))
    h = F // 8; hot = np.argsort(rng.random((N, 8, F)), axis=-1)[..., :h]
    a = np.take_along_axis(hot, rng.integers(0, h, (N, 8, 16 * F)), 2).reshape(su.shape); su = np.where(rng.random(su.shape) < 0.5, a, su)
    a = np.take_along_axis(hot, rng.integers(0, h, (N, 8, LV * S)), 2).reshape(st.shape); st = np.where(rng.random(st.shape) < 0.75, a, st)
    near = np.take_along_axis(th, rng.integers(0, F, (N, 8, 1, S)), 3)[:, :, :, None, :] + rng.integers(-600, 601, (N, 8, 16, T, S))
    xs = np.where(rng.random((N, 8, 1, 1, S)) < 0.5, np.clip(near, 0, 4095), rng.integers(0, 4096, (N, 8, 16, T, S)))
    hv = (1 + rng.random((N, 8, 16, 16))) * np.exp2(rng.integers(-1, 1, (N, 8, 16, 16)))
    return th, su, st, xs, hv
def pack(th, su, st, xs, hv):
    return {"th": np.ascontiguousarray(th.reshape(N, 128, F)).astype(np.int32), "su": np.ascontiguousarray(su.reshape(N, 128, F)).astype(np.int32),
            "st": np.stack([gtable(a.reshape(8, -1)) for a in st]), "xs": np.ascontiguousarray(xs.reshape(N, 128, T * S)).astype(np.int32),
            "hv": np.ascontiguousarray(hv.reshape(N, 128, 16)).astype(np.float32).astype(BF)}
def setup_inputs(rng):
    return pack(*parts(rng))
def setup_inputs_corners(rng):
    th, su, st, xs, hv = parts(rng); v = np.arange(F)[None, :]; i = np.arange(16)[:, None]
    for q in range(N):
        for g in range(8):
            k = (g + q) % 4; o = su[q, g].copy()
            if k == 0: su[q, g] = np.where(rng.random((1, F)) < 0.5, v, o)
            if k == 1: su[q, g] = (v + i) % F
            if k == 2: su[q, g] = np.where(o % 3 == 0, 0, np.where(o % 3 == 1, F - 1, v))
            if k == 3: su[q, g] = np.where(i == rng.integers(0, 16, (1, F)), o, o[3:4])
    e = rng.random(st.shape); st = np.where(e < 0.15, 0, np.where(e < 0.3, F - 1, st)); st[..., S - 1] = F - 1; st[..., 0] = 0
    return pack(th, su, st, xs, hv)
def setup_inputs_crowd(rng):
    th, su, st, xs, hv = parts(rng)
    for q in range(N):
        for g in range(8):
            k = (g + q) % 4; n = S if k == 3 else 3; x0 = xs[q, g].copy()
            o = rng.permutation(F)[:LV * n].reshape(LV, n); y = rng.integers(0, 4096, (16, n))
            for l in range(LV):
                th[q, g][:, o[l]] = np.clip(y + rng.integers(-60, 61, (16, n)), 0, 4095)
                su[q, g][C::2, o[l]] = o[l]
                su[q, g][C + 1::2, o[l]] = o[l][rng.integers(0, n, (len(range(C + 1, 16, 2)), n))]
            lane = np.arange(S) if k == 3 else rng.integers(0, 3, S) if k == 2 else np.ones(S, np.int64)
            st[q, g] = o[:, lane]; xs[q, g] = np.clip(y[:, None, lane] + rng.integers(-100, 101, (16, T, S)), 0, 4095)
            if k == 1:
                z = 0 if (g >> 2) % 2 == q % 2 else S - 1
                st[q, g, :, z] = (o[:, 1] + 1 + rng.integers(0, F - 1, LV)) % F; xs[q, g, :, :, z] = x0[:, :, z]
    return pack(th, su, st, xs, hv)
def setup_inputs_ends(rng):
    kind = rng.integers(0, 4, (N, 8, 1, F)); mix = rng.integers(0, 2, (N, 8, 16, F)); i = np.arange(16)
    th = 4095 * np.where(kind == 0, 0, np.where(kind == 1, 1, mix))
    off = (rng.random((N, 8, 1, F)) < 0.25) & (i[:, None] == rng.integers(0, 16, (N, 8, 1, F))); th = np.where(off, np.abs(th - 1), th)
    th[..., [0, 1, 4]] = 0; th[..., [F - 1, F - 2, 2]] = 4095; th[:, :, 15, 1] = 1; th[:, :, 15, F - 2] = 4094
    e = rng.random((N, 8, 16, F)); su = np.where(e < 0.35, 0, np.where(e < 0.7, F - 1, rng.integers(0, F, e.shape)))
    su[..., F - 3] = np.where(i == 15, F - 2, np.where(i % 2 == 0, F - 1, 2)); su[..., 5] = np.where(i == 15, 1, np.where(i % 2 == 0, 4, 0))
    su[..., 3] = np.where(i % 2 == 0, F - 1, 2); su[..., 7] = np.where(i % 2 == 0, 4, 0)
    e = rng.random((N, 8, LV, S)); st = np.where(e < 0.35, 0, np.where(e < 0.7, F - 1, rng.integers(0, F, e.shape)))
    kind = rng.integers(0, 4, (N, 8, 1, T, S)); mix = rng.integers(0, 2, (N, 8, 16, T, S)); xs = 4095 * np.where(kind == 0, 0, np.where(kind == 1, 1, mix))
    for j, a, x in ((1, F - 3, 0), (2, 5, 4095), (3, 3, 0), (4, 7, 0)): st[..., S - j] = a; xs[..., S - j] = x
    hv = np.where(rng.random((N, 8, 16, 16)) < 0.5, 0.25, 2.0)
    return pack(th, su, st, xs, hv)
def setup_inputs_spread(rng):
    th, su, st, xs, hv = parts(rng)
    def uneven(n, shape, own):
        return np.minimum((n * np.power(rng.random(shape), np.exp2(rng.integers(-2, 3, own)))).astype(np.int64), n - 1)
    th = uneven(4096, th.shape, (N, 8, 1, F)); xs = uneven(4096, xs.shape, (N, 8, 1, T, S))
    su = uneven(F, su.shape, (N, 8, 1, F)); st = uneven(F, st.shape, (N, 8, LV, S))
    hv = (1 + rng.random((N, 8, 16, 16))) * np.exp2(rng.integers(-2, 1, (N, 8, 1, 16)))
    return pack(th, su, st, xs, hv)
def setup_inputs_ties(rng):
    th, su, st, xs, hv = parts(rng); m = F // 8
    for q in range(N):
        for g in range(8):
            base = rng.integers(0, 4093, (16, 8)); base[:, 0] = 0; base[:, 1] = 4092; pat = rng.integers(0, 4, (16, 8, 12))
            o = rng.permutation(F)[:8 * m].reshape(8, m); fam = rng.integers(0, 8, F); fam[o] = np.arange(8)[:, None]
            th[q, g] = base[:, fam] + pat[:, fam, rng.integers(0, 12, F)]
            su[q, g] = o[rng.integers(0, 8, F)[None, :], rng.integers(0, m, (16, F))]
            fs = rng.integers(0, 8, S); fs[0] = 0; fs[S - 1] = 1
            close = base[:, fs][:, None, :] + rng.integers(0, 4, (16, T, S))
            keep = (rng.random(S) < 0.6) | (fs < 2); xs[q, g] = np.where(keep[None, None, :], close, xs[q, g])
    st = rng.integers(0, F, st.shape)
    return pack(th, su, st, xs, hv)
def check_ranges(d):
    bad = []
    for k, lo, hi in (("th", 0, 4095), ("su", 0, F - 1), ("st", 0, F - 1), ("xs", 0, 4095), ("hv", 0.25, 2.0)):
        a = np.asarray(d[k]).astype(np.float64)
        if not (np.min(a) >= lo and np.max(a) <= hi): bad.append("range of " + k)
    return bad
def pick(A, ix):
    return np.stack([np.stack([np.take(A[q, g], ix[q, g], axis=1) for g in range(8)]) for q in range(N)])
def members(P, names):
    return pick(P, np.ascontiguousarray(names.transpose(0, 1, 3, 2)).reshape(N, 8, S * 16)).reshape(N, 8, 16, S, 16)
def reference(th, su, st, xs, hv):
    P = np.zeros((N, 8, 16, W), np.int64); P[..., :F] = th.reshape(N, 8, 16, F)
    U = np.zeros((N, 8, 16, W), np.int64); U[..., :F] = su.reshape(N, 8, 16, F)
    x = xs.astype(np.int64).reshape(N, 8, 16, T, S); first = np.stack([gentries(a) for a in st]).astype(np.int64).reshape(N, 8, LV, S)
    opener = [first[:, :, l] for l in range(LV)]; cand = [pick(U, a) for a in opener]
    X = [np.zeros((N, 8, 16, S), np.int64) for l in range(LV)]; kids = [np.ones((N, 8, 16, S)) for l in range(LV)]
    ym = []; m = 0
    for t in range(1, T + 1):
        for l in range(LV): X[l] = X[l] + x[:, :, :, t - 1]
        for l in range(LV):
            L = LN[l]
            if t % L != 0: continue
            D = np.abs(L * members(P, cand[l]) - X[l][..., None])
            M = np.add.reduce(np.exp(D * -(2.0 ** -(9 + SH[l]))), axis=-1) * 2.0 ** -4
            if l > 0: M = 0.5 * M + 0.5 * kids[l]
            ym.append(M)
            win = np.argmin(np.add.reduce(D, axis=2), axis=-1)
            b = np.take_along_axis(cand[l], win[:, :, None, :], 2)[:, :, 0]
            new = (3 * L * pick(P, b) + X[l]) >> (2 + SH[l])
            n0 = F + m * S
            for q in range(N):
                for g in range(8):
                    a, s = np.unique(opener[l][q, g], return_index=True)
                    U[q, g, m, a] = n0 + s
            col = pick(U, b)
            P[..., n0:n0 + S] = np.roll(new, l, axis=0); U[..., n0:n0 + S] = np.roll(col, l, axis=0)
            opener[l] = b; cand[l] = col; X[l] = np.zeros((N, 8, 16, S), np.int64); kids[l] = np.ones((N, 8, 16, S))
            if l + 1 < LV: kids[l + 1] = kids[l + 1] * M
            m += 1
    h = np.asarray(hv).astype(np.float64).reshape(N, 8, 16, 1, 16); yz = []
    for m in range(C):
        n0 = F + m * S
        D = np.abs(members(P, U[..., n0:n0 + S]) - P[..., n0:n0 + S][..., None])
        yz.append(np.add.reduce(h * np.exp(D * -(2.0 ** -9)), axis=-1) * 2.0 ** -4)
    return {"ym": np.concatenate(ym, axis=3).reshape(N, 128, C * S).astype(np.float32), "yz": np.concatenate(yz, axis=3).reshape(N, 128, C * S).astype(np.float32)}

def check_inputs(d):
    bad = list(check_ranges(d))
    if not bad:
        for name, y in reference(**d).items():
            for q in range(N):
                v = np.abs(np.asarray(y[q], np.float64)); s = np.sqrt(np.mean(v * v))
                if v.max() > 6 * s or s < 2.0 ** -4: bad.append('%s of rank %d is uneven or too small' % (name, q))
    return bad

@@ -1,0 +1,738 @@
+import math
+from concourse.bass import DstId, RemoteDMATransfer
+from concourse.mybir import AluOpType as Alu, AxisListType as Ax, ActivationFunctionType as Act
+
+F, S, W = 864, 128, 1760
+LEV = [0, 0, 1, 0, 0, 1, 2]
+TIMES = [[0], [1], [0, 1], [2], [3], [2, 3], [0, 1, 2, 3]]
+TOP = [0, 1, 0, 2, 4, 3, 0]
+BIG = float(2 ** 23)
+MAG = float(3 * 2 ** 22)
+SUMV = {"R4", "R5", "R6"}
+HALVE = {"E0": 4, "E1": 4, "E2": 3, "E3": 4, "E4": 4, "E5": 3, "E6": 3, "R0": 3, "R1": 3, "R2": 4, "R3": 4,
+         "R4": 0, "R5": 0, "R6": 0}
+FINE = {"E0", "E1", "E3", "E4"}
+AEOF = {"E0": 0, "E1": 1, "E2": 2, "E3": 3, "E4": 4, "E5": 5, "E6": 6, "R0": 7, "R1": 8, "R2": 9, "R3": 10,
+        "R4": 0, "R5": 1, "R6": 2}
+AEOF.update({"R5": 11, "R6": 12})
+SCOF = {"R2": 2, "R3": 1, "R4": 1, "R5": 2, "R6": 3}
+LATE = {("R0", 3): 0, ("R0", 4): 1, ("R1", 4): 2}
+ONV = {"yz4", "yz5", "yz6", "yz0", "yz1", "ym5", "ym6"}
+SMALL = set()
+ONS = {"cf1", "cf2", "Uc0", "Uc1", "old2", "old3", "cf3", "Uc3"}
+ROUNDS = 4000
+VARY = ({}, {"gam": 1.15, "fix": 25.0}, {"gam": 1.95, "sca": 5.5, "fix": 100.0, "lat": 180.0}, {"pe": 0.62, "gdma": 1400.0, "bw": 150.0})
+RANK = "E0:200 E1:150 E3:100 E4:40 S0:180 S1:130 S3:60 S4:20 E2:60 S2:60 X0:170 X1:120 X3:60"
+BOOST = {x.split(":")[0]: 1000.0 * int(x.split(":")[1]) for x in RANK.split()}
+GOF = {"E0": 0, "E1": 1, "E2": 2, "E3": 3, "E4": 4, "E5": 5, "E6": 6, "R0": 1, "R1": 3, "R3": 4,
+       "R2": 7, "R4": 0, "R5": 2, "R6": 6}
+SLACK = 250.0
+
+f32, f16, b16, i32, u16 = "float32", "float16", "bfloat16", "int32", "uint16"
+SCRATCH = {
+    "Pt": ("sbuf", [128, W], i32), "Ut": ("sbuf", [128, 128 + W], f32), "sui": ("sbuf", [128, F], i32),
+    "sti": ("sbuf", [128, 24], i32), "stu": ("sbuf", [128, 24], u16), "stf": ("sbuf", [128, 24], f32),
+    "xsi": ("sbuf", [128, 512], i32), "X16": ("sbuf", [128, 512], f16), "lnh": ("sbuf", [128, 16], f32),
+    "hvb": ("sbuf", [128, 16], b16), "hvf": ("sbuf", [128, 16], f32), "hrec": ("sbuf", [128, 16], f32),
+    "r16": ("sbuf", [128, 16], f32), "RT": ("sbuf", [128, 1024], f32),
+    "ones": ("sbuf", [128, 144], f32), "zer": ("sbuf", [128, 144], f32), "one16": ("sbuf", [128, 128], b16),
+    "cm16": ("sbuf", [128, 128], b16),
+    "idf": ("sbuf", [128, 128], f32), "idh": ("sbuf", [128, 128], f32), "IDS": ("sbuf", [128, 8 * 128], b16),
+    "RB": ("sbuf", [128, 144], b16), "RA": ("sbuf", [128, 1032], b16), "CC": ("sbuf", [128, 1032], b16),
+    "rowp": ("sbuf", [128, 144], f32), "io129": ("sbuf", [128, 144], f32),
+    "Sel": ("sbuf", [128, 512], b16),
+    "BO": ("sbuf", [128, 8], f32), "BO1": ("sbuf", [128, 8], f32), "G8f": ("sbuf", [128, 8], f32),
+    "G8": ("sbuf", [128, 8], b16),
+    "BBf": ("sbuf", [128, 128], f32), "BB": ("sbuf", [128, 128], b16), "sel34": ("sbuf", [128, 256], f32),
+    "mri": ("sbuf", [128, 128], i32), "mrj": ("sbuf", [128, 128], i32), "mR": ("sbuf", [128, 128], f32),
+    "negm": ("sbuf", [128, 128], b16),
+    "keyf": ("sbuf", [128, 144], f32), "keyc": ("sbuf", [128, 144], b16), "rst": ("sbuf", [128, 144], f32),
+    "rst16": ("sbuf", [128, 128], f32),
+    "DmA": ("sbuf", [128, 144], f32), "DmB": ("sbuf", [128, 144], f32), "Dm": ("sbuf", [128, 144], f32),
+    "pi": ("sbuf", [128, 64], i32), "pj": ("sbuf", [128, 64], i32), "rl": ("sbuf", [128, 64], u16),
+    "rcol": ("sbuf", [128, 8], f32), "c18": ("sbuf", [128, 16], f32), "c2": ("sbuf", [128, 16], f32),
+    "c2b": ("sbuf", [128, 16], f32), "c2c": ("sbuf", [128, 16], f32),
+    "bc18": ("sbuf", [128, 16], u16), "bcv": ("sbuf", [128, 16], u16), "bc8": ("sbuf", [128, 16], u16),
+    "c1": ("sbuf", [128, 16], f32), "scol": ("sbuf", [128, 8], f32), "sb": ("sbuf", [128, 8], f32),
+    "CT": ("sbuf", [128, 128], f32), "mins": ("sbuf", [128, 56], f32), "io896": ("sbuf", [128, 896], f32),
+    "BM": ("sbuf", [128, 7 * 128], f32),
+    "cu": ("sbuf", [128, 10 * 128], u16),
+    "cf": ("sbuf", [128, 4 * 128], f32),
+    "rcu": ("sbuf", [128, 3 * 128], u16), "rxt": ("sbuf", [128, 3 * 128], f16),
+    "snew": ("sbuf", [128, 3 * 128], i32), "nxt": ("sbuf", [128, 7 * 128], f16),
+    "rm": ("sbuf", [128, 7 * 144], f32), "stp": ("sbuf", [128, 7 * 144], f32), "val": ("sbuf", [128, 7 * 144], f32),
+    "M1": ("sbuf", [128, 3 * 128], f16), "A12": ("sbuf", [128, 10 * 256], f16),
+    "bl": ("sbuf", [128, 7 * 8], u16), "Pb": ("sbuf", [128, 7 * 128], f16),
+    "offf": ("sbuf", [128, 7 * 8], f32), "offu": ("sbuf", [128, 7 * 8], u16), "old": ("sbuf", [128, 7 * 128], f32),
+    "fxs": ("sbuf", [128, 384], f32), "fxu": ("sbuf", [128, 24], u16),
+    "prod": ("sbuf", [128, 3 * 128], f32), "ymb": ("sbuf", [128, 896], f32), "yzb": ("sbuf", [128, 896], f32),
+    "GX": ("sbuf", [128, 384], f16), "U2": ("sbuf", [128, 512 + F], f32),
+}
+for _k in range(max(AEOF.values()) + 1):
+    SCRATCH["AE%d" % _k] = ("sbuf", [128, 2048], f32)
+for _k in range(8):
+    SCRATCH["G%d" % _k] = ("sbuf", [128, 2048], f16)
+for _k in range(4):
+    SCRATCH["ps%d" % _k] = ("psum", [128, 1024], f32)
+SEMAPHORES = ["cv", "cs", "cp", "cg", "sto", "sent", "arr2", "arr5", "arr6", "ld0", "ld1", "ld2", "ld3", "ld4", "cpu", "rt"] + ["a" + _u for _u in AEOF] + ["t" + _u for _u in AEOF]
+CSEM = {"v": "cv", "s": "cs", "p": "cp", "g": "cg"}
+COST = {"cyc": 1.0, "pe": 0.52, "gam": 1.56, "sca": 3.8, "fix": 60.0, "lat": 90.0, "dma": 2300.0, "rem": 3500.0,
+        "gdma": 1000.0, "bw": 250.0}
+
+
+def build(T, topo, core, C):
+    ops = []
+    bank = {}
+    part = ["C"]
+
+    def op(name, eng, fn, rd, wr, cost, kind="c", sem=None, acq=None, rel=None):
+        ops.append({"name": name, "eng": eng, "fn": fn, "rd": list(rd), "wr": list(wr), "cost": cost, "kind": kind,
+                    "sem": sem, "acq": acq, "rel": rel, "part": part[0]})
+
+    def cv(n, k=1.0):
+        return C["fix"] + max(64, n * k) * C["cyc"]
+
+    def cg(n):
+        return C["fix"] + n * C["gam"] * C["cyc"]
+
+    def cp(n):
+        return C["fix"] + n * C["pe"]
+
+    def ps(h, a, b, st=1):
+        k = bank[h]
+        o = (k % 2) * 512
+        return T["ps%d" % (k // 2)][:, o + a:o + b:st]
+
+    def blk(t, m, w=128):
+        return t[:, m * w:(m + 1) * w]
+
+    def ident(k):
+        return blk(T.IDS, k)
+
+    def gi(name, out, pat, base, cm, n, fl=True):
+        if fl:
+            op(name, "g", lambda q: [q.iota(out, pat, base, cm, allow_small_or_imprecise_dtypes=True)], [], [name], 130 + 2 * n * C["cyc"])
+        else:
+            op(name, "g", lambda q: [q.iota(out, pat, base, cm)], [], [name], 130 + 2 * n * C["cyc"])
+
+    def ga(name, out, in_, rd, pat, cmp, fill, base, cm, n):
+        op(name, "g", lambda q: [q.affine_select(out, in_, pat, cmp, fill, base, cm)], rd, [name], 170 + 2 * n * C["cyc"])
+
+    def vts(name, out, in0, s1, s2, o0, o1, rd, n, wr=None, cost=None, **kw):
+        if o1 is None:
+            fn = lambda q: [q.tensor_scalar(out, in0, s1, None, o0)]
+        else:
+            fn = lambda q: [q.tensor_scalar(out, in0, s1, s2, o0, o1)]
+        op(name, "v", fn, rd, wr or [name], cost or cv(n), **kw)
+
+    def vcp(name, out, in_, rd, n, wr=None, cost=None):
+        op(name, "v", lambda q: [q.tensor_copy(out, in_)], rd, wr or [name], cost or cv(n))
+
+    def vtt(name, out, a, b, o, rd, n, wr=None, cost=None):
+        op(name, "v", lambda q: [q.tensor_tensor(out, a, b, o)], rd, wr or [name], cost or cv(n, 2))
+
+    def sact(name, out, in_, func, rd, n, wr=None, cost=None, **kw):
+        op(name, "s", lambda q: [q.activation(out, in_, func, **kw)], rd, wr or [name], cost or cv(n))
+
+    for k, (nm, eng, o, i) in enumerate([("sti", "y", T.sti[:], T.st[:]), ("sui", "y", T.sui[:], T.su[:]),
+                                         ("P0", "s", T.Pt[:, 0:F], T.th[:]), ("xsi", "y", T.xsi[:], T.xs[:]),
+                                         ("hvb", "y", T.hvb[:], T.hv[:])]):
+        op(nm, eng, lambda q, o=o, i=i: [q.dma_start(o, i)], [], [nm], 60.0, kind="d", sem="ld%d" % k)
+
+    op("ones", "v", lambda q: [q.memset(T.ones[:], 1.0)], [], ["ones"], cv(144))
+    op("zer", "v", lambda q: [q.memset(T.zer[:], 0.0)], [], ["zer"], cv(144))
+    op("one16", "v", lambda q: [q.memset(T.one16[:], 1.0)], [], ["one16"], cv(64))
+    op("cm16", "v", lambda q: [q.memset(T.cm16[:], -15.0 / 32)], [], ["cm16"], cv(64))
+    ga("idf", T.idf[:], T.ones[:, 0:128], ["ones"], [[-1, 128]], Alu.is_equal, 0.0, 0, 1, 128)
+    for k, sc in enumerate([1.0, 2.0, 4.0, 0.75, 0.25, 0.125, 0.0625, -1.0]):
+        if k in (0, 7):
+            sact("I%d" % k, ident(k), T.idf[:], Act.Copy, ["idf"], 128, scale=sc)
+        else:
+            ga("I%d" % k, ident(k), T.zer[:, 0:128], ["zer"], [[-1, 128]], Alu.not_equal, sc, 0, 1, 128)
+    ga("idh", T.idh[:], T.zer[:, 0:128], ["zer"], [[-1, 128]], Alu.not_equal, 0.5, 0, 1, 128)
+    op("RB0", "v", lambda q: [q.memset(T.RB[:, 0:1], 0.0)], [], ["RB0"], cv(1))
+    sact("RB", T.RB[:, 1:129], T.idf[:], Act.Copy, ["idf"], 128, scale=4096.0)
+    ga("BO1", T.BO1[:], T.ones[:, 0:8], ["ones"], [[-16, 8]], Alu.is_ge, 0.0, 0, 1, 8)
+    ga("G8f", T.G8f[:], T.BO1[:], ["BO1"], [[16, 8]], Alu.is_ge, 0.0, 15, -1, 8)
+    sact("BO", T.BO[:], T.G8f[:], Act.Copy, ["G8f"], 8, scale=16.0)
+    sact("G8", T.G8[:], T.G8f[:], Act.Copy, ["G8f"], 8)
+    gi("c1", T.c1[:], [[1, 16]], 0, 0, 16)
+    vcp("bc8", T.bc8[:], T.c1[:], ["c1"], 16)
+    sact("BBf", T.BBf[:], T.G8f[:].indirect(T.bc8[:, 0:8]), Act.Copy, ["G8f", "bc8"], 128, cost=cg(128))
+    sact("BB", T.BB[:], T.BBf[:], Act.Copy, ["BBf"], 128)
+    gi("mri", T.mri[:], [[-1, 128]], 0, 1, 128, False)
+    vts("mrj", T.mrj[:], T.mri[:], 15, None, Alu.bitwise_and, None, ["mri"], 128)
+    vts("mR", T.mR[:], T.mrj[:], 0.0, None, Alu.is_equal, None, ["mrj"], 128)
+    sact("negm", T.negm[:], T.mR[:], Act.Identity, ["mR"], 128, scale=4096.0, bias=-4096.0)
+    for k in range(2):
+        sact("sel%d" % (3 + k), blk(T.sel34, k), T.BBf[:], Act.Copy, ["BBf", "mR"], 128, scale=T.mR[:, 3 + k:4 + k])
+    gi("keyf", T.keyf[:], [[0, 8], [1, 18]], -2, 0, 144)
+    ga("keyc", T.keyc[:], T.keyf[:], ["keyf"], [[0, 8], [1, 18]], Alu.is_ge, BIG, -2, 0, 144)
+    ga("rst", T.rst[:], T.zer[:, 0:144], ["zer"], [[0, 8], [1, 18]], Alu.not_equal, BIG, 0, 0, 144)
+    ga("rst16", T.rst16[:], T.zer[:, 0:128], ["zer"], [[0, 8], [1, 16]], Alu.not_equal, -8192.0, 0, 0, 128)
+    ga("DmA", T.DmA[:], T.zer[:], ["zer"], [[-16, 8], [-1, 18]], Alu.not_equal, -1.0, 1, 1, 144)
+    ga("DmB", T.DmB[:], T.DmA[:], ["DmA"], [[0, 8], [-1, 18]], Alu.is_gt, 0.0, 17, 0, 144)
+    ga("Dm", T.Dm[:], T.DmB[:], ["DmB"], [[-16, 8], [-1, 18]], Alu.not_equal, 1.0, 2, 1, 144)
+    gi("pi", T.pi[:], [[0, 64]], 0, 1, 64, False)
+    vts("pj", T.pj[:], T.pi[:], 15, None, Alu.bitwise_and, None, ["pi"], 64)
+    vcp("rcol", T.rcol[:], T.pj[:, 0:8], ["pj"], 8)
+    vts("bcv", T.bcv[:], T.c1[:], 18.0, 17.0, Alu.mult, Alu.add, ["c1"], 16)
+    vts("c2", T.c2[:], T.c1[:], 2.0, T.rcol[:, 0:1], Alu.mult, Alu.is_gt, ["c1", "rcol"], 16)
+    vtt("c2c", T.c2c[:], T.c1[:], T.c2[:], Alu.subtract, ["c1", "c2"], 16)
+    vts("bc18", T.bc18[:], T.c2c[:], 7.0, None, Alu.min, None, ["c2c"], 16)
+    sact("scol", T.scol[:], T.c1[:, 0:8], Act.Identity, ["c1", "rcol"], 8, scale=16.0, bias=T.rcol[:, 0:1])
+    sact("sb", T.sb[:], T.scol[:], Act.Identity, ["scol"], 8, scale=-float(2 ** 25), bias=float(2 ** 24))
+    gi("io129", T.io129[:], [[1, 144]], -1, 0, 144)
+    ga("rowp0", T.rowp[:], T.ones[:], ["ones"], [[1, 144]], Alu.is_equal, -4096.0, 0, 0, 144)
+    for b in range(8):
+        n = 16 * (b + 1) + 1
+        sact("RA%d" % b, T.RA[:, b * 129:b * 129 + n], T.rowp[:, 0:n], Act.Copy, ["rowp0", "G8f"], n, scale=T.G8f[:, b:b + 1])
+    for b in range(8):
+        n = 16 * (b + 1) + 1
+        tmp = T.BM[:, b * 112:b * 112 + n - 1] if b < 7 else T.CT[:]
+        sact("CT%d" % b, tmp, T.io129[:, 1:n], Act.Relu, ["io129", "sb"], n, wr=["BMt%d" % b], scale=float(2 ** 25), bias=T.sb[:, b:b + 1])
+        sact("CC%d" % b, T.CC[:, b * 129 + 1:b * 129 + n], tmp, Act.Identity, ["BMt%d" % b, "scol"], n, bias=T.scol[:, b:b + 1])
+    sact("CCx", T.CC[:, 0:1032:129], T.scol[:], Act.Identity, ["scol"], 8, scale=0.0, bias=128.0)
+    gi("io896", T.io896[:], [[1, 896]], F, 0, 896)
+    for m in range(7):
+        sact("BM%d" % m, blk(T.BM, m), blk(T.io896, m), Act.Copy, ["io896", "mR"], 128,
+             wr=["BM%d" % m] + ["BMt%d" % b for b in range(7)], scale=T.mR[:, m:m + 1])
+    sact("hvf", T.hvf[:], T.hvb[:], Act.Copy, ["hvb"], 16)
+    if any(u[0] == "R" for u in SUMV):
+        op("hrec", "v", lambda q: [q.reciprocal(T.hrec[:], T.hvf[:])], ["hvf"], ["hrec"], 300.0)
+        op("r160", "v", lambda q: [q.memset(T.RT[:, 0:1], 0.0)], [], ["r160"], cv(1))
+        vtt("RT", T.RT[:, 1:16], T.hvf[:, 0:15], T.hrec[:, 1:16], Alu.mult, ["hvf", "hrec"], 16)
+        for w in (16, 32, 64, 128, 256, 512):
+            op("RT%d" % w, "y", lambda q, w=w: [q.dma_start(T.RT[:, w:2 * w], T.RT[:, 0:w])], ["RT", "r160"], ["RT"], 60.0, kind="d", sem="rt")
+        op("Sel0", "g", lambda q: [q.iota(T.Sel[:], [[0, 512]], 0, 0, allow_small_or_imprecise_dtypes=True)], [], ["Sel"], 130 + 1024 * C["cyc"])
+        for k in range(4):
+            sl = T.Sel[32 * k:32 * k + 32, :]
+            op("Sel%d" % (k + 1), "g", lambda q, sl=sl: [q.affine_select(sl, sl, [[-1, 32], [0, 16]], Alu.not_equal, -1.0, 0, 1)],
+               ["Sel"], ["Sel"], 170 + 1024 * C["cyc"])
+    sact("lnh", T.lnh[:], T.hvf[:], Act.Ln, ["hvf"], 16, scale=1.0 / 16, cost=1600.0)
+
+    def column(name, out, c, lst, lk, top):
+        win = T.Ut[:, 128:128 + F + 128 * top].indirect(lst)
+        rd = ["U0", lk] + ["Uc%d" % k for k in range(top)]
+        if name in ("old5", "old6"):
+            win, rd = T.U2[:, 128:128 + F].indirect(lst), ["U2", lk]
+        if name in ONS:
+            sact(name, out, win, Act.Copy, rd, 0, cost=cg(128))
+        elif c is None:
+            vcp(name, out, win, rd, 0, cost=cg(128))
+        else:
+            vcp(name, out, blk(T.cu, c), ["cu%d" % c], 128)
+
+    vcp("stu", T.stu[:], T.sti[:], ["sti"], 24)
+    vcp("stf", T.stf[:], T.sti[:], ["sti"], 24)
+    for l in range(3):
+        vcp("cu%d" % (7 + l), blk(T.cu, 7 + l), T.sui[:].indirect(T.stu[:, 8 * l:8 * l + 8]), ["sui", "stu"], 128, cost=cg(128))
+    ga("U0", T.Ut[:, 128:128 + F], T.sui[:], ["sui"], [[0, F]], Alu.is_equal, 0.0, 0, 0, F)
+    for l in range(3):
+        column("cf%d" % l, blk(T.cf, l), 7 + l, T.stu[:, 8 * l:8 * l + 8], "stu", 0)
+    vts("X16", T.X16[:], T.xsi[:], -2048.0, None, Alu.add, None, ["xsi"], 512)
+    MX, MK = {}, {}
+    for l in range(3):
+        a = 7 + l
+        vtt("M1%d" % l, blk(T.M1, l), T.stf[:, 8 * l:8 * l + 8].indirect(T.bc8[:, 0:8]), T.mR[:], Alu.mult,
+            ["stf", "bc8", "mR"], 128, cost=cg(128))
+        op("Ap%d" % a, "p", lambda q, l=l, a=a: [q.matmul(ps("a%d" % a, 0, 128), blk(T.M1, l), ident(0), True, True),
+                                               q.matmul(ps("a%d" % a, 128, 256), blk(T.M1, l), T.BB[:], True, True)],
+           ["M1%d" % l, "I0", "BB"], ["Ap%d" % a], cp(256), acq=("a%d" % a, 1))
+        op("A12%d" % a, "v", lambda q, a=a: [q.tensor_copy(blk(T.A12, a, 256), ps("a%d" % a, 0, 256))],
+           ["Ap%d" % a], ["A1%d" % a, "A2%d" % a], cv(256), rel="a%d" % a)
+
+    def pk(n):
+        return ["P0"] + ["Pc%d" % k for k in range(n)]
+
+    def uk(n):
+        return ["U0"] + ["Uc%d" % k for k in range(n)]
+
+    def chunks(u):
+        if u in ("R0", "R1") and u not in SUMV:
+            return [(0, 1024), (1024, 1536), (1536, 2048)]
+        w = 512 if u in FINE or u in SMALL else 1024
+        return [(a, a + w) for a in range(0, 2048, w)]
+
+    def slots(u):
+        late = [i for i in range(16) if (u, i) in LATE]
+        return [i for i in range(16) if i not in late] + late
+
+    def gkeys(k, a=0, b=2048):
+        return ["G%d_%d" % (k, x) for x in range(a // 512, b // 512)]
+
+    def akeys(k, a=0, b=2048):
+        return ["AE%d_%d" % (k, x) for x in range(a // 512, b // 512)]
+
+    def gather(u, cand, ck, top):
+        G = T["G%d" % GOF[u]]
+        for a, b in ([(0, 1024), (1024, 2048)] if u not in SMALL else chunks(u)):
+            vts("g%s_%d" % (u, a), G[:, a:b], T.Pt[:, 0:F + 128 * top].indirect(cand[:, a // 16:b // 16]), -2048.0, None,
+                Alu.add, None, pk(top) + [ck], 0, wr=gkeys(GOF[u], a, b), cost=cg(b - a))
+
+    def dist(u, lev, xts, xk):
+        G = T["G%d" % GOF[u]]
+        A = T["AE%d" % AEOF[u]]
+        for a, b in chunks(u):
+            h = "d%s_%d" % (u, a)
+
+            def mm(q, a=a, b=b, h=h):
+                r = []
+                if u in SUMV:
+                    for c in range(a, b, 512):
+                        o = ps(h, c - a, c - a + 512)
+                        r.append(q.matmul(o, ident(lev), G[:, c:c + 512], True, False))
+                        p0 = c // 16
+                        x = xts[0]
+                        r.append(q.matmul(o, x[0][p0:p0 + 32, x[1]:x[1] + 128], T.Sel[p0:p0 + 32, :], False, True))
+                    return r
+                for c in range(a, b, 128):
+                    o = ps(h, c - a, c - a + 128)
+                    i = slots(u)[c // 128]
+                    if u not in FINE:
+                        for j, x in enumerate(xts):
+                            r.append(q.matmul(o, ident(7), x[0][:, x[1]:x[1] + 128], j == 0, False))
+                    r.append(q.matmul(o, ident(lev), blk(T.GX, LATE[u, i]) if (u, i) in LATE else G[:, i::16], False,
+                                      u not in FINE or c + 128 == b))
+                return r
+            late = ["fx%d" % LATE[u, i] for i in slots(u)[a // 128:b // 128] if (u, i) in LATE]
+            if u in FINE:
+                x = xts[0]
+                op(h + "x", "p", lambda q, h=h, x=x: [q.matmul(ps(h, c, c + 128), ident(7), x[0][:, x[1]:x[1] + 128], c == 0, False)
+                                                     for c in range(0, 512, 128)],
+                   gkeys(GOF[u], 0, 512) + ["I7", xk], [h], cp(512), acq=(h, 1))
+                op(h, "p", mm, gkeys(GOF[u]) + [h, "I%d" % lev], [h], cp(512))
+            else:
+                op(h, "p", mm, (gkeys(GOF[u], a, b) + ["Sel"] if u in SUMV else gkeys(GOF[u]) + ["I7"]) + [xk, "I%d" % lev] + late, [h],
+                   cp((b - a) * (1 + len(xts))), acq=(h, (b - a) // 512))
+            op("abs" + h, "s", lambda q, a=a, b=b, h=h: [q.activation(A[:, a:b], ps(h, 0, b - a), Act.Abs)], [h],
+               akeys(AEOF[u], a, b), cv(b - a), rel=h)
+
+    def mix(u, lev, m):
+        k = AEOF[u]
+        A = T["AE%d" % k]
+        ro = u[0] == "R"
+        bias = -math.log(32.0 if lev else 16.0)
+        if ro and u not in SUMV:
+            for a in range(0, 2048, 512):
+                op("exp%s_%d" % (u, a), "s", lambda q, a=a: [q.activation(blk(A, i), blk(A, i), Act.Exp, scale=-1.0 / 512, bias=T.lnh[:, slots(u)[i]:slots(u)[i] + 1])
+                                                              for i in range(a // 128, a // 128 + 4)],
+                   akeys(k, a, a + 512) + ["lnh"], akeys(k, a, a + 512), 4 * cv(128))
+        else:
+            for a in (0, 1024):
+                sact("exp%s_%d" % (u, a), A[:, a:a + 1024], A[:, a:a + 1024], Act.Exp, akeys(k, a, a + 1024) + ["lnh"], 1024,
+                     wr=akeys(k, a, a + 1024), scale=-1.0 / (512 << lev), bias=bias)
+        out = blk(T.yzb if ro else T.ymb, m)
+        nm = ("yz%d" if ro else "ym%d") % m
+        if u in SUMV:
+            sc = T["AE%d" % SCOF[u]]
+            for a in (0, 1024):
+                op("scan%s_%d" % (u, a), "v", lambda q, a=a: [q.tensor_tensor_scan(sc[:, a:a + 1024], T.RT[:], A[:, a:a + 1024], 0.0, Alu.mult, Alu.add)],
+                   akeys(k, a, a + 1024) + ["RT"], akeys(SCOF[u], a, a + 1024), cv(1024))
+            if nm in ONV:
+                vts(nm, out, sc[:, 15::16], T.hvf[:, 15:16], None, Alu.mult, None, akeys(SCOF[u]) + ["hvf"], 128)
+            else:
+                sact(nm, out, sc[:, 15::16], Act.Copy, akeys(SCOF[u]) + ["hvf"], 128, scale=T.hvf[:, 15:16])
+        else:
+            h = "sum" + u
+            tail = [12, 13, 14, 15] if u in ("R0", "R1") else []
+            top = 2048 - 128 * len(tail)
+            for j in range(HALVE.get(u, 0)):
+                w = top // 256 * 128
+                op("add%s_%d" % (u, j), "g", lambda q, w=w, top=top: [q.dma_start(A[:, 0:w], A[:, top - w:top], accum_op=Alu.add)],
+                   akeys(k, 0, top + 511), akeys(k, 0, w + 511), C["gdma"], kind="a", sem="a" + u)
+                ops[-1]["lat"] = C["dma"] + w * 512 / C["bw"]
+                top -= w
+            slabs = list(range(top // 128)) + tail
+            pr = None
+            if lev:
+                x, y = {2: (0, 1), 5: (3, 4), 6: (2, 5)}[m]
+                pr = blk(T.prod, {2: 0, 5: 1, 6: 2}[m])
+                vtt("prod%d" % m, pr, MX[x], MX[y], Alu.mult, MK[x] + MK[y], 128)
+            if len(slabs) == 1 and not lev:
+                out = A[:, 0:128]
+                [o for o in ops if o["name"] == "add%s_3" % u][0]["wr"].append(nm)
+            else:
+                for j in sorted(set(i // 4 for i in slabs)):
+                    some = [i for i in slabs if i // 4 == j]
+
+                    def mm(q, some=some):
+                        return [q.matmul(ps(h, 0, 128), T.idf[:], blk(A, i), i == 0, i == slabs[-1] and not lev) for i in some]
+                    op("%s_%d" % (h, j), "p", mm, akeys(k, 512 * j, 512 * j + 512) + ["idf"] + ([h] if j else []), [h],
+                       cp(len(some) * 512), acq=(h, 1) if j == 0 else None)
+                if lev:
+                    op(h + "x", "p", lambda q: [q.matmul(ps(h, 0, 128), T.idh[:], pr, False, True)], [h, "idh", "prod%d" % m], [h], cp(512))
+                if nm in ONV:
+                    op(nm, "v", lambda q: [q.tensor_copy(out, ps(h, 0, 128))], [h], [nm], cv(128), rel=h)
+                else:
+                    op(nm, "s", lambda q: [q.activation(out, ps(h, 0, 128), Act.Copy)], [h], [nm], cv(128), rel=h)
+        keys = [nm] + (akeys(k, 0, 512) if u not in SUMV and HALVE.get(u, 0) == 4 and not lev and u not in ("R0", "R1") else [])
+        if not ro:
+            MX[m] = out
+            MK[m] = keys
+        dst = (T.yz if ro else T.ym)[:, m * 128:(m + 1) * 128]
+        op("st" + nm, "y", lambda q: [q.dma_start(dst, out)], keys, [], 60.0, kind="d", sem="t" + u)
+
+    def elect(m, cf, cfk):
+        u = "E%d" % m
+        k = AEOF[u]
+        A = T["AE%d" % k]
+        h = "k%d" % m
+        for j in range(4):
+            def mm(q, j=j):
+                r = []
+                if j == 0:
+                    r.append(q.matmul(ps(h, 144, 288), cf, T.Dm[:], True, True))
+                    r.append(q.matmul(ps(h, 0, 144), T.one16[0:1, :], T.keyc[0:1, :], True, False))
+                for i in range(4 * j, 4 * j + 4):
+                    r.append(q.matmul(ps(h, 2 + i, 144, 18), blk(A, i), T.BO[:], False, i == 15))
+                return r
+            op("%s_%d" % (h, j), "p", mm, akeys(k, 512 * j, 512 * j + 512) + [cfk, "Dm", "one16", "keyc", "BO"] + ([h] if j else []), [h],
+               cp(4 * 256 + (720 if j == 0 else 0)), acq=(h, 1) if j == 0 else None)
+        rm, stp, val = blk(T.rm, m, 144), blk(T.stp, m, 144), blk(T.val, m, 144)
+        op("rm%d" % m, "v", lambda q: [q.tensor_tensor_scan(rm, T.rst[:], ps(h, 0, 144), 0.0, Alu.add, Alu.min)],
+           [h, "rst"], ["rm%d" % m], cv(144))
+        vcp("mins%d" % m, blk(T.mins, m, 8), T.rm[:, m * 144 + 17:(m + 1) * 144:18], ["rm%d" % m], 8)
+        vtt("stp%d" % m, stp, blk(T.mins, m, 8).indirect(T.bc18[:, 0:9]), rm, Alu.is_equal, ["rm%d" % m, "mins%d" % m, "bc18"], 0, cost=cg(144))
+        op("val%d" % m, "v", lambda q: [q.tensor_tensor_scan(val, ps(h, 144, 288), stp, 0.0, Alu.add, Alu.mult)],
+           [h, "stp%d" % m], ["val%d" % m], cv(144))
+        a1 = T.A12[:, m * 256:m * 256 + 128]
+        vtt("A1%d" % m, a1, val.indirect(T.bcv[:, 0:8]), T.mR[:], Alu.mult, ["val%d" % m, "bcv", "mR"], 0, cost=cg(128))
+        op("L%d" % m, "p", lambda q: [q.matmul(ps(h, 288, 296), a1, T.G8[:], True, True)], ["A1%d" % m, "G8", "rm%d" % m], ["L%d" % m], cp(64))
+        op("bl%d" % m, "v", lambda q: [q.tensor_copy(blk(T.bl, m, 8), ps(h, 288, 296))], ["L%d" % m], ["bl%d" % m], cv(8), rel=h)
+        if m in (0, 1, 2, 3):
+            vcp("A2%d" % m, T.A12[:, m * 256 + 128:m * 256 + 256], val.indirect(T.bcv[:, 0:8]), ["val%d" % m, "bcv"], 0, cost=cg(128))
+
+    SEG = []
+    o = 0
+    for b in range(8):
+        if b == 6:
+            o = 512
+        SEG.append((o, 16 * (b + 1) + 1))
+        o += 16 * (b + 1) + 1
+
+    def extend(m, a, lst, lk, top, old, oldk):
+        h = "x%d" % m
+        a1, a2 = T.A12[:, a * 256:a * 256 + 128], T.A12[:, a * 256 + 128:a * 256 + 256]
+
+        def mm(q):
+            r = []
+            for b, (o, n) in enumerate(SEG):
+                r.append(q.matmul(ps(h, o, o + n), a1, T.RA[:, b * 129:b * 129 + n], True, False))
+                r.append(q.matmul(ps(h, o, o + n), a2, T.RB[:, 0:n], False, False))
+                r.append(q.matmul(ps(h, o, o + n), ident(0), T.CC[:, b * 129:b * 129 + n], False, True))
+            return r
+        op(h, "p", mm, ["A1%d" % a, "A2%d" % a, "RB", "RB0", "CCx", "I0"] + ["RA%d" % b for b in range(8)] + ["CC%d" % b for b in range(8)],
+           [h], cp(3 * 700), acq=(h, 2))
+        op("off%d" % m, "v", lambda q: [q.tensor_reduce(T.offf[:, m * 8 + b:m * 8 + b + 1], ps(h, o, o + n), Ax.X, Alu.min, apply_absolute_value=True)
+                                        for b, (o, n) in enumerate(SEG)], [h], ["off%d" % m], sum(cv(n) for o, n in SEG), rel=h)
+        vcp("offu%d" % m, blk(T.offu, m, 8), blk(T.offf, m, 8), ["off%d" % m], 8)
+        if old is None:
+            old, oldk = blk(T.old, m), "old%d" % m
+            column(oldk, old, None, lst, lk, top)
+        vtt("ext%d" % m, (T.Ut if m < 5 else T.U2)[:, 0:128 + F + 128 * top].indirect(blk(T.offu, m, 8)), old, blk(T.BM, m), Alu.max,
+            ["offu%d" % m, oldk, "BM%d" % m], 0, wr=uk(top) + ["spare"] if m < 5 else ["U2"], cost=C["fix"] + 128 * C["sca"] * C["cyc"])
+        if m == 4:
+            op("U2", "y", lambda q: [q.dma_start(T.U2[:, 128:512 + F], T.Ut[:, 128:512 + F])], uk(3), ["U2"], 60.0, kind="a", sem="cpu")
+            ops[-1]["lat"] = C["dma"] + 1000.0
+
+    def snap(m):
+        lev, top = LEV[m], TOP[m]
+        h = "s%d" % m
+        bl, pb = blk(T.bl, m, 8), blk(T.Pb, m)
+        rem = {2: 0, 5: 1, 6: 2}.get(m)
+        vts("Pb%d" % m, pb, T.Pt[:, 0:F + 128 * top].indirect(bl), -2048.0, None, Alu.add, None, pk(top) + ["bl%d" % m], 0, cost=cg(128))
+
+        def mm(q, tr):
+            o = ps(h, 128 * tr, 128 * tr + 128)
+            prs = [(T.one16[0:1, :], T.cm16[0:1, :])] + [(ident(4 + lev), blk(T.X16, t)) for t in TIMES[m]] + [(ident(3), pb)]
+            return [q.matmul(o, p[tr], p[1 - tr], j == 0, j == len(prs) - 1) for j, p in enumerate(prs)]
+        tr = 1 if "R%d" % m in SUMV else 0
+        op(h, "p", lambda q: mm(q, 0) + (mm(q, 1) if tr else []), ["Pb%d" % m, "X16", "one16", "cm16", "I3", "I%d" % (4 + lev)], [h],
+           cp(128 * (1 + tr) * (2 + len(TIMES[m]))), acq=(h, 1))
+        new = T.Pt[:, F + 128 * m:F + 128 * m + 128] if rem is None else blk(T.snew, rem)
+        op("new%d" % m, "v", lambda q: [q.tensor_scalar(new, ps(h, 0, 128), MAG, 2048.0 - MAG, Alu.add, Alu.add)], [h],
+           ["Pc%d" % m if rem is None else "snew%d" % m], cv(128), rel=h)
+        op("nxt%d" % m, "v", lambda q: [q.tensor_scalar(blk(T.nxt, m), ps(h, 128 * tr, 128 * tr + 128), MAG, -MAG, Alu.add, Alu.add)], [h],
+           ["nxt%d" % m], cv(128), rel=h)
+        vcp("cu%d" % m, blk(T.cu, m), (T.Ut if m < 5 else T.U2)[:, 128:128 + F + 128 * top].indirect(bl),
+            (uk(top) if m < 5 else ["U2"]) + ["bl%d" % m], 0, cost=cg(128))
+        ub = T.Ut[:, 128 + F + 128 * m:256 + F + 128 * m]
+        if m in (0, 1, 3):
+            column("Uc%d" % m, ub, m, bl, "bl%d" % m, top)
+        if m == 2:
+            column("cf3", blk(T.cf, 3), m, bl, "bl%d" % m, top)
+        if rem is None:
+            return
+        n = len(T.cores)
+        r = T.rank_of(core)
+        dst, src = T.cores[(r + lev) % n], T.cores[(r - lev) % n]
+        wide = [(new, T.Pt[:, F + 128 * m:F + 128 * m + 128])] + ([(blk(T.cf, 3), ub)] if m == 2 else [])
+        thin = [(blk(T.cu, m), blk(T.rcu, rem)), (blk(T.nxt, m), blk(T.rxt, rem))]
+
+        def send(q):
+            rid, pid = topo.addr(dst, core)
+            e = topo.engines(core, dst)
+            for prs in (wide, thin):
+                w = len(e) // len(prs)
+                q.remote_dma_fused([RemoteDMATransfer(dst_ids=[DstId(rid=rid, pnc=pid)], dma_engine_mask=sum(1 << x for x in e[j * w:(j + 1) * w]),
+                                                      remote_sem=T.sem["arr%d" % m], src=a, dst=b) for j, (a, b) in enumerate(prs)],
+                                   local_sem=T.sem.sent)
+            return 2 * len(e)
+        op("send%d" % m, "g", send, ["snew%d" % m, "cu%d" % m, "nxt%d" % m] + (["cf3"] if m == 2 else []), ["sent%d" % m], 1000.0, kind="r")
+        op("recv%d" % m, "n%d" % m, 2 * len(topo.engines(src, core)), ["sent%d" % m], ["Pc%d" % m, "rc%d" % m] + (["Uc2"] if m == 2 else []),
+           C["rem"], kind="w", sem="arr%d" % m)
+
+    def ublk(m):
+        return T.Ut[:, 128 + F + 128 * m:256 + F + 128 * m]
+
+    def fix(j, c, slot, u):
+        h = "f%d" % j
+        op(h, "p", lambda q: [q.matmul(ps(h, 0, 128), ident(0), T.negm[:], True, False),
+                              q.matmul(ps(h, 0, 128), blk(T.sel34, slot - 3), ublk(c), False, True)],
+           ["I0", "negm", "sel%d" % slot, "Uc%d" % c], [h], cp(640), acq=(h, 1))
+        op("fxs%d" % j, "v", lambda q: [q.tensor_tensor_scan(blk(T.fxs, j), T.rst16[:, 0:128], ps(h, 0, 128), 0.0, Alu.add, Alu.max)],
+           [h, "rst16"], ["fxs%d" % j], cv(128), rel=h)
+        vcp("fxu%d" % j, blk(T.fxu, j, 8), T.fxs[:, j * 128 + 15:(j + 1) * 128:16], ["fxs%d" % j], 8)
+        vts("fx%d" % j, T["G%d" % GOF[u]][:, slot::16] if u in SUMV else blk(T.GX, j),
+            T.Pt[:, 0:F + 128 * (slot + 1)].indirect(blk(T.fxu, j, 8)), -2048.0, None,
+            Alu.add, None, pk(slot + 1) + ["fxu%d" % j], 0, wr=gkeys(GOF[u]) if u in SUMV else None, cost=cg(128))
+
+    cand = {0: (7, blk(T.cf, 0), "cf0"), 1: (0, ublk(0), "Uc0"), 2: (8, blk(T.cf, 1), "cf1"), 3: (1, ublk(1), "Uc1"),
+            4: (3, ublk(3), "Uc3"), 5: (2, blk(T.cf, 3), "cf3"), 6: (9, blk(T.cf, 2), "cf2")}
+    opn = {0: (7, T.stu[:, 0:8], "stu", 0, blk(T.cf, 0), "cf0"), 1: (0, None, None, 0, ublk(0), "Uc0"),
+           2: (8, T.stu[:, 8:16], "stu", 0, None, None), 3: (1, blk(T.bl, 1, 8), "bl1", 1, None, None),
+           4: (3, None, None, 2, ublk(3), "Uc3"), 5: (2, blk(T.bl, 2, 8), "bl2", 0, None, None),
+           6: (9, T.stu[:, 16:24], "stu", 0, None, None)}
+    for m in range(7):
+        u = "E%d" % m
+        c, cf, cfk = cand[m]
+        part[0] = u
+        gather(u, blk(T.cu, c), "cu%d" % c, TOP[m])
+        dist(u, LEV[m], [(T.X16, 128 * t) for t in TIMES[m]], "X16")
+        elect(m, cf, cfk)
+        part[0] = "X%d" % m
+        extend(m, *opn[m])
+        part[0] = "S%d" % m
+        snap(m)
+        part[0] = "M%d" % m
+        mix(u, LEV[m], m)
+    part[0] = "F"
+    fix(0, 0, 3, "R0")
+    fix(1, 0, 4, "R0")
+    fix(2, 1, 4, "R1")
+    for m in (2, 3, 0, 1, 4, 5, 6):
+        u = "R%d" % m
+        part[0] = u
+        rem = {2: 0, 5: 1, 6: 2}.get(m)
+        if rem is not None:
+            gather(u, blk(T.rcu, rem), "rc%d" % m, m + 1)
+            dist(u, 0, [(T.rxt, 128 * rem)], "rc%d" % m)
+        else:
+            if m == 4:
+                gather(u, blk(T.cu, 4), "cu4", 5)
+            dist(u, 0, [(T.nxt, 128 * m)], "nxt%d" % m)
+        mix(u, 0, m)
+    return ops, bank
+
+
+def depend(ops, C):
+    lw, rs = {}, {}
+    for k, o in enumerate(ops):
+        d = set()
+        for x in o["rd"]:
+            d.add(lw[x])
+        for x in o["wr"]:
+            if x in lw:
+                d.add(lw[x])
+            d.update(rs.get(x, []))
+        d.discard(k)
+        same = set(x for x in d if o["eng"] == "p" and ops[x]["eng"] == "p" and o["wr"] == ops[x]["wr"])
+        o["dep"] = d - same
+        o["lag"] = [(x, 0.0 if x in same else after(ops[x], C)) for x in sorted(d)]
+        for x in o["rd"]:
+            rs.setdefault(x, []).append(k)
+        for x in o["wr"]:
+            lw[x] = k
+            rs[x] = []
+
+
+def after(o, C):
+    return o["lat"] if o["kind"] == "a" else C["dma"] if o["kind"] == "d" else C["lat"]
+
+
+def plan(ops, C, boost=None):
+    n = len(ops)
+    boost = BOOST if boost is None else boost
+    pr = [0.0] * n
+    cost = [o["cost"] for o in ops]
+    eng = [o["eng"] for o in ops]
+    acq = [o["acq"] for o in ops]
+    for k in range(n - 1, -1, -1):
+        pr[k] = max(pr[k], boost.get(ops[k]["part"], 0.0)) + cost[k]
+        for d, lag in ops[k]["lag"]:
+            if pr[k] + lag > pr[d]:
+                pr[d] = pr[k] + lag
+    rels, users = {}, [[] for o in ops]
+    for k, o in enumerate(ops):
+        pr[k] += boost.get(o["part"] + o["eng"], 0.0) + boost.get(o["name"], 0.0)
+        if o["rel"]:
+            rels.setdefault(o["rel"], []).append(k)
+        for d, lag in o["lag"]:
+            users[d].append((k, lag))
+    fin = [0.0] * n
+    holder, bfree, held = [None] * 8, [0.0] * 8, {}
+    banks, extra, order = {}, {}, []
+    wait = [len(o["lag"]) for o in ops]
+    rdy = [0.0] * n
+    left = {e: [] for e in eng}
+    free = {e: 0.0 for e in eng}
+    for k in range(n):
+        if not wait[k]:
+            left[eng[k]].append(k)
+    far = 1e30
+    for step in range(n):
+        one, two = min(bfree), min(max(bfree[x], bfree[x + 1]) for x in (0, 2, 4, 6))
+        t0, e0 = far, None
+        for e, ks in left.items():
+            if ks:
+                if e == "p":
+                    t = min(max(rdy[k], (0.0, one, two)[acq[k][1]]) if acq[k] else rdy[k] for k in ks)
+                else:
+                    t = min(rdy[k] for k in ks)
+                t = max(t, free[e])
+                if t < t0:
+                    t0, e0 = t, e
+        k, t = None, 0.0
+        for x in left[e0]:
+            tx = max(rdy[x], (0.0, one, two)[acq[x][1]]) if acq[x] else rdy[x]
+            if tx <= t0 + SLACK and (k is None or pr[x] > pr[k]):
+                k, t = x, max(tx, t0)
+        o = ops[k]
+        if acq[k]:
+            h, w = acq[k]
+            fit = [b for b in range(0, 8, w) if max(bfree[b:b + w]) <= t]
+            b = fit[0] if w == 2 else max(fit, key=lambda x: (bfree[x ^ 1] > t, x))
+            banks[h] = b
+            extra[k] = [r for x in range(b, b + w) if holder[x] for r in rels[holder[x]]]
+            held[h] = [len(rels[h]), 0.0, b, w]
+            for x in range(b, b + w):
+                holder[x] = h
+                bfree[x] = far
+        fin[k] = free[e0] = t + cost[k]
+        if o["rel"]:
+            z = held[o["rel"]]
+            z[0] -= 1
+            z[1] = max(z[1], fin[k] + C["lat"])
+            if not z[0]:
+                for x in range(z[2], z[2] + z[3]):
+                    bfree[x] = z[1]
+        order.append(k)
+        left[e0].remove(k)
+        for x, lag in users[k]:
+            wait[x] -= 1
+            if fin[k] + lag > rdy[x]:
+                rdy[x] = fin[k] + lag
+            if not wait[x]:
+                left[eng[x]].append(x)
+    return order, banks, extra, fin
+
+
+def replay(ops, order, extra, C):
+    fin, free = [0.0] * len(ops), {}
+    for k in order:
+        o = ops[k]
+        t = free.get(o["eng"], 0.0)
+        for d, lag in o["lag"]:
+            if fin[d] + lag > t:
+                t = fin[d] + lag
+        for d in extra.get(k, ()):
+            if fin[d] + C["lat"] > t:
+                t = fin[d] + C["lat"]
+        fin[k] = free[o["eng"]] = t + o["cost"]
+    return max(fin) + C["dma"]
+
+
+def search(T, topo, core, rounds):
+    sets = []
+    for ch in VARY:
+        C = dict(COST)
+        C.update(ch)
+        ops = build(T, topo, core, C)[0]
+        depend(ops, C)
+        sets.append((ops, C))
+    ops, C = sets[0]
+    names = sorted(set(o["part"] + o["eng"] for o in ops if o["eng"] in "vspg")) + sorted(set(o["part"] for o in ops))
+    single = [o["name"] for o in ops if o["eng"] in "vspg"]
+    seed = [12345]
+
+    def rnd():
+        seed[0] = (seed[0] * 1103515245 + 12345) % 2147483648
+        return (seed[0] >> 8) / 8388608.0
+
+    def value(b):
+        p = plan(ops, C, b)
+        r = [replay(o, p[0], p[2], c) for o, c in sets]
+        return (r[0] + sum(r)) / (len(r) + 1), p, r
+    cur = dict(BOOST)
+    now = best = value(cur)
+    for j in range(rounds):
+        b = dict(cur)
+        for z in range(1 + int(rnd() * 2.5)):
+            pool = names if rnd() < 0.6 else single
+            x = pool[int(rnd() * len(pool))]
+            b[x] = b.get(x, 0.0) + (rnd() + rnd() - 1.0) * (4000.0, 16000.0, 50000.0)[int(rnd() * 3)]
+        v = value(b)
+        if v[0] <= now[0] or rnd() < math.exp((now[0] - v[0]) / (400.0 * (1.0 - j / rounds))):
+            cur, now = b, v
+            if v[0] < best[0]:
+                best = v
+    return best
+
+
+PLAN = {}
+
+
+def rank_program(g, core, T, topo):
+    if T.rank_of(core) is None:
+        return
+    ops, bank = build(T, topo, core, COST)
+    depend(ops, COST)
+    if not PLAN:
+        PLAN["p"] = search(T, topo, core, ROUNDS)[1]
+    order, banks, extra, fin = PLAN["p"]
+    bank.update(banks)
+    Q = {"v": g.vector, "s": g.scalar, "p": g.tensor, "g": g, "y": g.sync}
+    total = {s: 0 for s in SEMAPHORES}
+    mark, seen, alone = {}, {}, [False]
+    for k in order:
+        o = ops[k]
+        if o["kind"] == "w":
+            total[o["sem"]] = o["fn"]
+            mark[k] = (o["sem"], o["fn"])
+            continue
+        q = Q[o["eng"]]
+        need = {}
+        for d in list(o["dep"]) + extra.get(k, []):
+            s, v = mark[d]
+            need[s] = max(need.get(s, 0), v)
+        if o["eng"] == "g" and o["kind"] == "c":
+            if o["name"][:3] == "Sel" or alone[0]:
+                need["cg"] = total["cg"]
+            alone[0] = o["name"][:3] == "Sel"
+        for s, v in sorted(need.items()):
+            if seen.get((o["eng"], s), 0) < v:
+                q.wait_ge(T.sem[s], v)
+                seen[(o["eng"], s)] = v
+        if o["kind"] == "r":
+            total["sent"] += o["fn"](q)
+            mark[k] = ("sent", 0)
+            continue
+        s, inc = (o["sem"], 16) if o["kind"] in "da" else (CSEM[o["eng"]], 1)
+        for ins in o["fn"](q):
+            ins.then_inc(T.sem[s], inc)
+            total[s] += inc
+        mark[k] = (s, total[s])
+    for s in SEMAPHORES:
+        if total[s]:
+            g.wait_ge(T.sem[s], total[s])

@@ -1,93 +1,107 @@
 import math
 from concourse.bass import DstId, RemoteDMATransfer
-from concourse.mybir import AluOpType as Alu, AxisListType as Ax, ActivationFunctionType as Act
+from concourse.mybir import AluOpType as Alu, ActivationFunctionType as Act
 
 F, S, W = 864, 128, 1760
+SP = 32
 LEV = [0, 0, 1, 0, 0, 1, 2]
 TIMES = [[0], [1], [0, 1], [2], [3], [2, 3], [0, 1, 2, 3]]
 TOP = [0, 1, 0, 2, 4, 3, 0]
 BIG = float(2 ** 23)
 MAG = float(3 * 2 ** 22)
-SUMV = {"R4", "R5", "R6"}
-HALVE = {"E0": 4, "E1": 4, "E2": 3, "E3": 4, "E4": 4, "E5": 3, "E6": 3, "R0": 3, "R1": 3, "R2": 4, "R3": 4,
-         "R4": 0, "R5": 0, "R6": 0}
+SETS = {"E0": ["E0"], "E1": ["E1"], "E2": ["E2"], "E6": ["E6"], "E3": ["E3"], "E4": ["E4"], "E5": ["E5"], "R23": ["R2", "R3"], "R01": ["R0", "R1"]}
+WIDE = {"E0": 2, "E1": 2, "E2": 4, "E6": 4, "E5": 4, "E4": 4, "E3": 4, "R23": 2}
+FOLD = ["E0", "E1", "E2", "E6", "E3", "R01", "E5", "E4", "R23"]
+HALVE = {"E01": 4, "E26": 3, "E35": 4, "E4": 3, "R01": 5, "R23": 4, "R56": 4}
+SCAN = ["R4", "R5", "R6"]
+WARM = ["hl"] if SCAN else []
+RELU = {}
+PART = {"R01": 14, "R23": 4}
+APART = list(WIDE)
 FINE = {"E0", "E1", "E3", "E4"}
-AEOF = {"E0": 0, "E1": 1, "E2": 2, "E3": 3, "E4": 4, "E5": 5, "E6": 6, "R0": 7, "R1": 8, "R2": 9, "R3": 10,
-        "R4": 0, "R5": 1, "R6": 2}
-AEOF.update({"R5": 11, "R6": 12})
-SCOF = {"R2": 2, "R3": 1, "R4": 1, "R5": 2, "R6": 3}
-LATE = {("R0", 3): 0, ("R0", 4): 1, ("R1", 4): 2}
-ONV = {"yz4", "yz5", "yz6", "yz0", "yz1", "ym5", "ym6"}
-SMALL = set()
-ONS = {"cf1", "cf2", "Uc0", "Uc1", "old2", "old3", "cf3", "Uc3"}
-ROUNDS = 4000
-VARY = ({}, {"gam": 1.15, "fix": 25.0}, {"gam": 1.95, "sca": 5.5, "fix": 100.0, "lat": 180.0}, {"pe": 0.62, "gdma": 1400.0, "bw": 150.0})
+EARLY = {"E0", "E1", "E3", "E4"}
+GOF = {"E0": 0, "E1": 1, "E3": 3, "E4": 4, "R0": 1, "R1": 3, "R3": 4, "R4": 0, "R5": 1, "R6": 4}
+ORDER01 = [0, 1, 2] + list(range(5, 16)) + [3, 4]
+CONV = set()
+QUART = set()
+ONS = {"X16", "gE0_0", "cf0", "gE1_0", "gE3_0"}
+ROUNDS = 30
+MORE = 60001
+SOFT, HEAT = 0.3, 150.0
+SOFT2 = 0.05
+HEAT2 = 250.0
+VARY = ({}, {"cyc": 0.85, "pe": 0.43, "fw": 350.0, "row": 50.0, "back": 5000.0, "gam": 1.6, "norm": 0.95},
+        {"cyc": 0.85, "pe": 0.43, "dma": 3200.0, "rem": 5500.0, "lat": 150.0, "back": 6000.0, "call": 2000.0, "norm": 0.95})
 RANK = "E0:200 E1:150 E3:100 E4:40 S0:180 S1:130 S3:60 S4:20 E2:60 S2:60 X0:170 X1:120 X3:60"
 BOOST = {x.split(":")[0]: 1000.0 * int(x.split(":")[1]) for x in RANK.split()}
-GOF = {"E0": 0, "E1": 1, "E2": 2, "E3": 3, "E4": 4, "E5": 5, "E6": 6, "R0": 1, "R1": 3, "R3": 4,
-       "R2": 7, "R4": 0, "R5": 2, "R6": 6}
-SLACK = 250.0
 
 f32, f16, b16, i32, u16 = "float32", "float16", "bfloat16", "int32", "uint16"
 SCRATCH = {
-    "Pt": ("sbuf", [128, W], i32), "Ut": ("sbuf", [128, 128 + W], f32), "sui": ("sbuf", [128, F], i32),
-    "sti": ("sbuf", [128, 24], i32), "stu": ("sbuf", [128, 24], u16), "stf": ("sbuf", [128, 24], f32),
-    "xsi": ("sbuf", [128, 512], i32), "X16": ("sbuf", [128, 512], f16), "lnh": ("sbuf", [128, 16], f32),
-    "hvb": ("sbuf", [128, 16], b16), "hvf": ("sbuf", [128, 16], f32), "hrec": ("sbuf", [128, 16], f32),
-    "r16": ("sbuf", [128, 16], f32), "RT": ("sbuf", [128, 1024], f32),
-    "ones": ("sbuf", [128, 144], f32), "zer": ("sbuf", [128, 144], f32), "one16": ("sbuf", [128, 128], b16),
+    "Pt": ("sbuf", [128, W], i32), "Ut": ("sbuf", [128, SP + W], f32), "U2": ("sbuf", [128, SP + F + 384], f32),
+    "sui": ("sbuf", [128, F], i32), "sti": ("sbuf", [128, 24], i32), "stu": ("sbuf", [128, 44], u16),
+    "xsi": ("sbuf", [128, 512], i32), "X16": ("sbuf", [128, 512], f16),
+    "hvb": ("sbuf", [128, 16], b16), "hrec": ("sbuf", [128, 16], f32),
+    "lnh": ("sbuf", [128, 32], f32), "hl": ("sbuf", [128, 8], f32), "RT": ("sbuf", [128, 1024], f32),
+    "ones": ("sbuf", [128, 128], f32), "zer": ("sbuf", [128, 128], f32), "one16": ("sbuf", [128, 128], b16),
     "cm16": ("sbuf", [128, 128], b16),
     "idf": ("sbuf", [128, 128], f32), "idh": ("sbuf", [128, 128], f32), "IDS": ("sbuf", [128, 8 * 128], b16),
-    "RB": ("sbuf", [128, 144], b16), "RA": ("sbuf", [128, 1032], b16), "CC": ("sbuf", [128, 1032], b16),
-    "rowp": ("sbuf", [128, 144], f32), "io129": ("sbuf", [128, 144], f32),
-    "Sel": ("sbuf", [128, 512], b16),
-    "BO": ("sbuf", [128, 8], f32), "BO1": ("sbuf", [128, 8], f32), "G8f": ("sbuf", [128, 8], f32),
-    "G8": ("sbuf", [128, 8], b16),
-    "BBf": ("sbuf", [128, 128], f32), "BB": ("sbuf", [128, 128], b16), "sel34": ("sbuf", [128, 256], f32),
-    "mri": ("sbuf", [128, 128], i32), "mrj": ("sbuf", [128, 128], i32), "mR": ("sbuf", [128, 128], f32),
-    "negm": ("sbuf", [128, 128], b16),
-    "keyf": ("sbuf", [128, 144], f32), "keyc": ("sbuf", [128, 144], b16), "rst": ("sbuf", [128, 144], f32),
-    "rst16": ("sbuf", [128, 128], f32),
-    "DmA": ("sbuf", [128, 144], f32), "DmB": ("sbuf", [128, 144], f32), "Dm": ("sbuf", [128, 144], f32),
-    "pi": ("sbuf", [128, 64], i32), "pj": ("sbuf", [128, 64], i32), "rl": ("sbuf", [128, 64], u16),
-    "rcol": ("sbuf", [128, 8], f32), "c18": ("sbuf", [128, 16], f32), "c2": ("sbuf", [128, 16], f32),
-    "c2b": ("sbuf", [128, 16], f32), "c2c": ("sbuf", [128, 16], f32),
-    "bc18": ("sbuf", [128, 16], u16), "bcv": ("sbuf", [128, 16], u16), "bc8": ("sbuf", [128, 16], u16),
-    "c1": ("sbuf", [128, 16], f32), "scol": ("sbuf", [128, 8], f32), "sb": ("sbuf", [128, 8], f32),
-    "CT": ("sbuf", [128, 128], f32), "mins": ("sbuf", [128, 56], f32), "io896": ("sbuf", [128, 896], f32),
-    "BM": ("sbuf", [128, 7 * 128], f32),
+    "Sel": ("sbuf", [128, 512], b16), "n32": ("sbuf", [128, 32], f32),
+    "BO": ("sbuf", [128, 24], f32), "BO1": ("sbuf", [128, 8], f32), "G8": ("sbuf", [128, 8], b16),
+    "BN": ("sbuf", [128, 384], b16), "nBB": ("sbuf", [128, 128], b16), "sel34": ("sbuf", [128, 256], f32),
+    "mR": ("sbuf", [128, 128], f32), "posm": ("sbuf", [128, 128], b16),
+    "kio": ("sbuf", [128, 256], b16), "TM": ("sbuf", [128, 256], b16), "rst": ("sbuf", [128, 384], f32),
+    "QA": ("sbuf", [128, 16], f32), "QB": ("sbuf", [128, 16], f32), "QE": ("sbuf", [128, 16], b16),
+    "DmA": ("sbuf", [128, 128], f32), "Dm": ("sbuf", [128, 128], f32),
+    "pi": ("sbuf", [128, 8], i32), "pj": ("sbuf", [128, 16], i32), "pf": ("sbuf", [128, 8], f32), "pg": ("sbuf", [128, 16], f32),
+    "lt": ("sbuf", [128, 8], u16), "TT": ("sbuf", [128, 512], f32), "XR": ("sbuf", [128, 2048], f32),
+    "lf": ("sbuf", [128, 40], f32), "lu": ("sbuf", [128, 40], u16), "BM": ("sbuf", [128, 896], f32),
     "cu": ("sbuf", [128, 10 * 128], u16),
-    "cf": ("sbuf", [128, 4 * 128], f32),
+    "cf": ("sbuf", [128, 4 * 144], f32),
     "rcu": ("sbuf", [128, 3 * 128], u16), "rxt": ("sbuf", [128, 3 * 128], f16),
     "snew": ("sbuf", [128, 3 * 128], i32), "nxt": ("sbuf", [128, 7 * 128], f16),
-    "rm": ("sbuf", [128, 7 * 144], f32), "stp": ("sbuf", [128, 7 * 144], f32), "val": ("sbuf", [128, 7 * 144], f32),
-    "M1": ("sbuf", [128, 3 * 128], f16), "A12": ("sbuf", [128, 10 * 256], f16),
-    "bl": ("sbuf", [128, 7 * 8], u16), "Pb": ("sbuf", [128, 7 * 128], f16),
-    "offf": ("sbuf", [128, 7 * 8], f32), "offu": ("sbuf", [128, 7 * 8], u16), "old": ("sbuf", [128, 7 * 128], f32),
-    "fxs": ("sbuf", [128, 384], f32), "fxu": ("sbuf", [128, 24], u16),
-    "prod": ("sbuf", [128, 3 * 128], f32), "ymb": ("sbuf", [128, 896], f32), "yzb": ("sbuf", [128, 896], f32),
-    "GX": ("sbuf", [128, 384], f16), "U2": ("sbuf", [128, 512 + F], f32),
+    "rm": ("sbuf", [128, 5 * 128], f32), "kp": ("sbuf", [128, 5 * 128], b16), "val": ("sbuf", [128, 5 * 128], f32),
+    "M1": ("sbuf", [128, 3 * 128], f16), "A1": ("sbuf", [128, 10 * 128], f16), "A2": ("sbuf", [128, 4 * 128], f16),
+    "bl": ("sbuf", [128, 7 * 10], u16), "Pb": ("sbuf", [128, 7 * 128], f16),
+    "eq": ("sbuf", [128, 3 * 256], b16), "offu": ("sbuf", [128, 7 * 8], u16), "old": ("sbuf", [128, 4 * 128], f32),
+    "fxu": ("sbuf", [128, 24], u16), "GX": ("sbuf", [128, 384], f16),
+    "prod": ("sbuf", [128, 3 * 128], f32), "yzb": ("sbuf", [128, 3 * 128], f32),
+    "pos": ("sbuf", [128, 2 * 1024 if RELU else 16], f16), "DmB": ("sbuf", [128, 128], b16),
+    "SC": ("sbuf", [128, 2048], f32), "RES": ("sbuf", [128, 128 * sum(len(SETS[_k]) * WIDE.get(_k, 1) for _k in FOLD) or 8], f32),
 }
-for _k in range(max(AEOF.values()) + 1):
-    SCRATCH["AE%d" % _k] = ("sbuf", [128, 2048], f32)
-for _k in range(8):
+ROT = [0, 1, 2, 0, 1, 3, 4]
+for _k in SETS:
+    SCRATCH["A" + _k] = ("sbuf", [128, len(SETS[_k]), 2048] if _k in APART else [128, 16, len(SETS[_k]), 128], f32)
+for _k in SCAN:
+    SCRATCH["A" + _k] = ("sbuf", [128, 2048], f32)
+for _k in sorted(set(GOF.values())):
     SCRATCH["G%d" % _k] = ("sbuf", [128, 2048], f16)
 for _k in range(4):
     SCRATCH["ps%d" % _k] = ("psum", [128, 1024], f32)
-SEMAPHORES = ["cv", "cs", "cp", "cg", "sto", "sent", "arr2", "arr5", "arr6", "ld0", "ld1", "ld2", "ld3", "ld4", "cpu", "rt"] + ["a" + _u for _u in AEOF] + ["t" + _u for _u in AEOF]
+SEMAPHORES = (["cv", "cs", "cp", "cg", "sent", "arr2", "arr5", "arr6", "ld0", "ld1", "ld2", "ld3", "ld4", "cpu", "cpv", "rt", "bz", "bm", "xr0", "xr1", "xr2", "xr3"]
+              + [_x + _u for _u in SETS for _x in "afb"] + ["t%d" % _u for _u in range(14)])
 CSEM = {"v": "cv", "s": "cs", "p": "cp", "g": "cg"}
-COST = {"cyc": 1.0, "pe": 0.52, "gam": 1.56, "sca": 3.8, "fix": 60.0, "lat": 90.0, "dma": 2300.0, "rem": 3500.0,
-        "gdma": 1000.0, "bw": 250.0}
+COST = {"norm": 1.0, "cyc": 0.96, "pe": 0.48, "pfix": 5.0, "gam": 1.56, "sca": 3.8, "fix": 60.0, "lat": 90.0, "dma": 2200.0,
+        "rem": 3500.0, "gdma": 800.0, "bw": 280.0, "fw": 650.0, "row": 28.0, "back": 3500.0, "tti": 0.3, "call": 1000.0}
+
+
+def helpers(T, topo, core):
+    return [c for c in topo.cores_of(core) if T.rank_of(c) is None and topo.die(c) == topo.die(core)]
+
+
+def result(T, k):
+    a = 128 * sum(len(SETS[x]) * WIDE.get(x, 1) for x in FOLD[:FOLD.index(k)])
+    return T.RES[:, a:a + 128 * len(SETS[k]) * WIDE.get(k, 1)]
 
 
 def build(T, topo, core, C):
     ops = []
     bank = {}
     part = ["C"]
+    setof = {u: (k, j) for k in SETS for j, u in enumerate(SETS[k])}
 
-    def op(name, eng, fn, rd, wr, cost, kind="c", sem=None, acq=None, rel=None):
+    def op(name, eng, fn, rd, wr, cost, kind="c", sem=None, acq=None, rel=None, lat=None):
         ops.append({"name": name, "eng": eng, "fn": fn, "rd": list(rd), "wr": list(wr), "cost": cost, "kind": kind,
-                    "sem": sem, "acq": acq, "rel": rel, "part": part[0]})
+                    "sem": sem, "acq": acq, "rel": rel, "part": part[0], "lat": C["lat"] if lat is None else lat})
 
     def cv(n, k=1.0):
         return C["fix"] + max(64, n * k) * C["cyc"]
@@ -95,8 +109,8 @@ def build(T, topo, core, C):
     def cg(n):
         return C["fix"] + n * C["gam"] * C["cyc"]
 
-    def cp(n):
-        return C["fix"] + n * C["pe"]
+    def cp(n, calls):
+        return C["fix"] + n * C["pe"] + calls * C["pfix"]
 
     def ps(h, a, b, st=1):
         k = bank[h]
@@ -115,8 +129,8 @@ def build(T, topo, core, C):
         else:
             op(name, "g", lambda q: [q.iota(out, pat, base, cm)], [], [name], 130 + 2 * n * C["cyc"])
 
-    def ga(name, out, in_, rd, pat, cmp, fill, base, cm, n):
-        op(name, "g", lambda q: [q.affine_select(out, in_, pat, cmp, fill, base, cm)], rd, [name], 170 + 2 * n * C["cyc"])
+    def ga(name, out, in_, rd, pat, cmp, fill, base, cm, n, wr=None):
+        op(name, "g", lambda q: [q.affine_select(out, in_, pat, cmp, fill, base, cm)], rd, [wr or name], 170 + 2 * n * C["cyc"])
 
     def vts(name, out, in0, s1, s2, o0, o1, rd, n, wr=None, cost=None, **kw):
         if o1 is None:
@@ -131,116 +145,108 @@ def build(T, topo, core, C):
     def vtt(name, out, a, b, o, rd, n, wr=None, cost=None):
         op(name, "v", lambda q: [q.tensor_tensor(out, a, b, o)], rd, wr or [name], cost or cv(n, 2))
 
+    def vset(name, out, x, n, rd=()):
+        op(name, "v", lambda q: [q.memset(out, x)], rd, [name], cv(n))
+
     def sact(name, out, in_, func, rd, n, wr=None, cost=None, **kw):
         op(name, "s", lambda q: [q.activation(out, in_, func, **kw)], rd, wr or [name], cost or cv(n))
 
-    for k, (nm, eng, o, i) in enumerate([("sti", "y", T.sti[:], T.st[:]), ("sui", "y", T.sui[:], T.su[:]),
-                                         ("P0", "s", T.Pt[:, 0:F], T.th[:]), ("xsi", "y", T.xsi[:], T.xs[:]),
-                                         ("hvb", "y", T.hvb[:], T.hv[:])]):
-        op(nm, eng, lambda q, o=o, i=i: [q.dma_start(o, i)], [], [nm], 60.0, kind="d", sem="ld%d" % k)
+    def both(name, out, in_, rd, cost, plus=None, wr=None, rel=None):
+        def fn(q, e):
+            b = ps(rel, 0, in_ or 128) if rel else in_
+            if e == "s":
+                return [q.activation(out, b, Act.Copy) if plus is None else q.activation(out, b, Act.Identity, bias=plus)]
+            return [q.tensor_copy(out, b) if plus is None else q.tensor_scalar(out, b, plus, None, Alu.add)]
+        op(name, "vs", fn, rd, wr or [name], cost, rel=rel)
 
-    op("ones", "v", lambda q: [q.memset(T.ones[:], 1.0)], [], ["ones"], cv(144))
-    op("zer", "v", lambda q: [q.memset(T.zer[:], 0.0)], [], ["zer"], cv(144))
-    op("one16", "v", lambda q: [q.memset(T.one16[:], 1.0)], [], ["one16"], cv(64))
-    op("cm16", "v", lambda q: [q.memset(T.cm16[:], -15.0 / 32)], [], ["cm16"], cv(64))
-    ga("idf", T.idf[:], T.ones[:, 0:128], ["ones"], [[-1, 128]], Alu.is_equal, 0.0, 0, 1, 128)
-    for k, sc in enumerate([1.0, 2.0, 4.0, 0.75, 0.25, 0.125, 0.0625, -1.0]):
-        if k in (0, 7):
+    def dma(name, eng, pairs, rd, wr, sem, size=0):
+        op(name, eng, lambda q: [q.dma_start(o, i) for o, i in pairs], rd, wr, 60.0 * len(pairs), kind="d", sem=sem, lat=C["dma"] + size / 500.0)
+
+    def add(name, out, in_, rd, wr, sem, size):
+        op(name, "g", lambda q: [q.dma_start(out, in_, accum_op=Alu.add, max_dma_last_dim=8192)], rd, wr + [name], C["gdma"], kind="d",
+           sem=sem, lat=C["dma"] / 2)
+        op(name + "d", "D", len(ops) - 1, rd + [name], wr, size / C["bw"], kind="e", lat=C["dma"] / 2)
+
+    dma("sti", "y", [(T.sti[:], T.st[:])], [], ["sti"], "ld0")
+    dma("sui", "y", [(T.sui[:], T.su[:])], [], ["sui"], "ld1")
+    dma("P0", "s", [(T.Pt[:, 0:F], T.th[:])], [], ["P0"], "ld2")
+    dma("xsi", "y", [(T.xsi[:], T.xs[:])], [], ["xsi"], "ld3")
+    dma("hvb", "y", [(T.hvb[:], T.hv[:])], [], ["hvb"], "ld4")
+
+    vset("ones", T.ones[:], 1.0, 128)
+    vset("zer", T.zer[:], 0.0, 128)
+    vset("one16", T.one16[:], 1.0, 64)
+    vset("cm16", T.cm16[:], -15.0 / 32, 64)
+    vset("QA", T.QA[:], -4096.0, 16)
+    ga("idf", T.idf[:], T.ones[:], ["ones"], [[-1, 128]], Alu.is_equal, 0.0, 0, 1, 128)
+    for k, sc in enumerate([1.0, 0.5, -2.0, 0.75, 0.25, 0.125, 0.0625, -1.0]):
+        if k == 2 and not RELU:
+            continue
+        if k in (0, 3, 4, 7):
             sact("I%d" % k, ident(k), T.idf[:], Act.Copy, ["idf"], 128, scale=sc)
         else:
-            ga("I%d" % k, ident(k), T.zer[:, 0:128], ["zer"], [[-1, 128]], Alu.not_equal, sc, 0, 1, 128)
-    ga("idh", T.idh[:], T.zer[:, 0:128], ["zer"], [[-1, 128]], Alu.not_equal, 0.5, 0, 1, 128)
-    op("RB0", "v", lambda q: [q.memset(T.RB[:, 0:1], 0.0)], [], ["RB0"], cv(1))
-    sact("RB", T.RB[:, 1:129], T.idf[:], Act.Copy, ["idf"], 128, scale=4096.0)
+            ga("I%d" % k, ident(k), T.zer[:], ["zer"], [[-1, 128]], Alu.not_equal, sc, 0, 1, 128)
+    ga("idh", T.idh[:], T.zer[:], ["zer"], [[-1, 128]], Alu.not_equal, 0.5, 0, 1, 128)
     ga("BO1", T.BO1[:], T.ones[:, 0:8], ["ones"], [[-16, 8]], Alu.is_ge, 0.0, 0, 1, 8)
-    ga("G8f", T.G8f[:], T.BO1[:], ["BO1"], [[16, 8]], Alu.is_ge, 0.0, 15, -1, 8)
-    sact("BO", T.BO[:], T.G8f[:], Act.Copy, ["G8f"], 8, scale=16.0)
-    sact("G8", T.G8[:], T.G8f[:], Act.Copy, ["G8f"], 8)
-    gi("c1", T.c1[:], [[1, 16]], 0, 0, 16)
-    vcp("bc8", T.bc8[:], T.c1[:], ["c1"], 16)
-    sact("BBf", T.BBf[:], T.G8f[:].indirect(T.bc8[:, 0:8]), Act.Copy, ["G8f", "bc8"], 128, cost=cg(128))
-    sact("BB", T.BB[:], T.BBf[:], Act.Copy, ["BBf"], 128)
-    gi("mri", T.mri[:], [[-1, 128]], 0, 1, 128, False)
-    vts("mrj", T.mrj[:], T.mri[:], 15, None, Alu.bitwise_and, None, ["mri"], 128)
-    vts("mR", T.mR[:], T.mrj[:], 0.0, None, Alu.is_equal, None, ["mrj"], 128)
-    sact("negm", T.negm[:], T.mR[:], Act.Identity, ["mR"], 128, scale=4096.0, bias=-4096.0)
+    ga("G8", T.G8[:], T.BO1[:], ["BO1"], [[16, 8]], Alu.is_ge, 0.0, 15, -1, 8)
+    for l in range(3):
+        sact("BO%d" % l, blk(T.BO, l, 8), T.G8[:], Act.Copy, ["G8"], 8, scale=16.0 * (1 << l))
+    gi("lf0", T.lf[:, 0:32], [[1, 32]], 0, 0, 32)
+    gi("lf1", T.lf[:, 32:40], [[16, 8]], 15, 0, 8)
+    vcp("lu", T.lu[:], T.lf[:], ["lf0", "lf1"], 40)
+    ga("nB1", T.DmB[:], T.zer[:], ["zer"], [[16, 8], [0, 16]], Alu.is_gt, -1.0, 0, -1, 128)
+    ga("nBB", T.nBB[:], T.DmB[:], ["nB1"], [[16, 8], [0, 16]], Alu.is_ge, 0.0, 15, -1, 128)
+    for e in range(2):
+        ga("BM%d" % e, blk(T.BN, 2), T.ones[:], ["ones"], [[-32, 4], [0, 32]], Alu.is_ge, 0.0, -16 * e, 1, 128, "BNt")
+        ga("BN%d" % e, blk(T.BN, e), blk(T.BN, 2), ["BNt"], [[32, 4], [0, 32]], Alu.is_ge, 0.0, 15 + 16 * e, -1, 128)
+    gi("pi", T.pi[:], [[0, 8]], 0, 1, 8, False)
+    vts("pj0", T.pj[:, 0:2], T.pi[:, 0:2], 15, None, Alu.bitwise_and, None, ["pi"], 2)
+    vts("pj1", T.pj[:, 2:4], T.pi[:, 2:4], 31, None, Alu.bitwise_and, None, ["pi"], 2)
+    vcp("pf", T.pf[:, 0:4], T.pj[:, 0:4], ["pj0", "pj1"], 4)
+    sact("pf4", T.pf[:, 4:5], T.pf[:, 0:1], Act.Identity, ["pf"], 1, bias=16.0)
+    sact("pf5", T.pf[:, 5:6], T.pf[:, 2:3], Act.Identity, ["pf"], 1, scale=4096.0, bias=4096.0)
+    for j, (sh, mask) in enumerate([(4, 1), (0, 1), (1, 3), (3, 1)]):
+        vts("pb%d" % j, T.pj[:, 4 + j:5 + j], T.pi[:, 0:1], sh, mask, Alu.logical_shift_right, Alu.bitwise_and, ["pi"], 1)
+    vcp("pc", T.pg[:, 0:4], T.pj[:, 4:8], ["pb0", "pb1", "pb2", "pb3"], 4)
+    vtt("pd", T.pg[:, 4:5], T.pg[:, 0:1], T.pg[:, 1:2], Alu.not_equal, ["pc"], 1)
+    vtt("pe", T.pg[:, 5:6], T.pg[:, 0:1], T.pg[:, 1:2], Alu.is_gt, ["pc"], 1)
+    vts("ph", T.pj[:, 8:9], T.pg[:, 2:3], 4.0, T.pg[:, 5:6], Alu.add, Alu.subtract, ["pc", "pe"], 1)
+    vts("pk", T.pj[:, 9:10], T.pj[:, 8:9], 3, None, Alu.bitwise_and, None, ["ph"], 1)
+    vts("pl", T.pg[:, 6:7], T.pj[:, 9:10], 32.0, T.pg[:, 3:4], Alu.mult, Alu.add, ["pk", "pc"], 1)
+    vts("pm", T.pg[:, 7:8], T.pg[:, 0:1], 16.0, T.pg[:, 6:7], Alu.mult, Alu.add, ["pl", "pc"], 1)
+    vts("pn", T.pg[:, 8:9], T.pg[:, 4:5], 128.0, T.pg[:, 7:8], Alu.mult, Alu.add, ["pm", "pd"], 1)
+    vts("lt", T.lt[:], T.lf[:, 0:8], 2.0, T.pg[:, 8:9], Alu.mult, Alu.add, ["lf0", "pn"], 8)
+    gi("kio", T.kio[:], [[16, 2], [0, 8], [1, 16]], 0, 0, 256)
+    vts("mR", T.mR[:], blk(T.kio, 0), T.pf[:, 0:1], None, Alu.is_equal, None, ["kio", "pf"], 128)
+    sact("TM", T.TM[:], T.kio[:], Act.Relu, ["kio", "pf5"], 256, scale=-4096.0, bias=T.pf[:, 5:6])
+    sact("posm", T.posm[:], T.mR[:], Act.Identity, ["mR"], 128, scale=-4096.0, bias=4096.0)
     for k in range(2):
-        sact("sel%d" % (3 + k), blk(T.sel34, k), T.BBf[:], Act.Copy, ["BBf", "mR"], 128, scale=T.mR[:, 3 + k:4 + k])
-    gi("keyf", T.keyf[:], [[0, 8], [1, 18]], -2, 0, 144)
-    ga("keyc", T.keyc[:], T.keyf[:], ["keyf"], [[0, 8], [1, 18]], Alu.is_ge, BIG, -2, 0, 144)
-    ga("rst", T.rst[:], T.zer[:, 0:144], ["zer"], [[0, 8], [1, 18]], Alu.not_equal, BIG, 0, 0, 144)
-    ga("rst16", T.rst16[:], T.zer[:, 0:128], ["zer"], [[0, 8], [1, 16]], Alu.not_equal, -8192.0, 0, 0, 128)
-    ga("DmA", T.DmA[:], T.zer[:], ["zer"], [[-16, 8], [-1, 18]], Alu.not_equal, -1.0, 1, 1, 144)
-    ga("DmB", T.DmB[:], T.DmA[:], ["DmA"], [[0, 8], [-1, 18]], Alu.is_gt, 0.0, 17, 0, 144)
-    ga("Dm", T.Dm[:], T.DmB[:], ["DmB"], [[-16, 8], [-1, 18]], Alu.not_equal, 1.0, 2, 1, 144)
-    gi("pi", T.pi[:], [[0, 64]], 0, 1, 64, False)
-    vts("pj", T.pj[:], T.pi[:], 15, None, Alu.bitwise_and, None, ["pi"], 64)
-    vcp("rcol", T.rcol[:], T.pj[:, 0:8], ["pj"], 8)
-    vts("bcv", T.bcv[:], T.c1[:], 18.0, 17.0, Alu.mult, Alu.add, ["c1"], 16)
-    vts("c2", T.c2[:], T.c1[:], 2.0, T.rcol[:, 0:1], Alu.mult, Alu.is_gt, ["c1", "rcol"], 16)
-    vtt("c2c", T.c2c[:], T.c1[:], T.c2[:], Alu.subtract, ["c1", "c2"], 16)
-    vts("bc18", T.bc18[:], T.c2c[:], 7.0, None, Alu.min, None, ["c2c"], 16)
-    sact("scol", T.scol[:], T.c1[:, 0:8], Act.Identity, ["c1", "rcol"], 8, scale=16.0, bias=T.rcol[:, 0:1])
-    sact("sb", T.sb[:], T.scol[:], Act.Identity, ["scol"], 8, scale=-float(2 ** 25), bias=float(2 ** 24))
-    gi("io129", T.io129[:], [[1, 144]], -1, 0, 144)
-    ga("rowp0", T.rowp[:], T.ones[:], ["ones"], [[1, 144]], Alu.is_equal, -4096.0, 0, 0, 144)
-    for b in range(8):
-        n = 16 * (b + 1) + 1
-        sact("RA%d" % b, T.RA[:, b * 129:b * 129 + n], T.rowp[:, 0:n], Act.Copy, ["rowp0", "G8f"], n, scale=T.G8f[:, b:b + 1])
-    for b in range(8):
-        n = 16 * (b + 1) + 1
-        tmp = T.BM[:, b * 112:b * 112 + n - 1] if b < 7 else T.CT[:]
-        sact("CT%d" % b, tmp, T.io129[:, 1:n], Act.Relu, ["io129", "sb"], n, wr=["BMt%d" % b], scale=float(2 ** 25), bias=T.sb[:, b:b + 1])
-        sact("CC%d" % b, T.CC[:, b * 129 + 1:b * 129 + n], tmp, Act.Identity, ["BMt%d" % b, "scol"], n, bias=T.scol[:, b:b + 1])
-    sact("CCx", T.CC[:, 0:1032:129], T.scol[:], Act.Identity, ["scol"], 8, scale=0.0, bias=128.0)
-    gi("io896", T.io896[:], [[1, 896]], F, 0, 896)
-    for m in range(7):
-        sact("BM%d" % m, blk(T.BM, m), blk(T.io896, m), Act.Copy, ["io896", "mR"], 128,
-             wr=["BM%d" % m] + ["BMt%d" % b for b in range(7)], scale=T.mR[:, m:m + 1])
-    sact("hvf", T.hvf[:], T.hvb[:], Act.Copy, ["hvb"], 16)
-    if any(u[0] == "R" for u in SUMV):
-        op("hrec", "v", lambda q: [q.reciprocal(T.hrec[:], T.hvf[:])], ["hvf"], ["hrec"], 300.0)
-        op("r160", "v", lambda q: [q.memset(T.RT[:, 0:1], 0.0)], [], ["r160"], cv(1))
-        vtt("RT", T.RT[:, 1:16], T.hvf[:, 0:15], T.hrec[:, 1:16], Alu.mult, ["hvf", "hrec"], 16)
+        ga("sel%d" % (3 + k), blk(T.sel34, k), T.zer[:], ["zer"], [[-16, 8], [0, 16]], Alu.not_equal, 1.0, -3 - k, 1, 128)
+    ga("QB", T.QB[:], T.QA[:], ["QA"], [[0, 2], [-32, 4], [0, 2]], Alu.is_ge, 0.0, 0, 1, 16)
+    ga("QA", T.QA[:], T.QB[:], ["QB"], [[0, 2], [32, 4], [0, 2]], Alu.is_ge, 0.0, 31, -1, 16)
+    ga("QE", T.QE[:], T.QA[:], ["QA"], [[1, 2], [0, 4], [-1, 2]], Alu.is_equal, 0.0, 0, 0, 16)
+    for k in range(3):
+        ga("rst%d" % k, blk(T.rst, k), T.zer[:], ["zer"], [[0, 8], [1, 16]], Alu.not_equal, BIG, 0, 0, 128)
+    ga("Dm", T.Dm[:], T.zer[:], ["zer"], [[-1, 128]], Alu.not_equal, -1.0, -1, 1, 128)
+    ga("DmA", T.DmA[:], T.Dm[:], ["Dm"], [[0, 8], [-1, 16]], Alu.is_gt, 0.0, 15, 0, 128)
+    ga("Dm", T.Dm[:], T.DmA[:], ["DmA"], [[-1, 128]], Alu.not_equal, 1.0, 0, 1, 128)
+    gi("U2", T.U2[:, 0:896], [[1, 896]], F, 0, 896)
+    dma("bz", "y", [(blk(T.BM, m), T.zer[:]) for m in range(7)], ["zer"], ["BM"], "bz")
+    dma("bm", "y", [(T.BM[m::16, m * 128:(m + 1) * 128], T.U2[m::16, m * 128:(m + 1) * 128]) for m in range(7)], ["U2"], ["BM"], "bm")
+    for l in range(2):
+        sact("lnc%d" % l, T.hl[:, 1 + l:2 + l], T.ones[:, 0:1], Act.Ln, ["ones"] + ["lnc0"] * l, 1, scale=1.0 / (16 << l), cost=None if l else 1400.0)
+    sact("lnh", T.lnh[:, 0:16], T.hvb[:], Act.Ln, ["hvb", "lnc1"], 16, scale=1.0 / 16)
+    if SCAN:
+        sact("hl", T.hl[:, 0:1], T.lnh[:, 15:16], Act.Exp, ["lnh"], 1, cost=1600.0)
+        op("hrec", "v", lambda q: [q.reciprocal(T.hrec[:], T.hvb[:])], ["hvb"], ["hrec"], 300.0)
+        vset("r160", T.RT[:, 0:1], 0.0, 1)
+        vtt("RT", T.RT[:, 1:16], T.hvb[:, 0:15], T.hrec[:, 1:16], Alu.mult, ["hvb", "hrec"], 16)
         for w in (16, 32, 64, 128, 256, 512):
-            op("RT%d" % w, "y", lambda q, w=w: [q.dma_start(T.RT[:, w:2 * w], T.RT[:, 0:w])], ["RT", "r160"], ["RT"], 60.0, kind="d", sem="rt")
-        op("Sel0", "g", lambda q: [q.iota(T.Sel[:], [[0, 512]], 0, 0, allow_small_or_imprecise_dtypes=True)], [], ["Sel"], 130 + 1024 * C["cyc"])
-        for k in range(4):
-            sl = T.Sel[32 * k:32 * k + 32, :]
-            op("Sel%d" % (k + 1), "g", lambda q, sl=sl: [q.affine_select(sl, sl, [[-1, 32], [0, 16]], Alu.not_equal, -1.0, 0, 1)],
-               ["Sel"], ["Sel"], 170 + 1024 * C["cyc"])
-    sact("lnh", T.lnh[:], T.hvf[:], Act.Ln, ["hvf"], 16, scale=1.0 / 16, cost=1600.0)
-
-    def column(name, out, c, lst, lk, top):
-        win = T.Ut[:, 128:128 + F + 128 * top].indirect(lst)
-        rd = ["U0", lk] + ["Uc%d" % k for k in range(top)]
-        if name in ("old5", "old6"):
-            win, rd = T.U2[:, 128:128 + F].indirect(lst), ["U2", lk]
-        if name in ONS:
-            sact(name, out, win, Act.Copy, rd, 0, cost=cg(128))
-        elif c is None:
-            vcp(name, out, win, rd, 0, cost=cg(128))
-        else:
-            vcp(name, out, blk(T.cu, c), ["cu%d" % c], 128)
-
-    vcp("stu", T.stu[:], T.sti[:], ["sti"], 24)
-    vcp("stf", T.stf[:], T.sti[:], ["sti"], 24)
-    for l in range(3):
-        vcp("cu%d" % (7 + l), blk(T.cu, 7 + l), T.sui[:].indirect(T.stu[:, 8 * l:8 * l + 8]), ["sui", "stu"], 128, cost=cg(128))
-    ga("U0", T.Ut[:, 128:128 + F], T.sui[:], ["sui"], [[0, F]], Alu.is_equal, 0.0, 0, 0, F)
-    for l in range(3):
-        column("cf%d" % l, blk(T.cf, l), 7 + l, T.stu[:, 8 * l:8 * l + 8], "stu", 0)
-    vts("X16", T.X16[:], T.xsi[:], -2048.0, None, Alu.add, None, ["xsi"], 512)
-    MX, MK = {}, {}
-    for l in range(3):
-        a = 7 + l
-        vtt("M1%d" % l, blk(T.M1, l), T.stf[:, 8 * l:8 * l + 8].indirect(T.bc8[:, 0:8]), T.mR[:], Alu.mult,
-            ["stf", "bc8", "mR"], 128, cost=cg(128))
-        op("Ap%d" % a, "p", lambda q, l=l, a=a: [q.matmul(ps("a%d" % a, 0, 128), blk(T.M1, l), ident(0), True, True),
-                                               q.matmul(ps("a%d" % a, 128, 256), blk(T.M1, l), T.BB[:], True, True)],
-           ["M1%d" % l, "I0", "BB"], ["Ap%d" % a], cp(256), acq=("a%d" % a, 1))
-        op("A12%d" % a, "v", lambda q, a=a: [q.tensor_copy(blk(T.A12, a, 256), ps("a%d" % a, 0, 256))],
-           ["Ap%d" % a], ["A1%d" % a, "A2%d" % a], cv(256), rel="a%d" % a)
+            dma("RT%d" % w, "y", [(T.RT[:, w:2 * w], T.RT[:, 0:w])], ["RT", "r160"], ["RT"], "rt")
+        vts("n32", T.n32[:], T.lf[:, 0:32], T.pf[:, 2:3], -1.0, Alu.is_equal, Alu.mult, ["lf0", "pf"], 32)
+        both("Sel", T.Sel[:], T.n32[:].indirect(T.lu[:, 0:32]), ["n32", "lu"], cg(512))
+    if any(k in SETS for k in RELU):
+        vts("lnr", T.lnh[:, 16:32], T.lnh[:, 0:16], -8.0, None, Alu.add, None, ["lnh"], 16)
 
     def pk(n):
         return ["P0"] + ["Pc%d" % k for k in range(n)]
@@ -248,295 +254,480 @@ def build(T, topo, core, C):
     def uk(n):
         return ["U0"] + ["Uc%d" % k for k in range(n)]
 
-    def chunks(u):
-        if u in ("R0", "R1") and u not in SUMV:
-            return [(0, 1024), (1024, 1536), (1536, 2048)]
-        w = 512 if u in FINE or u in SMALL else 1024
-        return [(a, a + w) for a in range(0, 2048, w)]
+    def uwin(t, top):
+        return t[:, SP:SP + F + 128 * top]
 
-    def slots(u):
-        late = [i for i in range(16) if (u, i) in LATE]
-        return [i for i in range(16) if i not in late] + late
+    def ublk(m):
+        return T.Ut[:, SP + F + 128 * m:SP + F + 128 * m + 128]
+
+    def cfb(l):
+        return T.cf[:, 144 * l:144 * l + 128]
+
+    def column(name, out, c, win, rd, wr=None):
+        if name in CONV:
+            vcp(name, out, blk(T.cu, c), ["cu%d" % c], 128, wr=wr)
+        else:
+            both(name, out, win, rd, cg(128), wr=wr)
+
+    vcp("stu", T.stu[:, 0:24], T.sti[:], ["sti"], 24)
+    for l in (1, 2):
+        vcp("stv%d" % l, T.stu[:, 14 + 10 * l:22 + 10 * l], T.sti[:, 8 * l:8 * l + 8], ["sti"], 8)
+        vcp("stw%d" % l, T.stu[:, 22 + 10 * l:23 + 10 * l], T.sti[:, 8 * l:8 * l + 1], ["sti"], 1)
+    vcp("cu7", blk(T.cu, 7), T.sui[:].indirect(T.stu[:, 0:8]), ["sui", "stu"], 128, cost=cg(128))
+    ga("U0", uwin(T.Ut, 0), T.sui[:], ["sui"], [[0, F]], Alu.is_equal, 0.0, 0, 0, F)
+    both("cf0", cfb(0), T.sui[:].indirect(T.stu[:, 0:8]), ["sui", "stu"], cg(128))
+    for l in (1, 2):
+        both("cf%d" % l, blk(T.cf, l, 144), T.sui[:].indirect(T.stu[:, 14 + 10 * l:23 + 10 * l]), ["sui", "stv%d" % l, "stw%d" % l], cg(144))
+    both("X16", T.X16[:], T.xsi[:], ["xsi"], cv(512), plus=-2048.0)
+    for z, m in enumerate((2, 5, 6)):
+        h = "Xm%d" % z
+        op(h, "p", lambda q, h=h, m=m: [q.matmul(ps(h, 0, 128), ident((0, 1, 4)[LEV[m]]), blk(T.X16, t), t == TIMES[m][0], t == TIMES[m][-1]) for t in TIMES[m]],
+           ["X16", "I1", "I4"], [h], cp(128 * len(TIMES[m]), len(TIMES[m])), acq=(h, 1))
+        both("Xe%d" % z, blk(T.XR, 4 * z), None, [h], cv(128), plus=2048.0, rel=h)
+        dma("XR%d" % z, "y", [(blk(T.XR, 4 * z + j), blk(T.XR, 4 * z)) for j in (1, 2, 3)], ["Xe%d" % z], ["XR%d" % z], "xr%d" % z)
+
+    def symbols(m):
+        return [blk(T.X16, t) for t in TIMES[m]], "X16"
+    for l in range(3):
+        a = 7 + l
+        vtt("M1%d" % l, blk(T.M1, l), T.sti[:, 8 * l:8 * l + 8].indirect(T.lu[:, 0:8]), T.mR[:], Alu.mult, ["sti", "lu", "mR"], 128, cost=cg(128))
+        op("Ap%d" % a, "p", lambda q, l=l, a=a: [q.matmul(ps("a%d" % a, 0, 128), blk(T.M1, l), ident(0), True, True)],
+           ["M1%d" % l, "I0"], ["Ap%d" % a], cp(128, 1), acq=("a%d" % a, 1))
+        both("A1%d" % a, blk(T.A1, a), None, ["Ap%d" % a], cv(128), rel="a%d" % a)
 
     def gkeys(k, a=0, b=2048):
         return ["G%d_%d" % (k, x) for x in range(a // 512, b // 512)]
 
-    def akeys(k, a=0, b=2048):
-        return ["AE%d_%d" % (k, x) for x in range(a // 512, b // 512)]
+    def akeys(u, a=0, b=16):
+        return ["A%s_%d" % (u, x) for x in range(a, b)]
+
+    def slab(u, a, b=None):
+        k, j = setof[u]
+        if k in APART:
+            return T["A" + k][:, j, 128 * a:128 * (b or a + 1)]
+        return T["A" + k][:, a, j, :] if b is None else T["A" + k][:, a:b, j, :]
+
+    def slot(k, i):
+        return T["A" + k][:, :, 128 * i:128 * i + 128] if k in APART else T["A" + k][:, i, :, :]
+
+    def slots(u):
+        return ORDER01 if u in ("R0", "R1") else list(range(16))
+
+    def turned(c, cf, cfk):
+        z = c % 2
+        for e in range(2):
+            op("tt%d_%d" % (c, e), "v", lambda q, e=e: [q.transpose(blk(T.TT, 2 * z + e), cf[:, 16 * e:16 * e + 128])], [cfk], ["TT%d_%d" % (z, e)], cv(128))
+        vcp("cu%d" % c, blk(T.cu, c), blk(T.TT, z, 256).indirect(T.lt[:]), ["TT%d_0" % z, "TT%d_1" % z, "lt"], 0, cost=cg(128))
+
+    def direct(u, cand, ck, top, z):
+        for a in range(0, 16, 4):
+            vtt("g%s_%d" % (u, a), slab(u, a, a + 4), T.Pt[:, 0:F + 128 * top].indirect(cand[:, 8 * a:8 * a + 32]), blk(T.XR, z, 512), Alu.subtract,
+                pk(top) + [ck, "XR%d" % z], 0, wr=akeys(u, a, a + 4), cost=cg(512) + 512 * C["tti"] * C["cyc"])
+        part[0] = u
+        for a in (0, 8):
+            sact("abs%s_%d" % (u, a), slab(u, a, a + 8), slab(u, a, a + 8), Act.Abs, akeys(u, a, a + 8), 1024, wr=akeys(u, a, a + 8))
 
     def gather(u, cand, ck, top):
         G = T["G%d" % GOF[u]]
-        for a, b in ([(0, 1024), (1024, 2048)] if u not in SMALL else chunks(u)):
-            vts("g%s_%d" % (u, a), G[:, a:b], T.Pt[:, 0:F + 128 * top].indirect(cand[:, a // 16:b // 16]), -2048.0, None,
-                Alu.add, None, pk(top) + [ck], 0, wr=gkeys(GOF[u], a, b), cost=cg(b - a))
+        w = 512 if u in QUART else 1024
+        for a in range(0, 2048, w):
+            both("g%s_%d" % (u, a), G[:, a:a + w], T.Pt[:, 0:F + 128 * top].indirect(cand[:, a // 16:(a + w) // 16]), pk(top) + [ck],
+                 cg(w), plus=-2048.0, wr=gkeys(GOF[u], a, a + w))
 
     def dist(u, lev, xts, xk):
         G = T["G%d" % GOF[u]]
-        A = T["AE%d" % AEOF[u]]
-        for a, b in chunks(u):
+        w = 4 if u in FINE else 8
+        a0 = 0 if u in SCAN else RELU.get(setof[u][0], 0)
+        end = 14 if u in ("R0", "R1") else 16
+        for a, b in [(a, min(a + w, end)) for a in range(a0, end, w)]:
             h = "d%s_%d" % (u, a)
+            n = 128 * (b - a)
 
-            def mm(q, a=a, b=b, h=h):
+            def mm(q, c0, c1, a=a, b=b, h=h):
                 r = []
-                if u in SUMV:
-                    for c in range(a, b, 512):
-                        o = ps(h, c - a, c - a + 512)
-                        r.append(q.matmul(o, ident(lev), G[:, c:c + 512], True, False))
-                        p0 = c // 16
-                        x = xts[0]
-                        r.append(q.matmul(o, x[0][p0:p0 + 32, x[1]:x[1] + 128], T.Sel[p0:p0 + 32, :], False, True))
+                if u in SCAN:
+                    for c in range(c0, c1, 4):
+                        o = ps(h, 128 * (c - a), 128 * (c - a) + 512)
+                        r.append(q.matmul(o, ident(lev), G[:, 128 * c:128 * c + 512], True, False))
+                        r.append(q.matmul(o, xts[0][8 * c:8 * c + 32, :], T.Sel[8 * c:8 * c + 32, :], False, a >= RELU.get(u, 0)))
                     return r
-                for c in range(a, b, 128):
-                    o = ps(h, c - a, c - a + 128)
-                    i = slots(u)[c // 128]
-                    if u not in FINE:
+                for c in range(c0, c1):
+                    o = ps(h, 128 * (c - a), 128 * (c - a) + 128)
+                    if u not in EARLY:
                         for j, x in enumerate(xts):
-                            r.append(q.matmul(o, ident(7), x[0][:, x[1]:x[1] + 128], j == 0, False))
-                    r.append(q.matmul(o, ident(lev), blk(T.GX, LATE[u, i]) if (u, i) in LATE else G[:, i::16], False,
-                                      u not in FINE or c + 128 == b))
+                            r.append(q.matmul(o, ident(7), x, j == 0, False))
+                    r.append(q.matmul(o, ident(lev), G[:, slots(u)[c]::16], False, u not in EARLY or c + 1 == b))
                 return r
-            late = ["fx%d" % LATE[u, i] for i in slots(u)[a // 128:b // 128] if (u, i) in LATE]
-            if u in FINE:
-                x = xts[0]
-                op(h + "x", "p", lambda q, h=h, x=x: [q.matmul(ps(h, c, c + 128), ident(7), x[0][:, x[1]:x[1] + 128], c == 0, False)
-                                                     for c in range(0, 512, 128)],
-                   gkeys(GOF[u], 0, 512) + ["I7", xk], [h], cp(512), acq=(h, 1))
-                op(h, "p", mm, gkeys(GOF[u]) + [h, "I%d" % lev], [h], cp(512))
+            if u in EARLY:
+                op(h + "x", "p", lambda q, h=h: [q.matmul(ps(h, c, c + 128), ident(7), xts[0], c == 0, False) for c in range(0, 512, 128)],
+                   [xk, "I7"], [h], cp(512, 4), acq=(h, 1))
+                op(h, "p", lambda q, a=a, b=b, mm=mm: mm(q, a, b), gkeys(GOF[u]) + [h, "I%d" % lev], [h], cp(512, 4))
+            elif u in SCAN:
+                for c in range(a, b, 4):
+                    op("%s_%d" % (h, c), "p", lambda q, c=c, mm=mm: mm(q, c, c + 4), gkeys(GOF[u], 128 * a, 128 * b) + ["Sel", xk, "I%d" % lev],
+                       [h], cp(1024, 2), acq=(h, w // 4) if c == a else None)
             else:
-                op(h, "p", mm, (gkeys(GOF[u], a, b) + ["Sel"] if u in SUMV else gkeys(GOF[u]) + ["I7"]) + [xk, "I%d" % lev] + late, [h],
-                   cp((b - a) * (1 + len(xts))), acq=(h, (b - a) // 512))
-            op("abs" + h, "s", lambda q, a=a, b=b, h=h: [q.activation(A[:, a:b], ps(h, 0, b - a), Act.Abs)], [h],
-               akeys(AEOF[u], a, b), cv(b - a), rel=h)
+                z = 4 if len(xts) == 1 else 2
+                for c in range(a, b, z):
+                    e = min(c + z, b)
+                    op("%s_%d" % (h, c), "p", lambda q, c=c, e=e, mm=mm: mm(q, c, e), gkeys(GOF[u]) + ["I7", xk, "I%d" % lev], [h],
+                       cp(128 * (e - c) * (1 + len(xts)), (e - c) * (1 + len(xts))), acq=(h, (b - a + 3) // 4) if c == a else None)
+            out = T["A" + u][:, 128 * a:128 * b] if u in SCAN else slab(u, a, b)
+            if u in SCAN and a < RELU.get(u, 0):
+                positive(h)
+                op("exp" + h, "s", lambda q, out=out, h=h: [q.activation(out, ps(h, 0, 1024), Act.Exp, scale=1.0 / 512, bias=-8.0)], [h, "hl"],
+                   akeys(u, a, b), cv(n), rel=h)
+            else:
+                op("abs" + h, "s", lambda q, out=out, n=n, h=h: [q.activation(out, ps(h, 0, n), Act.Abs)], [h], akeys(u, a, b), cv(n), rel=h)
 
-    def mix(u, lev, m):
-        k = AEOF[u]
-        A = T["AE%d" % k]
-        ro = u[0] == "R"
-        bias = -math.log(32.0 if lev else 16.0)
-        if ro and u not in SUMV:
-            for a in range(0, 2048, 512):
-                op("exp%s_%d" % (u, a), "s", lambda q, a=a: [q.activation(blk(A, i), blk(A, i), Act.Exp, scale=-1.0 / 512, bias=T.lnh[:, slots(u)[i]:slots(u)[i] + 1])
-                                                              for i in range(a // 128, a // 128 + 4)],
-                   akeys(k, a, a + 512) + ["lnh"], akeys(k, a, a + 512), 4 * cv(128))
+    turn = [0]
+
+    def positive(h):
+        z = turn[0] % 2
+        turn[0] += 1
+        r = blk(T.pos, z, 1024)
+        op("pos" + h, "v", lambda q: [q.tensor_scalar(r, ps(h, 0, 1024), 0.0, -2048.0, Alu.max, Alu.add)], [h], ["pos%d" % z], cv(1024))
+        op(h + "r", "p", lambda q: [q.matmul(ps(h, c, c + 512), ident(2), r[:, c:c + 512], False, True) for c in (0, 512)],
+           ["pos%d" % z, "I2", h], [h, h + "r"], cp(1024, 2))
+
+    def joint(k, xs):
+        A, us = T["A" + k], SETS[k]
+        for a in range(0, RELU.get(k, 0), 4):
+            h = "j%s_%d" % (k, a)
+            for c in (a, a + 2):
+                def mm(q, c=c, a=a, h=h):
+                    r = []
+                    for i in (c, c + 1):
+                        for j, u in enumerate(us):
+                            o = ps(h, 256 * (i - a) + 128 * j, 256 * (i - a) + 128 * j + 128)
+                            r.append(q.matmul(o, ident(7), xs[u][0], i == c and j == 0, False))
+                            r.append(q.matmul(o, ident(0), T["G%d" % GOF[u]][:, slots(u)[i]::16], False, False))
+                    return r
+                op("%s_%d" % (h, c), "p", mm, [x for u in us for x in gkeys(GOF[u]) + [xs[u][1]]] + ["I0", "I7"], [h], cp(1024, 8),
+                   acq=(h, 2) if c == a else None)
+            positive(h)
+            op("exp" + h, "s", lambda q, a=a, h=h: [q.activation(A[:, i, :, :], ps(h, 256 * (i - a), 256 * (i - a) + 256), Act.Exp, scale=1.0 / 512,
+                                                                 bias=T.lnh[:, 16 + slots(us[0])[i]:17 + slots(us[0])[i]]) for i in range(a, a + 4)],
+               [h, "lnr"] + WARM, [x for u in us for x in akeys(u, a, a + 4)], 4 * cv(256), rel=h)
+
+    MX, MK = {}, {}
+
+    def store(name, dst, src, rd, k):
+        dma("st" + name, "y", [(dst, src)], rd, [], "t%d" % k)
+
+    def expo(u, lev):
+        for a in range(RELU.get(u, 0), 16, 8):
+            o = T["A" + u][:, 128 * a:128 * a + 1024] if u in SCAN else slab(u, a, a + 8)
+            sact("exp%s_%d" % (u, a), o, o, Act.Exp, akeys(u, a, a + 8) + WARM, 1024, wr=akeys(u, a, a + 8), scale=-1.0 / 512,
+                 bias=0.0 if u in SCAN else T.hl[:, 2:3] if lev else T.hl[:, 1:2])
+
+    def weigh(k, a, b):
+        A, us = T["A" + k], SETS[k]
+        keys = [x for u in us for x in akeys(u, a, b)]
+        op("exp%s_%d" % (k, a), "s", lambda q: [q.activation(slot(k, i), slot(k, i), Act.Exp, scale=-1.0 / 512,
+                                                             bias=T.lnh[:, slots(us[0])[i]:slots(us[0])[i] + 1]) for i in range(a, b)],
+           keys + ["lnh"] + WARM, keys, (b - a) * cv(128 * len(us)))
+
+    def total(k, steps):
+        A, us = T["A" + k], SETS[k]
+        if k not in FOLD:
+            for j, (to, fr, n) in enumerate(steps):
+                add("add%s_%d" % (k, j), A[:, to:to + n, :, :], A[:, fr:fr + n, :, :], [x for u in us for x in akeys(u, fr, fr + n)],
+                    [x for u in us for x in akeys(u, to, to + n)] + ["sem" + k], "a" + k, n * len(us) * 65536)
+            return
+        hs = helpers(T, topo, core)
+        j = FOLD.index(k) % len(hs)
+        n, z = PART.get(k, 16), WIDE.get(k, 1)
+        keys = [x for u in us for x in akeys(u, 0, n)]
+
+        def fold(q):
+            rid, pid = topo.addr(hs[j], core)
+            e = topo.engines(core, hs[j])
+            prs = ([([slab(u, i, i + z) for i in range(0, n, z)], blk(result(T, k), x, 128 * z)) for x, u in enumerate(us)] if k in APART else
+                   [([slot(k, i) for i in range(n)], result(T, k))])
+            w = len(e) // len(prs)
+            q.remote_dma_fused([RemoteDMATransfer(dst_ids=[DstId(rid=rid, pnc=pid)], dma_engine_mask=sum(1 << y for y in e[x * w:(x + 1) * w]),
+                                                  remote_sem=T.sem["f" + k], srcs=a, dsts=[b], alu_op=1) for x, (a, b) in enumerate(prs)],
+                               local_sem=T.sem.sent)
+            return len(e)
+        op("fold" + k, "g", fold, keys, ["fold" + k, "help%d" % j], C["call"], kind="r", lat=C["dma"] / 2)
+        op("fold" + k + "d", "D", len(ops) - 1, keys + ["fold" + k], ["fold" + k, "help%d" % j],
+           8 * n // z * (len(us) if k in APART else 1) * C["row"] + n * len(us) * 65536 / C["fw"], kind="e", lat=C["dma"] / 2)
+        op("back" + k, "h%d" % j, len(topo.engines(hs[j], core)), ["fold" + k], ["res" + k], C["back"] + 110.0 * z * len(us), kind="w", sem="b" + k)
+
+    def summed(u):
+        k, j = setof[u]
+        if k in FOLD:
+            z = WIDE.get(k, 1)
+            return [blk(result(T, k), z * j + i) for i in range(z)], ["res" + k]
+        left = max(1, 16 >> HALVE[k])
+        return [slab(u, i) for i in range(left)], akeys(u, 0, left)
+
+    def rest(k, m, w):
+        h, n = "sum" + k, PART[k]
+        z = 512 // w
+        for a in range(n, 16, z):
+            op("%s_%d" % (h, a), "p", lambda q, a=a: [q.matmul(ps(h, 0, w), T.idf[:], slot(k, i), i == n, i == 15 and not n)
+                                                      for i in range(a, a + z)],
+               [x for u in SETS[k] for x in akeys(u, a, a + z)] + ["idf"], [h], cp(2048, z), acq=(h, 1) if a == n else None)
+        if n:
+            xs = [(128 * j, x) for j, u in enumerate(SETS[k]) for x in summed(u)[0]]
+            op(h + "f", "p", lambda q: [q.matmul(ps(h, a, a + 128), T.idf[:], x, False, j + 1 == len(xs)) for j, (a, x) in enumerate(xs)],
+               ["res" + k, "idf"], [h], cp(512 * len(xs), len(xs)))
+        out = result(T, k)[:, 0:w]
+        both("yz%d" % m, out, w, [h], cv(w), rel=h, wr=["res" + k])
+        store("yz%d" % m, T.yz[:, 128 * m:128 * m + w], out, ["res" + k], 7 + m)
+
+    def mixture(m):
+        u = "E%d" % m
+        lev = LEV[m]
+        xs, keys = summed(u)
+        if len(xs) == 1 and not lev:
+            MX[m], MK[m] = xs[0], keys
         else:
-            for a in (0, 1024):
-                sact("exp%s_%d" % (u, a), A[:, a:a + 1024], A[:, a:a + 1024], Act.Exp, akeys(k, a, a + 1024) + ["lnh"], 1024,
-                     wr=akeys(k, a, a + 1024), scale=-1.0 / (512 << lev), bias=bias)
-        out = blk(T.yzb if ro else T.ymb, m)
-        nm = ("yz%d" if ro else "ym%d") % m
-        if u in SUMV:
-            sc = T["AE%d" % SCOF[u]]
-            for a in (0, 1024):
-                op("scan%s_%d" % (u, a), "v", lambda q, a=a: [q.tensor_tensor_scan(sc[:, a:a + 1024], T.RT[:], A[:, a:a + 1024], 0.0, Alu.mult, Alu.add)],
-                   akeys(k, a, a + 1024) + ["RT"], akeys(SCOF[u], a, a + 1024), cv(1024))
-            if nm in ONV:
-                vts(nm, out, sc[:, 15::16], T.hvf[:, 15:16], None, Alu.mult, None, akeys(SCOF[u]) + ["hvf"], 128)
-            else:
-                sact(nm, out, sc[:, 15::16], Act.Copy, akeys(SCOF[u]) + ["hvf"], 128, scale=T.hvf[:, 15:16])
-        else:
+            MX[m], MK[m] = xs[0], list(keys)
             h = "sum" + u
-            tail = [12, 13, 14, 15] if u in ("R0", "R1") else []
-            top = 2048 - 128 * len(tail)
-            for j in range(HALVE.get(u, 0)):
-                w = top // 256 * 128
-                op("add%s_%d" % (u, j), "g", lambda q, w=w, top=top: [q.dma_start(A[:, 0:w], A[:, top - w:top], accum_op=Alu.add)],
-                   akeys(k, 0, top + 511), akeys(k, 0, w + 511), C["gdma"], kind="a", sem="a" + u)
-                ops[-1]["lat"] = C["dma"] + w * 512 / C["bw"]
-                top -= w
-            slabs = list(range(top // 128)) + tail
-            pr = None
+            prs = [(T.idf[:], x) for x in xs]
             if lev:
                 x, y = {2: (0, 1), 5: (3, 4), 6: (2, 5)}[m]
                 pr = blk(T.prod, {2: 0, 5: 1, 6: 2}[m])
                 vtt("prod%d" % m, pr, MX[x], MX[y], Alu.mult, MK[x] + MK[y], 128)
-            if len(slabs) == 1 and not lev:
-                out = A[:, 0:128]
-                [o for o in ops if o["name"] == "add%s_3" % u][0]["wr"].append(nm)
-            else:
-                for j in sorted(set(i // 4 for i in slabs)):
-                    some = [i for i in slabs if i // 4 == j]
+                prs.append((T.idh[:], pr))
+                keys = keys + ["prod%d" % m, "idh"]
+            op(h, "p", lambda q: [q.matmul(ps(h, 0, 128), a, b, i == 0, i == len(prs) - 1) for i, (a, b) in enumerate(prs)],
+               keys + ["idf"], [h], cp(len(prs) * 512, len(prs)), acq=(h, 1))
+            both("ym%d" % m, MX[m], None, [h], cv(128), rel=h, wr=MK[m])
+        store("ym%d" % m, blk(T.ym, m), MX[m], MK[m], m)
 
-                    def mm(q, some=some):
-                        return [q.matmul(ps(h, 0, 128), T.idf[:], blk(A, i), i == 0, i == slabs[-1] and not lev) for i in some]
-                    op("%s_%d" % (h, j), "p", mm, akeys(k, 512 * j, 512 * j + 512) + ["idf"] + ([h] if j else []), [h],
-                       cp(len(some) * 512), acq=(h, 1) if j == 0 else None)
-                if lev:
-                    op(h + "x", "p", lambda q: [q.matmul(ps(h, 0, 128), T.idh[:], pr, False, True)], [h, "idh", "prod%d" % m], [h], cp(512))
-                if nm in ONV:
-                    op(nm, "v", lambda q: [q.tensor_copy(out, ps(h, 0, 128))], [h], [nm], cv(128), rel=h)
-                else:
-                    op(nm, "s", lambda q: [q.activation(out, ps(h, 0, 128), Act.Copy)], [h], [nm], cv(128), rel=h)
-        keys = [nm] + (akeys(k, 0, 512) if u not in SUMV and HALVE.get(u, 0) == 4 and not lev and u not in ("R0", "R1") else [])
-        if not ro:
-            MX[m] = out
-            MK[m] = keys
-        dst = (T.yz if ro else T.ym)[:, m * 128:(m + 1) * 128]
-        op("st" + nm, "y", lambda q: [q.dma_start(dst, out)], keys, [], 60.0, kind="d", sem="t" + u)
+    def scan(u, m):
+        out = blk(T.yzb, m - 4)
+        for a in (0, 8):
+            sc = blk(T.SC, a // 8, 1024)
+            op("scan%s_%d" % (u, a), "v", lambda q, a=a, sc=sc: [q.tensor_tensor_scan(sc, T.RT[:], T["A" + u][:, 128 * a:128 * a + 1024], 0.0, Alu.mult, Alu.add)],
+               akeys(u, a, a + 8) + ["RT"], ["SC%d" % a], cv(1024))
+        op("yz%d" % m, "vs", lambda q, e: [q.tensor_scalar(out, T.SC[:, 15::16], T.hl[:, 0:1], None, Alu.mult) if e == "v" else
+                                           q.activation(out, T.SC[:, 15::16], Act.Copy, scale=T.hl[:, 0:1])], ["SC0", "SC8", "hl"], ["yz%d" % m], cv(128))
+        store("yz%d" % m, blk(T.yz, m), out, ["yz%d" % m], 7 + m)
 
     def elect(m, cf, cfk):
         u = "E%d" % m
-        k = AEOF[u]
-        A = T["AE%d" % k]
         h = "k%d" % m
+        op(h + "n", "p", lambda q: [q.matmul(ps(h, 128, 256), cf, T.Dm[:], True, True),
+                                    q.matmul(ps(h, 0, 128), T.one16[0:1, :], T.kio[0:1, 0:128], True, False)],
+           [cfk, "Dm", "one16", "kio"], [h], cp(640, 2), acq=(h, 1))
         for j in range(4):
-            def mm(q, j=j):
-                r = []
-                if j == 0:
-                    r.append(q.matmul(ps(h, 144, 288), cf, T.Dm[:], True, True))
-                    r.append(q.matmul(ps(h, 0, 144), T.one16[0:1, :], T.keyc[0:1, :], True, False))
-                for i in range(4 * j, 4 * j + 4):
-                    r.append(q.matmul(ps(h, 2 + i, 144, 18), blk(A, i), T.BO[:], False, i == 15))
-                return r
-            op("%s_%d" % (h, j), "p", mm, akeys(k, 512 * j, 512 * j + 512) + [cfk, "Dm", "one16", "keyc", "BO"] + ([h] if j else []), [h],
-               cp(4 * 256 + (720 if j == 0 else 0)), acq=(h, 1) if j == 0 else None)
-        rm, stp, val = blk(T.rm, m, 144), blk(T.stp, m, 144), blk(T.val, m, 144)
-        op("rm%d" % m, "v", lambda q: [q.tensor_tensor_scan(rm, T.rst[:], ps(h, 0, 144), 0.0, Alu.add, Alu.min)],
-           [h, "rst"], ["rm%d" % m], cv(144))
-        vcp("mins%d" % m, blk(T.mins, m, 8), T.rm[:, m * 144 + 17:(m + 1) * 144:18], ["rm%d" % m], 8)
-        vtt("stp%d" % m, stp, blk(T.mins, m, 8).indirect(T.bc18[:, 0:9]), rm, Alu.is_equal, ["rm%d" % m, "mins%d" % m, "bc18"], 0, cost=cg(144))
-        op("val%d" % m, "v", lambda q: [q.tensor_tensor_scan(val, ps(h, 144, 288), stp, 0.0, Alu.add, Alu.mult)],
-           [h, "stp%d" % m], ["val%d" % m], cv(144))
-        a1 = T.A12[:, m * 256:m * 256 + 128]
-        vtt("A1%d" % m, a1, val.indirect(T.bcv[:, 0:8]), T.mR[:], Alu.mult, ["val%d" % m, "bcv", "mR"], 0, cost=cg(128))
-        op("L%d" % m, "p", lambda q: [q.matmul(ps(h, 288, 296), a1, T.G8[:], True, True)], ["A1%d" % m, "G8", "rm%d" % m], ["L%d" % m], cp(64))
-        op("bl%d" % m, "v", lambda q: [q.tensor_copy(blk(T.bl, m, 8), ps(h, 288, 296))], ["L%d" % m], ["bl%d" % m], cv(8), rel=h)
-        if m in (0, 1, 2, 3):
-            vcp("A2%d" % m, T.A12[:, m * 256 + 128:m * 256 + 256], val.indirect(T.bcv[:, 0:8]), ["val%d" % m, "bcv"], 0, cost=cg(128))
-
-    SEG = []
-    o = 0
-    for b in range(8):
-        if b == 6:
-            o = 512
-        SEG.append((o, 16 * (b + 1) + 1))
-        o += 16 * (b + 1) + 1
+            op("%s_%d" % (h, j), "p", lambda q, j=j: [q.matmul(ps(h, i, 128, 16), slab(u, i), blk(T.BO, LEV[m], 8), False, i == 15) for i in range(4 * j, 4 * j + 4)],
+               akeys(u, 4 * j, 4 * j + 4) + ["BO%d" % LEV[m], h], [h], cp(4 * 256, 4))
+        z = ROT[m]
+        rm, kp, val = blk(T.rm, z), blk(T.kp, z), blk(T.val, z)
+        rk, kk, vk = "rm_%d" % z, "kp_%d" % z, "val_%d" % z
+        op("rm%d" % m, "v", lambda q: [q.tensor_tensor_scan(rm, blk(T.rst, 0), ps(h, 0, 128), 0.0, Alu.add, Alu.min)], [h, "rst0"], [rk], cv(128))
+        op("kp%d" % m, "v", lambda q: [q.tensor_tensor(kp, ps(h, 0, 128), rm, Alu.is_gt)], [h, rk], [kk], cv(128))
+        op("val%d" % m, "v", lambda q: [q.tensor_tensor_scan(val, kp, ps(h, 128, 256), 0.0, Alu.mult, Alu.add)], [h, kk], [vk], cv(128))
+        a1 = blk(T.A1, m)
+        vtt("A1%d" % m, a1, val.indirect(T.lu[:, 32:40]), T.mR[:], Alu.mult, [vk, "lu", "mR"], 0, cost=cg(128))
+        op("L%d" % m, "p", lambda q: [q.matmul(ps(h, 256, 264), a1, T.G8[:], True, True)] +
+           ([q.matmul(ps(h, 264, 265), a1, T.G8[:, 0:1], True, True)] if m == 2 else []), ["A1%d" % m, "G8"], ["L%d" % m], cp(64, 1))
+        n = 9 if m == 2 else 8
+        op("bl%d" % m, "v", lambda q: [q.tensor_copy(T.bl[:, 10 * m:10 * m + n], ps(h, 256, 256 + n))], ["L%d" % m], ["bl%d" % m], cv(8), rel=h)
+        if m < 4:
+            both("A2%d" % m, blk(T.A2, m), val.indirect(T.lu[:, 32:40]), [vk, "lu"], cg(128))
 
     def extend(m, a, lst, lk, top, old, oldk):
         h = "x%d" % m
-        a1, a2 = T.A12[:, a * 256:a * 256 + 128], T.A12[:, a * 256 + 128:a * 256 + 256]
+        a1 = blk(T.A1, a)
+        own = (blk(T.M1, a - 7), T.nBB[:], ["M1%d" % (a - 7), "nBB"]) if a >= 7 else (ident(7), blk(T.A2, a), ["I7", "A2%d" % a])
+        z = (0, 1, 2, 0, 1, 2, 0)[m]
+        eq, ek = blk(T.eq, z, 256), "eq_%d" % z
 
         def mm(q):
             r = []
-            for b, (o, n) in enumerate(SEG):
-                r.append(q.matmul(ps(h, o, o + n), a1, T.RA[:, b * 129:b * 129 + n], True, False))
-                r.append(q.matmul(ps(h, o, o + n), a2, T.RB[:, 0:n], False, False))
-                r.append(q.matmul(ps(h, o, o + n), ident(0), T.CC[:, b * 129:b * 129 + n], False, True))
+            for e in range(2):
+                r.append(q.matmul(ps(h, 128 * e, 128 * e + 128), own[0], own[1], True, False))
+                r.append(q.matmul(ps(h, 128 * e, 128 * e + 128), blk(T.BN, e), a1, False, True))
             return r
-        op(h, "p", mm, ["A1%d" % a, "A2%d" % a, "RB", "RB0", "CCx", "I0"] + ["RA%d" % b for b in range(8)] + ["CC%d" % b for b in range(8)],
-           [h], cp(3 * 700), acq=(h, 2))
-        op("off%d" % m, "v", lambda q: [q.tensor_reduce(T.offf[:, m * 8 + b:m * 8 + b + 1], ps(h, o, o + n), Ax.X, Alu.min, apply_absolute_value=True)
-                                        for b, (o, n) in enumerate(SEG)], [h], ["off%d" % m], sum(cv(n) for o, n in SEG), rel=h)
-        vcp("offu%d" % m, blk(T.offu, m, 8), blk(T.offf, m, 8), ["off%d" % m], 8)
+        op(h, "p", mm, ["A1%d" % a, "BN0", "BN1"] + own[2], [h], cp(512, 4), acq=(h, 1))
+        op("eq%d" % m, "v", lambda q: [q.tensor_tensor(eq, ps(h, 0, 256), T.TM[:], Alu.is_equal)], [h, "TM"], [ek], cv(256))
+        op(h + "c", "p", lambda q: [q.matmul(ps(h, 256, 264), a1, T.G8[:], True, False)] +
+           [q.matmul(ps(h, 256, 264), blk(eq, e), blk(T.QE, e, 8), False, e == 1) for e in range(2)], [ek, "QE", "G8", "A1%d" % a], [h + "c"], cp(192, 3))
+        op("off%d" % m, "v", lambda q: [q.tensor_scalar(T.offu[:, 8 * m + e:8 * m + 8:2], ps(h, 256 + e, 264, 2), float(SP), T.pf[:, 4 * e:4 * e + 1], Alu.add, Alu.max)
+                                        for e in range(2)], [h + "c", "pf", "pf4"], ["off%d" % m], 2 * cv(4), rel=h)
+        U, keys = (T.Ut, uk(top)) if m < 5 else (T.U2, ["U2"])
         if old is None:
-            old, oldk = blk(T.old, m), "old%d" % m
-            column(oldk, old, None, lst, lk, top)
-        vtt("ext%d" % m, (T.Ut if m < 5 else T.U2)[:, 0:128 + F + 128 * top].indirect(blk(T.offu, m, 8)), old, blk(T.BM, m), Alu.max,
-            ["offu%d" % m, oldk, "BM%d" % m], 0, wr=uk(top) + ["spare"] if m < 5 else ["U2"], cost=C["fix"] + 128 * C["sca"] * C["cyc"])
+            old, oldk = blk(T.old, {2: 0, 3: 1, 5: 2, 6: 3}[m]), "old%d" % m
+            column(oldk, old, None, uwin(U, top).indirect(lst), keys + [lk])
+        for k in (3, 2, 1, 0):
+            vtt("ext%d_%d" % (m, k), U[:, 0:SP + F + 128 * top].indirect(T.offu[:, 8 * m + 2 * k:8 * m + 2 * k + 2]), blk(old, k, 32),
+                T.BM[:, 128 * m + 32 * k:128 * m + 32 * k + 32], Alu.max, ["off%d" % m, oldk, "BM"], 0, wr=keys + ["spare"],
+                cost=C["fix"] + 32 * C["sca"] * C["cyc"])
         if m == 4:
-            op("U2", "y", lambda q: [q.dma_start(T.U2[:, 128:512 + F], T.Ut[:, 128:512 + F])], uk(3), ["U2"], 60.0, kind="a", sem="cpu")
-            ops[-1]["lat"] = C["dma"] + 1000.0
+            dma("U4", "y", [(uwin(T.U2, 3), uwin(T.Ut, 3))], uk(3), ["U2"], "cpu", 640000)
+        if m == 1:
+            dma("U1", "y", [(uwin(T.U2, 1), uwin(T.Ut, 1))], uk(1), ["U2"], "cpv", 510000)
 
     def snap(m):
         lev, top = LEV[m], TOP[m]
         h = "s%d" % m
-        bl, pb = blk(T.bl, m, 8), blk(T.Pb, m)
+        bl, pb = T.bl[:, 10 * m:10 * m + 8], blk(T.Pb, m)
         rem = {2: 0, 5: 1, 6: 2}.get(m)
-        vts("Pb%d" % m, pb, T.Pt[:, 0:F + 128 * top].indirect(bl), -2048.0, None, Alu.add, None, pk(top) + ["bl%d" % m], 0, cost=cg(128))
+        both("Pb%d" % m, pb, T.Pt[:, 0:F + 128 * top].indirect(bl), pk(top) + ["bl%d" % m], cg(128), plus=-2048.0)
+        xts, xk = symbols(m)
 
         def mm(q, tr):
             o = ps(h, 128 * tr, 128 * tr + 128)
-            prs = [(T.one16[0:1, :], T.cm16[0:1, :])] + [(ident(4 + lev), blk(T.X16, t)) for t in TIMES[m]] + [(ident(3), pb)]
+            prs = [(T.one16[0:1, :], T.cm16[0:1, :])] + [(ident(4 + lev), x) for x in xts] + [(ident(3), pb)]
             return [q.matmul(o, p[tr], p[1 - tr], j == 0, j == len(prs) - 1) for j, p in enumerate(prs)]
-        tr = 1 if "R%d" % m in SUMV else 0
-        op(h, "p", lambda q: mm(q, 0) + (mm(q, 1) if tr else []), ["Pb%d" % m, "X16", "one16", "cm16", "I3", "I%d" % (4 + lev)], [h],
-           cp(128 * (1 + tr) * (2 + len(TIMES[m]))), acq=(h, 1))
+        tr = 1 if "R%d" % m in SCAN else 0
+        n = (1 + tr) * (2 + len(xts))
+        op(h, "p", lambda q: mm(q, 0) + (mm(q, 1) if tr else []), ["Pb%d" % m, xk, "one16", "cm16", "I3", "I%d" % (4 + lev)], [h],
+           cp(128 * n, n), acq=(h, 1))
         new = T.Pt[:, F + 128 * m:F + 128 * m + 128] if rem is None else blk(T.snew, rem)
-        op("new%d" % m, "v", lambda q: [q.tensor_scalar(new, ps(h, 0, 128), MAG, 2048.0 - MAG, Alu.add, Alu.add)], [h],
-           ["Pc%d" % m if rem is None else "snew%d" % m], cv(128), rel=h)
-        op("nxt%d" % m, "v", lambda q: [q.tensor_scalar(blk(T.nxt, m), ps(h, 128 * tr, 128 * tr + 128), MAG, -MAG, Alu.add, Alu.add)], [h],
-           ["nxt%d" % m], cv(128), rel=h)
-        vcp("cu%d" % m, blk(T.cu, m), (T.Ut if m < 5 else T.U2)[:, 128:128 + F + 128 * top].indirect(bl),
-            (uk(top) if m < 5 else ["U2"]) + ["bl%d" % m], 0, cost=cg(128))
-        ub = T.Ut[:, 128 + F + 128 * m:256 + F + 128 * m]
-        if m in (0, 1, 3):
-            column("Uc%d" % m, ub, m, bl, "bl%d" % m, top)
+        nk = "Pc%d" % m if rem is None else "snew%d" % m
+        op("new%d" % m, "v", lambda q: [q.tensor_scalar(new, ps(h, 0, 128), MAG, 2048.0 - MAG, Alu.add, Alu.add)], [h], [nk], cv(128), rel=h)
+        if tr:
+            op("nxt%d" % m, "v", lambda q: [q.tensor_scalar(blk(T.nxt, m), ps(h, 128, 256), MAG, -MAG, Alu.add, Alu.add)], [h],
+               ["nxt%d" % m], cv(128), rel=h)
+        elif m != 2:
+            both("nxt%d" % m, blk(T.nxt, m), new, [nk], cv(128), plus=-2048.0)
+        copy = m in (1, 5, 6)
+        win, rd = uwin(T.U2 if copy else T.Ut, top).indirect(bl), (["U2"] if copy else uk(top)) + ["bl%d" % m]
         if m == 2:
-            column("cf3", blk(T.cf, 3), m, bl, "bl%d" % m, top)
+            both("cf3", blk(T.cf, 3, 144), uwin(T.Ut, top).indirect(T.bl[:, 20:29]), rd, cg(144))
+            turned(2, blk(T.cf, 3, 144), "cf3")
+        else:
+            vcp("cu%d" % m, blk(T.cu, m), win, rd, 0, cost=cg(128))
+        if m in (0, 1, 3):
+            column("Uc%d" % m, ublk(m), m, win, rd)
         if rem is None:
             return
         n = len(T.cores)
         r = T.rank_of(core)
         dst, src = T.cores[(r + lev) % n], T.cores[(r - lev) % n]
-        wide = [(new, T.Pt[:, F + 128 * m:F + 128 * m + 128])] + ([(blk(T.cf, 3), ub)] if m == 2 else [])
-        thin = [(blk(T.cu, m), blk(T.rcu, rem)), (blk(T.nxt, m), blk(T.rxt, rem))]
+        wide = [(new, T.Pt[:, F + 128 * m:F + 128 * m + 128])] + ([(cfb(3), ublk(2))] if m == 2 else [])
+        prs = [(blk(a, j, 64), blk(b, j, 64)) for a, b in wide for j in range(2)] + [(blk(T.cu, m), blk(T.rcu, rem))]
+        if m != 2:
+            prs.append((blk(T.nxt, m), blk(T.rxt, rem)))
+
+        def share(k):
+            w = 1
+            while 2 * w * len(prs) <= k:
+                w *= 2
+            return w
 
         def send(q):
             rid, pid = topo.addr(dst, core)
             e = topo.engines(core, dst)
-            for prs in (wide, thin):
-                w = len(e) // len(prs)
-                q.remote_dma_fused([RemoteDMATransfer(dst_ids=[DstId(rid=rid, pnc=pid)], dma_engine_mask=sum(1 << x for x in e[j * w:(j + 1) * w]),
-                                                      remote_sem=T.sem["arr%d" % m], src=a, dst=b) for j, (a, b) in enumerate(prs)],
-                                   local_sem=T.sem.sent)
-            return 2 * len(e)
-        op("send%d" % m, "g", send, ["snew%d" % m, "cu%d" % m, "nxt%d" % m] + (["cf3"] if m == 2 else []), ["sent%d" % m], 1000.0, kind="r")
-        op("recv%d" % m, "n%d" % m, 2 * len(topo.engines(src, core)), ["sent%d" % m], ["Pc%d" % m, "rc%d" % m] + (["Uc2"] if m == 2 else []),
-           C["rem"], kind="w", sem="arr%d" % m)
+            w = share(len(e))
+            q.remote_dma_fused([RemoteDMATransfer(dst_ids=[DstId(rid=rid, pnc=pid)], dma_engine_mask=sum(1 << x for x in e[j * w:(j + 1) * w]),
+                                                  remote_sem=T.sem["arr%d" % m], src=a, dst=b) for j, (a, b) in enumerate(prs)],
+                               local_sem=T.sem.sent)
+            return w * len(prs)
+        op("send%d" % m, "g", send, ["snew%d" % m, "cu%d" % m, "cf3" if m == 2 else "nxt%d" % m], ["sent%d" % m], 1000.0, kind="r")
+        op("recv%d" % m, "n%d" % m, share(len(topo.engines(src, core))) * len(prs), ["sent%d" % m],
+           ["Pc%d" % m, "rc%d" % m] + (["Uc2"] if m == 2 else []), C["rem"], kind="w", sem="arr%d" % m)
 
-    def ublk(m):
-        return T.Ut[:, 128 + F + 128 * m:256 + F + 128 * m]
+    def late():
+        h = "fx"
+        rows = [(3, 0), (4, 0), (4, 1)]
 
-    def fix(j, c, slot, u):
-        h = "f%d" % j
-        op(h, "p", lambda q: [q.matmul(ps(h, 0, 128), ident(0), T.negm[:], True, False),
-                              q.matmul(ps(h, 0, 128), blk(T.sel34, slot - 3), ublk(c), False, True)],
-           ["I0", "negm", "sel%d" % slot, "Uc%d" % c], [h], cp(640), acq=(h, 1))
-        op("fxs%d" % j, "v", lambda q: [q.tensor_tensor_scan(blk(T.fxs, j), T.rst16[:, 0:128], ps(h, 0, 128), 0.0, Alu.add, Alu.max)],
-           [h, "rst16"], ["fxs%d" % j], cv(128), rel=h)
-        vcp("fxu%d" % j, blk(T.fxu, j, 8), T.fxs[:, j * 128 + 15:(j + 1) * 128:16], ["fxs%d" % j], 8)
-        vts("fx%d" % j, T["G%d" % GOF[u]][:, slot::16] if u in SUMV else blk(T.GX, j),
-            T.Pt[:, 0:F + 128 * (slot + 1)].indirect(blk(T.fxu, j, 8)), -2048.0, None,
-            Alu.add, None, pk(slot + 1) + ["fxu%d" % j], 0, wr=gkeys(GOF[u]) if u in SUMV else None, cost=cg(128))
+        def mm(q):
+            r = []
+            for j, (slot, c) in enumerate(rows):
+                r.append(q.matmul(ps(h, 128 * j, 128 * j + 128), ident(0), T.posm[:], True, False))
+                r.append(q.matmul(ps(h, 128 * j, 128 * j + 128), blk(T.sel34, slot - 3), ublk(c), False, True))
+            return r
+        op(h, "p", mm, ["I0", "posm", "sel3", "sel4", "Uc0", "Uc1"], [h], cp(3 * 640, 6), acq=(h, 1))
+        op("fxs", "v", lambda q: [q.tensor_tensor_scan(T.TT[:, 0:384], T.rst[:], ps(h, 0, 384), 0.0, Alu.add, Alu.min)],
+           [h, "rst0", "rst1", "rst2"], ["TT0_0", "TT0_1", "TT1_0"], cv(384), rel=h)
+        vcp("fxu", T.fxu[:], T.TT[:, 15:384:16], ["TT0_0", "TT0_1", "TT1_0"], 24)
+        both("GX", T.GX[:], T.Pt[:, 0:F + 128 * 5].indirect(T.fxu[:]), pk(5) + ["fxu"], cg(384), plus=-2048.0)
+        h2 = "dl"
+        src = [(blk(T.GX, 0), 0), (T["G%d" % GOF["R1"]][:, 3::16], 1), (blk(T.GX, 1), 0), (blk(T.GX, 2), 1)]
 
-    cand = {0: (7, blk(T.cf, 0), "cf0"), 1: (0, ublk(0), "Uc0"), 2: (8, blk(T.cf, 1), "cf1"), 3: (1, ublk(1), "Uc1"),
-            4: (3, ublk(3), "Uc3"), 5: (2, blk(T.cf, 3), "cf3"), 6: (9, blk(T.cf, 2), "cf2")}
-    opn = {0: (7, T.stu[:, 0:8], "stu", 0, blk(T.cf, 0), "cf0"), 1: (0, None, None, 0, ublk(0), "Uc0"),
-           2: (8, T.stu[:, 8:16], "stu", 0, None, None), 3: (1, blk(T.bl, 1, 8), "bl1", 1, None, None),
-           4: (3, None, None, 2, ublk(3), "Uc3"), 5: (2, blk(T.bl, 2, 8), "bl2", 0, None, None),
+        def mm2(q):
+            r = []
+            for j, (x, c) in enumerate(src):
+                r.append(q.matmul(ps(h2, 128 * j, 128 * j + 128), ident(7), blk(T.nxt, c), True, False))
+                r.append(q.matmul(ps(h2, 128 * j, 128 * j + 128), ident(0), x, False, True))
+            return r
+        op(h2, "p", mm2, ["GX", "I0", "I7", "nxt0", "nxt1"] + gkeys(GOF["R1"]), [h2], cp(1024, 8), acq=(h2, 1))
+        op("abs" + h2, "s", lambda q: [q.activation(T.AR01[:, 14:16, :, :], ps(h2, 0, 512), Act.Abs)], [h2],
+           akeys("R0", 14, 16) + akeys("R1", 14, 16), cv(512), rel=h2)
+
+    cand = {0: (7, cfb(0), "cf0"), 1: (0, ublk(0), "Uc0"), 2: (8, cfb(1), "cf1"), 3: (1, ublk(1), "Uc1"),
+            4: (3, ublk(3), "Uc3"), 5: (2, cfb(3), "cf3"), 6: (9, cfb(2), "cf2")}
+    opn = {0: (7, None, None, 0, cfb(0), "cf0"), 1: (0, None, None, 0, ublk(0), "Uc0"),
+           2: (8, T.stu[:, 8:16], "stu", 0, None, None), 3: (1, T.bl[:, 10:18], "bl1", 1, None, None),
+           4: (3, None, None, 2, ublk(3), "Uc3"), 5: (2, T.bl[:, 20:28], "bl2", 0, None, None),
            6: (9, T.stu[:, 16:24], "stu", 0, None, None)}
     for m in range(7):
         u = "E%d" % m
         c, cf, cfk = cand[m]
-        part[0] = u
-        gather(u, blk(T.cu, c), "cu%d" % c, TOP[m])
-        dist(u, LEV[m], [(T.X16, 128 * t) for t in TIMES[m]], "X16")
+        part[0] = "g" + u
+        if LEV[m]:
+            if c > 7:
+                turned(c, blk(T.cf, c - 7, 144), cfk)
+            direct(u, blk(T.cu, c), "cu%d" % c, TOP[m], (2, 5, 6).index(m))
+        else:
+            gather(u, blk(T.cu, c), "cu%d" % c, TOP[m])
+            part[0] = u
+            dist(u, 0, *symbols(m))
         elect(m, cf, cfk)
         part[0] = "X%d" % m
         extend(m, *opn[m])
         part[0] = "S%d" % m
         snap(m)
         part[0] = "M%d" % m
-        mix(u, LEV[m], m)
-    part[0] = "F"
-    fix(0, 0, 3, "R0")
-    fix(1, 0, 4, "R0")
-    fix(2, 1, 4, "R1")
+        expo(u, LEV[m])
+    halves = [(0, 8, 8), (0, 4, 4), (0, 2, 2), (0, 1, 1)]
+    own = {}
     for m in (2, 3, 0, 1, 4, 5, 6):
         u = "R%d" % m
-        part[0] = u
         rem = {2: 0, 5: 1, 6: 2}.get(m)
+        part[0] = "g" + u
+        if m == 2:
+            both("Xe3", blk(T.XR, 12), T.Pt[:, F + 256:F + 384], ["Pc2"], cv(128))
+            dma("XR3", "y", [(blk(T.XR, 12 + j), blk(T.XR, 12)) for j in (1, 2, 3)], ["Xe3"], ["XR3"], "xr3")
+            direct(u, blk(T.rcu, 0), "rc2", 3, 3)
+            continue
         if rem is not None:
             gather(u, blk(T.rcu, rem), "rc%d" % m, m + 1)
-            dist(u, 0, [(T.rxt, 128 * rem)], "rc%d" % m)
-        else:
-            if m == 4:
-                gather(u, blk(T.cu, 4), "cu4", 5)
-            dist(u, 0, [(T.nxt, 128 * m)], "nxt%d" % m)
-        mix(u, 0, m)
+        elif m == 4:
+            gather(u, blk(T.cu, 4), "cu4", 5)
+        part[0] = u
+        own[u] = (blk(T.nxt, m), "nxt%d" % m) if rem is None else (blk(T.rxt, rem), "rc%d" % m)
+        dist(u, 0, [own[u][0]], own[u][1])
+        if u in SCAN:
+            expo(u, 0)
+            scan(u, m)
+    for k in FOLD + [k for k in SETS if k not in FOLD]:
+        part[0] = "H" + k
+        if k[0] == "R":
+            joint(k, own)
+            end = 14 if k == "R01" else 16
+            for a in range(RELU.get(k, 0), end, 4):
+                weigh(k, a, min(end, a + 4))
+        if k == "R01":
+            part[0] = "F"
+            late()
+            weigh(k, 14, 16)
+            part[0] = "H" + k
+        if PART.get(k, 16):
+            total(k, [(0, 7, 7), (0, 4, 3), (0, 2, 2), (0, 14, 2), (0, 1, 1)] if k == "R01" else halves[:HALVE.get(k, 4)])
+        if k[0] == "R":
+            m, w = int(k[1]), 128 * len(SETS[k])
+            if k in PART:
+                rest(k, m, w)
+            else:
+                store("yz%d" % m, T.yz[:, 128 * m:128 * m + w], result(T, k) if k in FOLD else T["A" + k][:, 0, :, :],
+                      [x for u in SETS[k] for x in summed(u)[1]], 7 + m)
+    part[0] = "M"
+    for m in range(7):
+        mixture(m)
     return ops, bank
 
 
-def depend(ops, C):
+def depend(ops):
     lw, rs = {}, {}
     for k, o in enumerate(ops):
         d = set()
@@ -549,7 +740,7 @@ def depend(ops, C):
         d.discard(k)
         same = set(x for x in d if o["eng"] == "p" and ops[x]["eng"] == "p" and o["wr"] == ops[x]["wr"])
         o["dep"] = d - same
-        o["lag"] = [(x, 0.0 if x in same else after(ops[x], C)) for x in sorted(d)]
+        o["lag"] = [(x, 0.0 if x in same else ops[x]["lat"]) for x in sorted(d)]
         for x in o["rd"]:
             rs.setdefault(x, []).append(k)
         for x in o["wr"]:
@@ -557,179 +748,384 @@ def depend(ops, C):
             rs[x] = []
 
 
-def after(o, C):
-    return o["lat"] if o["kind"] == "a" else C["dma"] if o["kind"] == "d" else C["lat"]
-
-
-def plan(ops, C, boost=None):
+def bundles(ops):
     n = len(ops)
-    boost = BOOST if boost is None else boost
-    pr = [0.0] * n
-    cost = [o["cost"] for o in ops]
-    eng = [o["eng"] for o in ops]
-    acq = [o["acq"] for o in ops]
-    for k in range(n - 1, -1, -1):
-        pr[k] = max(pr[k], boost.get(ops[k]["part"], 0.0)) + cost[k]
-        for d, lag in ops[k]["lag"]:
-            if pr[k] + lag > pr[d]:
-                pr[d] = pr[k] + lag
-    rels, users = {}, [[] for o in ops]
+    users = [[] for o in ops]
+    rels = {}
     for k, o in enumerate(ops):
-        pr[k] += boost.get(o["part"] + o["eng"], 0.0) + boost.get(o["name"], 0.0)
+        for d, lag in o["lag"]:
+            users[d].append(k)
         if o["rel"]:
             rels.setdefault(o["rel"], []).append(k)
-        for d, lag in o["lag"]:
-            users[d].append((k, lag))
-    fin = [0.0] * n
-    holder, bfree, held = [None] * 8, [0.0] * 8, {}
-    banks, extra, order = {}, {}, []
-    wait = [len(o["lag"]) for o in ops]
-    rdy = [0.0] * n
-    left = {e: [] for e in eng}
-    free = {e: 0.0 for e in eng}
+    own = list(range(n))
+    for k, o in enumerate(ops):
+        if o["acq"]:
+            last = max(rels[o["acq"][0]])
+            down, up = {k}, set(rels[o["acq"][0]])
+            for x in range(k + 1, last + 1):
+                if any(d in down for d, lag in ops[x]["lag"]):
+                    down.add(x)
+            for x in range(last, k - 1, -1):
+                if any(y in up for y in users[x]):
+                    up.add(x)
+            for x in down & up:
+                own[x] = k
+    members = {}
     for k in range(n):
-        if not wait[k]:
-            left[eng[k]].append(k)
-    far = 1e30
-    for step in range(n):
-        one, two = min(bfree), min(max(bfree[x], bfree[x + 1]) for x in (0, 2, 4, 6))
-        t0, e0 = far, None
-        for e, ks in left.items():
-            if ks:
-                if e == "p":
-                    t = min(max(rdy[k], (0.0, one, two)[acq[k][1]]) if acq[k] else rdy[k] for k in ks)
-                else:
-                    t = min(rdy[k] for k in ks)
-                t = max(t, free[e])
-                if t < t0:
-                    t0, e0 = t, e
-        k, t = None, 0.0
-        for x in left[e0]:
-            tx = max(rdy[x], (0.0, one, two)[acq[x][1]]) if acq[x] else rdy[x]
-            if tx <= t0 + SLACK and (k is None or pr[x] > pr[k]):
-                k, t = x, max(tx, t0)
-        o = ops[k]
-        if acq[k]:
-            h, w = acq[k]
-            fit = [b for b in range(0, 8, w) if max(bfree[b:b + w]) <= t]
-            b = fit[0] if w == 2 else max(fit, key=lambda x: (bfree[x ^ 1] > t, x))
-            banks[h] = b
-            extra[k] = [r for x in range(b, b + w) if holder[x] for r in rels[holder[x]]]
-            held[h] = [len(rels[h]), 0.0, b, w]
-            for x in range(b, b + w):
-                holder[x] = h
-                bfree[x] = far
-        fin[k] = free[e0] = t + cost[k]
-        if o["rel"]:
-            z = held[o["rel"]]
-            z[0] -= 1
-            z[1] = max(z[1], fin[k] + C["lat"])
-            if not z[0]:
-                for x in range(z[2], z[2] + z[3]):
-                    bfree[x] = z[1]
-        order.append(k)
-        left[e0].remove(k)
-        for x, lag in users[k]:
+        members.setdefault(own[k], []).append(k)
+    pre = {u: set(own[d] for x in members[u] for d, lag in ops[x]["lag"]) - {u} for u in members}
+    post = {u: [x for x in pre if u in pre[x]] for u in members}
+    inner = {k: [(x, lag) for x in users[k] if own[x] == own[k] for d, lag in ops[x]["lag"] if d == k] for k in range(n)}
+    return members, pre, post, rels, inner
+
+
+def plan(ops, C, bun, key, eng):
+    members, pre, post, rels, inner = bun
+    n = len(ops)
+    cost = [o["cost"] for o in ops]
+    lags = [o["lag"] for o in ops]
+    st, fin = [0.0] * n, [0.0] * n
+    busy = {e: ([], []) for e in eng}
+    held = [[] for b in range(8)]
+    banks = {}
+    wait = {u: len(pre[u]) for u in pre}
+    ready = [u for u in wait if not wait[u]]
+
+    def find(b, t):
+        lo, hi = 0, len(b)
+        while lo < hi:
+            mid = (lo + hi) // 2
+            if b[mid] <= t:
+                lo = mid + 1
+            else:
+                hi = mid
+        return lo
+
+    def put(k, t):
+        for d, lag in lags[k]:
+            if fin[d] + lag > t:
+                t = fin[d] + lag
+        a, b = busy[eng[k]]
+        c = cost[k]
+        j = find(b, t)
+        while j < len(a) and a[j] < t + c:
+            t = b[j]
+            j += 1
+        a.insert(j, t)
+        b.insert(j, t + c)
+        st[k], fin[k] = t, t + c
+
+    def take(k):
+        a, b = busy[eng[k]]
+        j = a.index(st[k])
+        del a[j], b[j]
+    while ready:
+        u = max(ready, key=key.get)
+        ready.remove(u)
+        ms = members[u]
+        if len(ms) == 1:
+            put(u, 0.0)
+        else:
+            h, w = ops[u]["acq"]
+            t = 0.0
+            while True:
+                for k in ms:
+                    put(k, t)
+                for k in ms[-2::-1]:
+                    c = cost[k]
+                    end = min([st[x] - lag for x, lag in inner[k]] or [0.0])
+                    if end - c > st[k] + 1.0:
+                        old = st[k]
+                        take(k)
+                        a, b = busy[eng[k]]
+                        j = find(a, end - 1e-6)
+                        while j and b[j - 1] > end - c + 1e-6:
+                            end = min(end, a[j - 1])
+                            j -= 1
+                        put(k, max(old, end - c - 1e-6))
+                s, e = st[u], max(fin[k] for k in ms) + C["lat"]
+                clash = [min([y for x, y, z in held[q] if x < e and y > s] or [0.0]) for q in range(8)]
+                fit = [q for q in range(0, 8, w) if not max(clash[q:q + w])]
+                if fit:
+                    q = fit[0] if w == 2 else max(fit, key=lambda x: (clash[x ^ 1] > 0, x))
+                    banks[h] = q
+                    for x in range(q, q + w):
+                        held[x].append((s, e, u))
+                    break
+                for k in ms:
+                    take(k)
+                t = max(t + 1.0, min(x for x in clash if x))
+        for x in post[u]:
             wait[x] -= 1
-            if fin[k] + lag > rdy[x]:
-                rdy[x] = fin[k] + lag
             if not wait[x]:
-                left[eng[x]].append(x)
-    return order, banks, extra, fin
+                ready.append(x)
+    extra = {}
+    for q in range(8):
+        hs = sorted(held[q])
+        for a, b in zip(hs, hs[1:]):
+            extra.setdefault(b[2], []).extend(rels[ops[a[2]]["acq"][0]])
+    return sorted(range(n), key=lambda k: (st[k], k)), banks, extra, fin, eng
 
 
-def replay(ops, order, extra, C):
+def replay(ops, p, C):
     fin, free = [0.0] * len(ops), {}
-    for k in order:
+    extra, eng = p[2], p[4]
+    for k in p[0]:
         o = ops[k]
-        t = free.get(o["eng"], 0.0)
+        t = free.get(eng[k], 0.0)
         for d, lag in o["lag"]:
             if fin[d] + lag > t:
                 t = fin[d] + lag
         for d in extra.get(k, ()):
             if fin[d] + C["lat"] > t:
                 t = fin[d] + C["lat"]
-        fin[k] = free[o["eng"]] = t + o["cost"]
+        fin[k] = free[eng[k]] = t + o["cost"]
     return max(fin) + C["dma"]
 
 
-def search(T, topo, core, rounds):
+def search(T, topo, core, rounds, seed0=12345):
     sets = []
     for ch in VARY:
         C = dict(COST)
         C.update(ch)
         ops = build(T, topo, core, C)[0]
-        depend(ops, C)
+        depend(ops)
         sets.append((ops, C))
     ops, C = sets[0]
-    names = sorted(set(o["part"] + o["eng"] for o in ops if o["eng"] in "vspg")) + sorted(set(o["part"] for o in ops))
-    single = [o["name"] for o in ops if o["eng"] in "vspg"]
-    seed = [12345]
+    n = len(ops)
+    bun = bundles(ops)
+    members = bun[0]
+    units = sorted(members)
+    parts = {}
+    for u in units:
+        parts.setdefault(ops[u]["part"], []).append(u)
+    names = sorted(parts)
+    free = [k for k in range(n) if ops[k]["eng"] == "vs"]
+    tail = [0.0] * n
+    for k in range(n - 1, -1, -1):
+        tail[k] = max(tail[k], BOOST.get(ops[k]["part"], 0.0)) + ops[k]["cost"]
+        for d, lag in ops[k]["lag"]:
+            tail[d] = max(tail[d], tail[k] + lag)
+    load = [o["cost"] if o["eng"] in "vsp" else 0.0 for o in ops]
+    seed = [seed0]
 
     def rnd():
         seed[0] = (seed[0] * 1103515245 + 12345) % 2147483648
         return (seed[0] >> 8) / 8388608.0
 
-    def value(b):
-        p = plan(ops, C, b)
-        r = [replay(o, p[0], p[2], c) for o, c in sets]
-        return (r[0] + sum(r)) / (len(r) + 1), p, r
-    cur = dict(BOOST)
-    now = best = value(cur)
+    def value(key, eng):
+        p = plan(ops, C, bun, key, eng)
+        r = [replay(o, p, c) / c["norm"] for o, c in sets]
+        return (r[0] + sum(r)) / (len(r) + 1) + SOFT * sum(c * f for c, f in zip(load, p[3])) / sum(load), p, r
+    eng = [("s" if o["name"] in ONS else "v") if o["eng"] == "vs" else o["eng"] for o in ops]
+    now = best = value({u: max(tail[x] for x in members[u]) for u in units}, eng)
     for j in range(rounds):
-        b = dict(cur)
-        for z in range(1 + int(rnd() * 2.5)):
-            pool = names if rnd() < 0.6 else single
-            x = pool[int(rnd() * len(pool))]
-            b[x] = b.get(x, 0.0) + (rnd() + rnd() - 1.0) * (4000.0, 16000.0, 50000.0)[int(rnd() * 3)]
-        v = value(b)
-        if v[0] <= now[0] or rnd() < math.exp((now[0] - v[0]) / (400.0 * (1.0 - j / rounds))):
-            cur, now = b, v
+        fin, eng = now[1][3], list(now[1][4])
+        key = {u: ops[u]["cost"] - fin[u] for u in units}
+        if rnd() < 0.25:
+            for z in range(1 + int(rnd() * 2)):
+                k = free[int(rnd() * len(free))]
+                eng[k] = "s" if eng[k] == "v" else "v"
+        else:
+            for z in range(1 + int(rnd() * 2)):
+                d = (rnd() + rnd() - 1.0) * (1500.0, 5000.0, 15000.0)[int(rnd() * 3)]
+                for u in (parts[names[int(rnd() * len(names))]] if rnd() < 0.3 else [units[int(rnd() * len(units))]]):
+                    key[u] += d
+        v = value(key, eng)
+        if v[0] <= now[0] or rnd() < math.exp(max(-50.0, (now[0] - v[0]) / (HEAT * (1.0 - j / rounds)))):
+            now = v
             if v[0] < best[0]:
                 best = v
     return best
 
 
+def improve(T, topo, core, p, rounds, seed0=777):
+    data = []
+    for j, ch in enumerate(VARY):
+        C = dict(COST)
+        C.update(ch)
+        ops = build(T, topo, core, C)[0]
+        depend(ops)
+        data.append(([o["cost"] for o in ops], [o["lag"] for o in ops], C["lat"], C["dma"], (1.0 if j else 2.0) / C["norm"] / (len(VARY) + 1)))
+    n = len(ops)
+    order, eng, bank = list(p[0]), list(p[4]), dict(p[1])
+    pred = [[d for d, lag in o["lag"]] for o in ops]
+    succ = [[] for o in ops]
+    rels = {}
+    for k, o in enumerate(ops):
+        for d in pred[k]:
+            succ[d].append(k)
+        if o["rel"]:
+            rels.setdefault(o["rel"], []).append(k)
+    acq = {o["acq"][0]: (k, o["acq"][1]) for k, o in enumerate(ops) if o["acq"]}
+    load = [c if o["eng"] in "vsp" else 0.0 for c, o in zip(data[0][0], ops)]
+    holds = set(k for k, o in enumerate(ops) if o["acq"] or o["rel"])
+    seed = [seed0]
+
+    def rnd():
+        seed[0] = (seed[0] * 1103515245 + 12345) % 2147483648
+        return (seed[0] >> 8) / 8388608.0
+
+    def chain(order, bank):
+        pos = [0] * n
+        for j, k in enumerate(order):
+            pos[k] = j
+        on = [[] for b in range(8)]
+        for h, (k, w) in acq.items():
+            for b in range(bank[h], bank[h] + w):
+                on[b].append((pos[k], max(pos[r] for r in rels[h]), h))
+        extra = {}
+        for b in range(8):
+            on[b].sort()
+            for x, y in zip(on[b], on[b][1:]):
+                if x[1] > y[0]:
+                    return None, y[2], on
+                extra.setdefault(acq[y[2]][0], []).extend(rels[x[2]])
+        return extra, None, on
+
+    def value(order, eng, extra):
+        v, res = 0.0, []
+        for cost, lags, lat, dma, wt in data:
+            fin, why, last = [0.0] * (n + 1), [-1] * n, dict.fromkeys(eng, -1)
+            for k in order:
+                w = last[eng[k]]
+                t = fin[w]
+                for d, lag in lags[k]:
+                    if fin[d] + lag > t:
+                        t = fin[d] + lag
+                        w = d
+                if k in extra:
+                    for d in extra[k]:
+                        if fin[d] + lat > t:
+                            t = fin[d] + lat
+                            w = d
+                fin[k] = t + cost[k]
+                why[k] = w
+                last[eng[k]] = k
+            v += (max(fin) + dma) * wt
+            res.append((fin, why))
+        return v + SOFT2 * sum(c * f for c, f in zip(load, res[0][0])) / sum(load), res
+    extra = chain(order, bank)[0]
+    now, res = value(order, eng, extra)
+    best = (now, order, bank, extra, res, eng)
+    for it in range(rounds):
+        fin, why = res[int(rnd() * len(res))]
+        path = []
+        k = fin.index(max(fin)) if rnd() < 0.7 else int(rnd() * n)
+        while k >= 0:
+            path.append(k)
+            k = why[k]
+        k = path[int(rnd() * len(path))]
+        o2, e2, b2 = order, eng, bank
+        r = rnd()
+        if ops[k]["eng"] == "vs" and r < 0.3:
+            e2 = list(eng)
+            e2[k] = "s" if eng[k] == "v" else "v"
+        elif ops[k]["acq"] and r < 0.3:
+            h, w = ops[k]["acq"]
+            b2 = dict(bank)
+            b2[h] = int(rnd() * 8) // w * w
+        else:
+            j = why[k]
+            up = rnd() < 0.75
+            if j >= 0 and eng[j] == eng[k] and j not in pred[k] and rnd() < 0.5:
+                k, up = j, False
+            at = to = order.index(k)
+            step, link = (-1, succ) if up else (1, pred)
+            hop = 1 + int(rnd() ** 3 * 8)
+            x = at + step
+            while hop and 0 <= x < n:
+                if eng[order[x]] == eng[k]:
+                    to = x
+                    hop -= 1
+                x += step
+            group = {k}
+            for x in range(at + step, to + step, step):
+                if not group.isdisjoint(link[order[x]]):
+                    group.add(order[x])
+            if order[to] in group:
+                continue
+            a, b = min(at, to), max(at, to) + 1
+            ins, out = [x for x in order[a:b] if x in group], [x for x in order[a:b] if x not in group]
+            o2 = order[:a] + (ins + out if up else out + ins) + order[b:]
+        x2, bad, on = chain(o2, b2) if b2 is not bank or (o2 is not order and not group.isdisjoint(holds)) else (extra, None, None)
+        for tries in range(3):
+            if x2 is not None:
+                break
+            w = acq[bad][1]
+            a = [x for x in on[b2[bad]] if x[2] == bad][0]
+            fit = [b for b in range(0, 8, w) if not any(x[0] < a[1] and a[0] < x[1] and x[2] != bad for q in range(b, b + w) for x in on[q])]
+            if not fit:
+                break
+            b2 = dict(b2)
+            b2[bad] = fit[int(rnd() * len(fit))]
+            x2, bad, on = chain(o2, b2)
+        if x2 is None:
+            continue
+        v, r2 = value(o2, e2, x2)
+        if v <= now or rnd() < math.exp(max(-50.0, (now - v) / (HEAT2 * (1.0 - it / rounds)))):
+            cost, f0 = data[0][0], r2[0][0]
+            order = sorted(o2, key=lambda k: f0[k] - cost[k])
+            now, res, eng, bank, extra = v, r2, e2, b2, x2
+            if v < best[0]:
+                best = (v, order, bank, extra, res, eng)
+    return best[0], (best[1], best[2], best[3], best[4][0][0], best[5]), [max(f) + d[3] for (f, w), d in zip(best[4], data)]
+
+
 PLAN = {}
+
+
+def hand_back(g, core, T, topo):
+    for r in T.cores:
+        hs = helpers(T, topo, r)
+        if core in hs:
+            rid, pid = topo.addr(r, core)
+            sent = 0
+            for k in FOLD[hs.index(core)::len(hs)]:
+                g.wait_ge(T.sem["f" + k], len(topo.engines(r, core)))
+                g.remote_dma(result(T, k), result(T, k), T.sem["b" + k], T.sem.sent, pid, rid, topo.mask(core, r))
+                sent += len(topo.engines(core, r))
+            if sent:
+                g.wait_ge(T.sem.sent, sent)
 
 
 def rank_program(g, core, T, topo):
     if T.rank_of(core) is None:
+        hand_back(g, core, T, topo)
         return
     ops, bank = build(T, topo, core, COST)
-    depend(ops, COST)
+    depend(ops)
     if not PLAN:
-        PLAN["p"] = search(T, topo, core, ROUNDS)[1]
-    order, banks, extra, fin = PLAN["p"]
+        PLAN["p"] = improve(T, topo, core, search(T, topo, core, ROUNDS, 3)[1], MORE, 9)[1]
+    order, banks, extra, fin, eng = PLAN["p"]
     bank.update(banks)
     Q = {"v": g.vector, "s": g.scalar, "p": g.tensor, "g": g, "y": g.sync}
     total = {s: 0 for s in SEMAPHORES}
-    mark, seen, alone = {}, {}, [False]
+    mark, seen = {}, {}
     for k in order:
         o = ops[k]
         if o["kind"] == "w":
             total[o["sem"]] = o["fn"]
             mark[k] = (o["sem"], o["fn"])
             continue
-        q = Q[o["eng"]]
+        if o["kind"] == "e":
+            mark[k] = mark[o["fn"]]
+            continue
+        q = Q[eng[k]]
         need = {}
         for d in list(o["dep"]) + extra.get(k, []):
             s, v = mark[d]
             need[s] = max(need.get(s, 0), v)
-        if o["eng"] == "g" and o["kind"] == "c":
-            if o["name"][:3] == "Sel" or alone[0]:
-                need["cg"] = total["cg"]
-            alone[0] = o["name"][:3] == "Sel"
         for s, v in sorted(need.items()):
-            if seen.get((o["eng"], s), 0) < v:
+            if seen.get((eng[k], s), 0) < v:
                 q.wait_ge(T.sem[s], v)
-                seen[(o["eng"], s)] = v
+                seen[(eng[k], s)] = v
         if o["kind"] == "r":
             total["sent"] += o["fn"](q)
             mark[k] = ("sent", 0)
             continue
-        s, inc = (o["sem"], 16) if o["kind"] in "da" else (CSEM[o["eng"]], 1)
-        for ins in o["fn"](q):
+        s, inc = (o["sem"], 16) if o["kind"] == "d" else (CSEM[eng[k]], 1)
+        for ins in (o["fn"](q, eng[k]) if o["eng"] == "vs" else o["fn"](q)):
             ins.then_inc(T.sem[s], inc)
             total[s] += inc
         mark[k] = (s, total[s])

@@ -1,6 +1,6 @@
 import math
 from concourse.bass import DstId, RemoteDMATransfer
-from concourse.mybir import AluOpType as Alu, ActivationFunctionType as Act
+from concourse.mybir import AluOpType as Alu, AxisListType as Ax, ActivationFunctionType as Act
 
 F, S, W = 864, 128, 1760
 SP = 32
@@ -16,23 +16,28 @@ HALVE = {"E01": 4, "E26": 3, "E35": 4, "E4": 3, "R01": 5, "R23": 4, "R56": 4}
 SCAN = ["R4", "R5", "R6"]
 WARM = ["hl"] if SCAN else []
 RELU = {}
-PART = {"R01": 14, "R23": 4}
+PART = {"R01": 14, "R23": 6}
 APART = list(WIDE)
 FINE = {"E0", "E1", "E3", "E4"}
 EARLY = {"E0", "E1", "E3", "E4"}
 GOF = {"E0": 0, "E1": 1, "E3": 3, "E4": 4, "R0": 1, "R1": 3, "R3": 4, "R4": 0, "R5": 1, "R6": 4}
 ORDER01 = [0, 1, 2] + list(range(5, 16)) + [3, 4]
-CONV = set()
+LAST = {"R6"}
+FIXV = ("ym4", "ym5", "ym6", "yz")
+UG = True
+WHOLE = set()
+CONV = {"Uc0", "Uc1", "Uc3"}
 QUART = set()
-ONS = {"X16", "gE0_0", "cf0", "gE1_0", "gE3_0"}
-ROUNDS = 30
-MORE = 60001
+ONS = {"X16", "gE0_0", "gE1_0"}
+ROUNDS = 1
+STAGES = ((95000, 170.0, 0.04, 2.0), (80000, 90.0, 0.02, 2.0))
 SOFT, HEAT = 0.3, 150.0
-SOFT2 = 0.05
-HEAT2 = 250.0
+HOP = 60
 VARY = ({}, {"cyc": 0.85, "pe": 0.43, "fw": 350.0, "row": 50.0, "back": 5000.0, "gam": 1.6, "norm": 0.95},
-        {"cyc": 0.85, "pe": 0.43, "dma": 3200.0, "rem": 5500.0, "lat": 150.0, "back": 6000.0, "call": 2000.0, "norm": 0.95})
-RANK = "E0:200 E1:150 E3:100 E4:40 S0:180 S1:130 S3:60 S4:20 E2:60 S2:60 X0:170 X1:120 X3:60"
+        {"cyc": 0.85, "pe": 0.43, "dma": 3200.0, "rem": 5500.0, "lat": 150.0, "back": 6000.0, "call": 2000.0, "gam": 1.45, "sca": 3.0, "norm": 0.95})
+RANK = ("E0:200 S0:180 X0:170 E1:150 X1:140 S1:130 M0:120 E2:110 S2:105 E3:100 HE0:100 M1:95 M2:90 X3:85 S3:80 HE1:80 HE2:78 E6:75 X4:70 "
+        "M3:66 E5:62 E4:60 M6:55 R0:52 R1:52 S4:50 HE3:50 S5:48 S6:46 M5:45 M4:44 HE6:42 HR01:35 HE5:30 HE4:30 R2:28 R3:28 HR23:20 "
+        "F:15 M:10 R4:10 R5:5")
 BOOST = {x.split(":")[0]: 1000.0 * int(x.split(":")[1]) for x in RANK.split()}
 
 f32, f16, b16, i32, u16 = "float32", "float16", "bfloat16", "int32", "uint16"
@@ -46,29 +51,30 @@ SCRATCH = {
     "cm16": ("sbuf", [128, 128], b16),
     "idf": ("sbuf", [128, 128], f32), "idh": ("sbuf", [128, 128], f32), "IDS": ("sbuf", [128, 8 * 128], b16),
     "Sel": ("sbuf", [128, 512], b16), "n32": ("sbuf", [128, 32], f32),
-    "BO": ("sbuf", [128, 24], f32), "BO1": ("sbuf", [128, 8], f32), "G8": ("sbuf", [128, 8], b16),
+    "BO": ("sbuf", [128, 48], f32), "BO1": ("sbuf", [128, 8], f32), "G8": ("sbuf", [128, 8], b16),
     "BN": ("sbuf", [128, 384], b16), "nBB": ("sbuf", [128, 128], b16), "sel34": ("sbuf", [128, 256], f32),
     "mR": ("sbuf", [128, 128], f32), "posm": ("sbuf", [128, 128], b16),
     "kio": ("sbuf", [128, 256], b16), "TM": ("sbuf", [128, 256], b16), "rst": ("sbuf", [128, 384], f32),
     "QA": ("sbuf", [128, 16], f32), "QB": ("sbuf", [128, 16], f32), "QE": ("sbuf", [128, 16], b16),
     "DmA": ("sbuf", [128, 128], f32), "Dm": ("sbuf", [128, 128], f32),
-    "pi": ("sbuf", [128, 8], i32), "pj": ("sbuf", [128, 16], i32), "pf": ("sbuf", [128, 8], f32), "pg": ("sbuf", [128, 16], f32),
-    "lt": ("sbuf", [128, 8], u16), "TT": ("sbuf", [128, 512], f32), "XR": ("sbuf", [128, 2048], f32),
+    "pi": ("sbuf", [128, 8], i32), "pj": ("sbuf", [128, 8], i32), "pf": ("sbuf", [128, 8], f32), "pg": ("sbuf", [128, 64], f32),
+    "lt": ("sbuf", [128, 8], u16), "TT": ("sbuf", [128, 512], f32), "XR": ("sbuf", [128, 1536], f32), "XQ": ("sbuf", [128, 512], i32),
+    "stj": ("sbuf", [128, 20], i32),
     "lf": ("sbuf", [128, 40], f32), "lu": ("sbuf", [128, 40], u16), "BM": ("sbuf", [128, 896], f32),
     "cu": ("sbuf", [128, 10 * 128], u16),
     "cf": ("sbuf", [128, 4 * 144], f32),
     "rcu": ("sbuf", [128, 3 * 128], u16), "rxt": ("sbuf", [128, 3 * 128], f16),
     "snew": ("sbuf", [128, 3 * 128], i32), "nxt": ("sbuf", [128, 7 * 128], f16),
-    "rm": ("sbuf", [128, 5 * 128], f32), "kp": ("sbuf", [128, 5 * 128], b16), "val": ("sbuf", [128, 5 * 128], f32),
+    "rm": ("sbuf", [128, 4 * 128], f32), "kp": ("sbuf", [128, 4 * 128], b16), "val": ("sbuf", [128, 4 * 128], f32),
     "M1": ("sbuf", [128, 3 * 128], f16), "A1": ("sbuf", [128, 10 * 128], f16), "A2": ("sbuf", [128, 4 * 128], f16),
     "bl": ("sbuf", [128, 7 * 10], u16), "Pb": ("sbuf", [128, 7 * 128], f16),
-    "eq": ("sbuf", [128, 3 * 256], b16), "offu": ("sbuf", [128, 7 * 8], u16), "old": ("sbuf", [128, 4 * 128], f32),
+    "eq": ("sbuf", [128, 3 * 256], b16), "offu": ("sbuf", [128, 7 * 8], u16), "old": ("sbuf", [128, 2 * 128], f32),
     "fxu": ("sbuf", [128, 24], u16), "GX": ("sbuf", [128, 384], f16),
-    "prod": ("sbuf", [128, 3 * 128], f32), "yzb": ("sbuf", [128, 3 * 128], f32),
+    "prod": ("sbuf", [128, 3 * 128], f32), "yzb": ("sbuf", [128, 3 * 128], f32), "ymb": ("sbuf", [128, 3 * 128], f32),
     "pos": ("sbuf", [128, 2 * 1024 if RELU else 16], f16), "DmB": ("sbuf", [128, 128], b16),
     "SC": ("sbuf", [128, 2048], f32), "RES": ("sbuf", [128, 128 * sum(len(SETS[_k]) * WIDE.get(_k, 1) for _k in FOLD) or 8], f32),
 }
-ROT = [0, 1, 2, 0, 1, 3, 4]
+ROT = [0, 1, 2, 0, 1, 2, 3]
 for _k in SETS:
     SCRATCH["A" + _k] = ("sbuf", [128, len(SETS[_k]), 2048] if _k in APART else [128, 16, len(SETS[_k]), 128], f32)
 for _k in SCAN:
@@ -77,11 +83,11 @@ for _k in sorted(set(GOF.values())):
     SCRATCH["G%d" % _k] = ("sbuf", [128, 2048], f16)
 for _k in range(4):
     SCRATCH["ps%d" % _k] = ("psum", [128, 1024], f32)
-SEMAPHORES = (["cv", "cs", "cp", "cg", "sent", "arr2", "arr5", "arr6", "ld0", "ld1", "ld2", "ld3", "ld4", "cpu", "cpv", "rt", "bz", "bm", "xr0", "xr1", "xr2", "xr3"]
+SEMAPHORES = (["cv", "cs", "cp", "cg", "sent", "arr2", "arr5", "arr6", "ld0", "ld1", "ld2", "ld3", "ld4", "ld5", "cpu", "cpv", "rt", "bz", "bm", "xr0", "xr1", "xr2", "xr3"]
               + [_x + _u for _u in SETS for _x in "afb"] + ["t%d" % _u for _u in range(14)])
 CSEM = {"v": "cv", "s": "cs", "p": "cp", "g": "cg"}
-COST = {"norm": 1.0, "cyc": 0.96, "pe": 0.48, "pfix": 5.0, "gam": 1.56, "sca": 3.8, "fix": 60.0, "lat": 90.0, "dma": 2200.0,
-        "rem": 3500.0, "gdma": 800.0, "bw": 280.0, "fw": 650.0, "row": 28.0, "back": 3500.0, "tti": 0.3, "call": 1000.0}
+COST = {"norm": 1.0, "cyc": 0.96, "pe": 0.48, "pfix": 5.0, "gam": 1.85, "sca": 4.8, "fix": 60.0, "lat": 90.0, "dma": 2200.0,
+        "rem": 3500.0, "gdma": 800.0, "bw": 280.0, "fw": 650.0, "row": 28.0, "back": 3500.0, "tti": 0.15, "call": 1000.0, "iss": 200.0}
 
 
 def helpers(T, topo, core):
@@ -157,10 +163,17 @@ def build(T, topo, core, C):
             if e == "s":
                 return [q.activation(out, b, Act.Copy) if plus is None else q.activation(out, b, Act.Identity, bias=plus)]
             return [q.tensor_copy(out, b) if plus is None else q.tensor_scalar(out, b, plus, None, Alu.add)]
-        op(name, "vs", fn, rd, wr or [name], cost, rel=rel)
+        if name.startswith(FIXV):
+            op(name, "v", lambda q: fn(q, "v"), rd, wr or [name], cost, rel=rel)
+        else:
+            op(name, "vs", fn, rd, wr or [name], cost, rel=rel)
+
+    def line(name, out, in_, a, b, rd, n):
+        op(name, "vs", lambda q, e: [q.tensor_scalar(out, in_, a, b, Alu.mult, Alu.add) if e == "v" else
+                                     q.activation(out, in_, Act.Identity, scale=a, bias=b)], rd, [name], cv(n))
 
     def dma(name, eng, pairs, rd, wr, sem, size=0):
-        op(name, eng, lambda q: [q.dma_start(o, i) for o, i in pairs], rd, wr, 60.0 * len(pairs), kind="d", sem=sem, lat=C["dma"] + size / 500.0)
+        op(name, eng, lambda q: [q.dma_start(o, i) for o, i in pairs], rd, wr, C["iss"] * len(pairs), kind="d", sem=sem, lat=C["dma"] + size / 500.0)
 
     def add(name, out, in_, rd, wr, sem, size):
         op(name, "g", lambda q: [q.dma_start(out, in_, accum_op=Alu.add, max_dma_last_dim=8192)], rd, wr + [name], C["gdma"], kind="d",
@@ -168,7 +181,7 @@ def build(T, topo, core, C):
         op(name + "d", "D", len(ops) - 1, rd + [name], wr, size / C["bw"], kind="e", lat=C["dma"] / 2)
 
     dma("sti", "y", [(T.sti[:], T.st[:])], [], ["sti"], "ld0")
-    dma("sui", "y", [(T.sui[:], T.su[:])], [], ["sui"], "ld1")
+    dma("sui", "s", [(T.sui[:], T.su[:])], [], ["sui"], "ld1")
     dma("P0", "s", [(T.Pt[:, 0:F], T.th[:])], [], ["P0"], "ld2")
     dma("xsi", "y", [(T.xsi[:], T.xs[:])], [], ["xsi"], "ld3")
     dma("hvb", "y", [(T.hvb[:], T.hv[:])], [], ["hvb"], "ld4")
@@ -183,14 +196,15 @@ def build(T, topo, core, C):
         if k == 2 and not RELU:
             continue
         if k in (0, 3, 4, 7):
-            sact("I%d" % k, ident(k), T.idf[:], Act.Copy, ["idf"], 128, scale=sc)
+            line("I%d" % k, ident(k), T.idf[:], sc, 0.0, ["idf"], 128)
         else:
             ga("I%d" % k, ident(k), T.zer[:], ["zer"], [[-1, 128]], Alu.not_equal, sc, 0, 1, 128)
     ga("idh", T.idh[:], T.zer[:], ["zer"], [[-1, 128]], Alu.not_equal, 0.5, 0, 1, 128)
     ga("BO1", T.BO1[:], T.ones[:, 0:8], ["ones"], [[-16, 8]], Alu.is_ge, 0.0, 0, 1, 8)
     ga("G8", T.G8[:], T.BO1[:], ["BO1"], [[16, 8]], Alu.is_ge, 0.0, 15, -1, 8)
     for l in range(3):
-        sact("BO%d" % l, blk(T.BO, l, 8), T.G8[:], Act.Copy, ["G8"], 8, scale=16.0 * (1 << l))
+        ga("BP%d" % l, blk(T.BO, 3 + l, 8), T.zer[:, 0:8], ["zer"], [[16, 8]], Alu.is_gt, 16.0 * (1 << l), 0, -1, 8)
+        ga("BQ%d" % l, blk(T.BO, l, 8), blk(T.BO, 3 + l, 8), ["BP%d" % l], [[16, 8]], Alu.is_ge, 0.0, 15, -1, 8)
     gi("lf0", T.lf[:, 0:32], [[1, 32]], 0, 0, 32)
     gi("lf1", T.lf[:, 32:40], [[16, 8]], 15, 0, 8)
     vcp("lu", T.lu[:], T.lf[:], ["lf0", "lf1"], 40)
@@ -199,27 +213,26 @@ def build(T, topo, core, C):
     for e in range(2):
         ga("BM%d" % e, blk(T.BN, 2), T.ones[:], ["ones"], [[-32, 4], [0, 32]], Alu.is_ge, 0.0, -16 * e, 1, 128, "BNt")
         ga("BN%d" % e, blk(T.BN, e), blk(T.BN, 2), ["BNt"], [[32, 4], [0, 32]], Alu.is_ge, 0.0, 15 + 16 * e, -1, 128)
-    gi("pi", T.pi[:], [[0, 8]], 0, 1, 8, False)
+    gi("pi", T.pi[:, 0:4], [[0, 4]], 0, 1, 4, False)
+    gi("pi2", T.pi[:, 4:8], [[0, 4]], 0, 128, 4, False)
     vts("pj0", T.pj[:, 0:2], T.pi[:, 0:2], 15, None, Alu.bitwise_and, None, ["pi"], 2)
-    vts("pj1", T.pj[:, 2:4], T.pi[:, 2:4], 31, None, Alu.bitwise_and, None, ["pi"], 2)
-    vcp("pf", T.pf[:, 0:4], T.pj[:, 0:4], ["pj0", "pj1"], 4)
-    sact("pf4", T.pf[:, 4:5], T.pf[:, 0:1], Act.Identity, ["pf"], 1, bias=16.0)
-    sact("pf5", T.pf[:, 5:6], T.pf[:, 2:3], Act.Identity, ["pf"], 1, scale=4096.0, bias=4096.0)
-    for j, (sh, mask) in enumerate([(4, 1), (0, 1), (1, 3), (3, 1)]):
-        vts("pb%d" % j, T.pj[:, 4 + j:5 + j], T.pi[:, 0:1], sh, mask, Alu.logical_shift_right, Alu.bitwise_and, ["pi"], 1)
-    vcp("pc", T.pg[:, 0:4], T.pj[:, 4:8], ["pb0", "pb1", "pb2", "pb3"], 4)
-    vtt("pd", T.pg[:, 4:5], T.pg[:, 0:1], T.pg[:, 1:2], Alu.not_equal, ["pc"], 1)
-    vtt("pe", T.pg[:, 5:6], T.pg[:, 0:1], T.pg[:, 1:2], Alu.is_gt, ["pc"], 1)
-    vts("ph", T.pj[:, 8:9], T.pg[:, 2:3], 4.0, T.pg[:, 5:6], Alu.add, Alu.subtract, ["pc", "pe"], 1)
-    vts("pk", T.pj[:, 9:10], T.pj[:, 8:9], 3, None, Alu.bitwise_and, None, ["ph"], 1)
-    vts("pl", T.pg[:, 6:7], T.pj[:, 9:10], 32.0, T.pg[:, 3:4], Alu.mult, Alu.add, ["pk", "pc"], 1)
-    vts("pm", T.pg[:, 7:8], T.pg[:, 0:1], 16.0, T.pg[:, 6:7], Alu.mult, Alu.add, ["pl", "pc"], 1)
-    vts("pn", T.pg[:, 8:9], T.pg[:, 4:5], 128.0, T.pg[:, 7:8], Alu.mult, Alu.add, ["pm", "pd"], 1)
-    vts("lt", T.lt[:], T.lf[:, 0:8], 2.0, T.pg[:, 8:9], Alu.mult, Alu.add, ["lf0", "pn"], 8)
+    vts("pj1", T.pj[:, 2:3], T.pi[:, 2:3], 31, None, Alu.bitwise_and, None, ["pi"], 1)
+    vts("pj2", T.pj[:, 3:4], T.pi[:, 4:5], 15 * 128, None, Alu.bitwise_and, None, ["pi2"], 1)
+    vcp("pf", T.pf[:, 0:4], T.pj[:, 0:4], ["pj0", "pj1", "pj2"], 4)
+    line("pf4", T.pf[:, 4:5], T.pf[:, 0:1], 1.0, 16.0, ["pf"], 1)
+    for j, (a, b, z, base, pat) in enumerate([(0, 16, 2, 0, [[1, 2], [32, 4]]), (1, 16, 2, 128, [[1, 2], [32, 4]]), (17, 32, 2, 16, [[1, 2], [32, 4]]),
+                                              (16, 32, 2, 112, [[1, 2], [32, 4]]), (16, 32, 8, 240, [[1, 2]])]):
+        op("tb%d" % j, "g", lambda q, a=a, b=b, z=z, base=base, pat=pat: [q.iota(T.pg[:, a:b:z], pat, base, 0, allow_small_or_imprecise_dtypes=True)],
+           [], ["tb"], 150.0)
+    for k in range(4):
+        ga("n32_%d" % k, T.n32[:], T.n32[:] if k else T.zer[:, 0:32], ["n32" if k else "zer"], [[-1, 32]], Alu.not_equal, -1.0, -32 * k, 1, 32, "n32")
+    vtt("pm", T.pg[:, 32:64], T.pg[:, 0:32], T.n32[:], Alu.mult, ["tb", "n32"], 32)
+    op("pn", "v", lambda q: [q.tensor_reduce(T.pf[:, 6:7], T.pg[:, 32:64], Ax.X, Alu.add, negate=True)], ["pm"], ["pn"], cv(32))
+    vts("lt", T.lt[:], T.lf[:, 0:8], 2.0, T.pf[:, 6:7], Alu.mult, Alu.add, ["lf0", "pn"], 8)
     gi("kio", T.kio[:], [[16, 2], [0, 8], [1, 16]], 0, 0, 256)
     vts("mR", T.mR[:], blk(T.kio, 0), T.pf[:, 0:1], None, Alu.is_equal, None, ["kio", "pf"], 128)
-    sact("TM", T.TM[:], T.kio[:], Act.Relu, ["kio", "pf5"], 256, scale=-4096.0, bias=T.pf[:, 5:6])
-    sact("posm", T.posm[:], T.mR[:], Act.Identity, ["mR"], 128, scale=-4096.0, bias=4096.0)
+    vts("TM", T.TM[:], T.kio[:], T.pf[:, 2:3], 4096.0, Alu.is_le, Alu.mult, ["kio", "pf"], 256)
+    line("posm", T.posm[:], T.mR[:], -4096.0, 4096.0, ["mR"], 128)
     for k in range(2):
         ga("sel%d" % (3 + k), blk(T.sel34, k), T.zer[:], ["zer"], [[-16, 8], [0, 16]], Alu.not_equal, 1.0, -3 - k, 1, 128)
     ga("QB", T.QB[:], T.QA[:], ["QA"], [[0, 2], [-32, 4], [0, 2]], Alu.is_ge, 0.0, 0, 1, 16)
@@ -230,21 +243,25 @@ def build(T, topo, core, C):
     ga("Dm", T.Dm[:], T.zer[:], ["zer"], [[-1, 128]], Alu.not_equal, -1.0, -1, 1, 128)
     ga("DmA", T.DmA[:], T.Dm[:], ["Dm"], [[0, 8], [-1, 16]], Alu.is_gt, 0.0, 15, 0, 128)
     ga("Dm", T.Dm[:], T.DmA[:], ["DmA"], [[-1, 128]], Alu.not_equal, 1.0, 0, 1, 128)
-    gi("U2", T.U2[:, 0:896], [[1, 896]], F, 0, 896)
-    dma("bz", "y", [(blk(T.BM, m), T.zer[:]) for m in range(7)], ["zer"], ["BM"], "bz")
-    dma("bm", "y", [(T.BM[m::16, m * 128:(m + 1) * 128], T.U2[m::16, m * 128:(m + 1) * 128]) for m in range(7)], ["U2"], ["BM"], "bm")
-    for l in range(2):
-        sact("lnc%d" % l, T.hl[:, 1 + l:2 + l], T.ones[:, 0:1], Act.Ln, ["ones"] + ["lnc0"] * l, 1, scale=1.0 / (16 << l), cost=None if l else 1400.0)
-    sact("lnh", T.lnh[:, 0:16], T.hvb[:], Act.Ln, ["hvb", "lnc1"], 16, scale=1.0 / 16)
+    gi("nm0", blk(T.U2, 1), [[1, 128]], F, 0, 128)
+    op("U2", "vs", lambda q, e: [q.tensor_scalar(blk(T.U2, 0), blk(T.U2, 1), T.pf[:, 3:4], None, Alu.add) if e == "v" else
+                                 q.activation(blk(T.U2, 0), blk(T.U2, 1), Act.Identity, bias=T.pf[:, 3:4])], ["nm0", "pf"], ["U2"], cv(128))
+    vset("BMa", T.BM[:, 0:256], 0.0, 256)
+    gi("BMb", T.BM[:, 256:896], [[0, 640]], 0, 0, 640)
+    for k, ms, sem in (("BMa", (0, 1), "bz"), ("BMb", range(2, 7), "bm")):
+        dma(sem, "y", [(T.BM[m::16, m * 128:(m + 1) * 128], T.U2[m::16, 0:128]) for m in ms], ["U2"], [k], sem)
+    sact("lnc", T.hl[:, 1:3], T.lf[:, 1:3], Act.Ln, ["lf0"], 2, scale=1.0 / 32, cost=1400.0)
+    sact("lnh", T.lnh[:, 0:16], T.hvb[:], Act.Ln, ["hvb", "lnc"], 16, scale=1.0 / 16)
     if SCAN:
         sact("hl", T.hl[:, 0:1], T.lnh[:, 15:16], Act.Exp, ["lnh"], 1, cost=1600.0)
         op("hrec", "v", lambda q: [q.reciprocal(T.hrec[:], T.hvb[:])], ["hvb"], ["hrec"], 300.0)
-        vset("r160", T.RT[:, 0:1], 0.0, 1)
+        gi("r160", T.RT[:, 0:1], [[0, 1]], 0, 0, 1)
         vtt("RT", T.RT[:, 1:16], T.hvb[:, 0:15], T.hrec[:, 1:16], Alu.mult, ["hvb", "hrec"], 16)
         for w in (16, 32, 64, 128, 256, 512):
             dma("RT%d" % w, "y", [(T.RT[:, w:2 * w], T.RT[:, 0:w])], ["RT", "r160"], ["RT"], "rt")
-        vts("n32", T.n32[:], T.lf[:, 0:32], T.pf[:, 2:3], -1.0, Alu.is_equal, Alu.mult, ["lf0", "pf"], 32)
-        both("Sel", T.Sel[:], T.n32[:].indirect(T.lu[:, 0:32]), ["n32", "lu"], cg(512))
+        gi("Sel", T.Sel[:], [[0, 512]], 0, 0, 512)
+        for k in range(4):
+            ga("Sel%d" % k, T.Sel[:], T.Sel[:], ["Sel"], [[-1, 32], [0, 16]], Alu.not_equal, -1.0, -32 * k, 1, 512, "Sel")
     if any(k in SETS for k in RELU):
         vts("lnr", T.lnh[:, 16:32], T.lnh[:, 0:16], -8.0, None, Alu.add, None, ["lnh"], 16)
 
@@ -270,14 +287,16 @@ def build(T, topo, core, C):
             both(name, out, win, rd, cg(128), wr=wr)
 
     vcp("stu", T.stu[:, 0:24], T.sti[:], ["sti"], 24)
-    for l in (1, 2):
-        vcp("stv%d" % l, T.stu[:, 14 + 10 * l:22 + 10 * l], T.sti[:, 8 * l:8 * l + 8], ["sti"], 8)
-        vcp("stw%d" % l, T.stu[:, 22 + 10 * l:23 + 10 * l], T.sti[:, 8 * l:8 * l + 1], ["sti"], 1)
+    dma("stj", "y", [(T.stj[:, 10 * l + a:10 * l + a + n], T.st[:, 8 * l + 8:8 * l + 8 + n]) for l in (0, 1) for a, n in ((0, 8), (8, 2))], ["sti"], ["stj"], "ld5")
+    vcp("stv", T.stu[:, 24:44], T.stj[:], ["stj"], 20)
     vcp("cu7", blk(T.cu, 7), T.sui[:].indirect(T.stu[:, 0:8]), ["sui", "stu"], 128, cost=cg(128))
-    ga("U0", uwin(T.Ut, 0), T.sui[:], ["sui"], [[0, F]], Alu.is_equal, 0.0, 0, 0, F)
+    if UG:
+        ga("U0", uwin(T.Ut, 0), T.sui[:], ["sui"], [[0, F]], Alu.is_equal, 0.0, 0, 0, F)
+    else:
+        both("U0", uwin(T.Ut, 0), T.sui[:], ["sui"], cv(F))
     both("cf0", cfb(0), T.sui[:].indirect(T.stu[:, 0:8]), ["sui", "stu"], cg(128))
     for l in (1, 2):
-        both("cf%d" % l, blk(T.cf, l, 144), T.sui[:].indirect(T.stu[:, 14 + 10 * l:23 + 10 * l]), ["sui", "stv%d" % l, "stw%d" % l], cg(144))
+        both("cf%d" % l, blk(T.cf, l, 144), T.sui[:].indirect(T.stu[:, 14 + 10 * l:23 + 10 * l]), ["sui", "stv"], cg(144))
     both("X16", T.X16[:], T.xsi[:], ["xsi"], cv(512), plus=-2048.0)
     for z, m in enumerate((2, 5, 6)):
         h = "Xm%d" % z
@@ -321,7 +340,7 @@ def build(T, topo, core, C):
 
     def direct(u, cand, ck, top, z):
         for a in range(0, 16, 4):
-            vtt("g%s_%d" % (u, a), slab(u, a, a + 4), T.Pt[:, 0:F + 128 * top].indirect(cand[:, 8 * a:8 * a + 32]), blk(T.XR, z, 512), Alu.subtract,
+            vtt("g%s_%d" % (u, a), slab(u, a, a + 4), T.Pt[:, 0:F + 128 * top].indirect(cand[:, 8 * a:8 * a + 32]), blk(T.XR, z, 512) if z < 3 else T.XQ[:], Alu.subtract,
                 pk(top) + [ck, "XR%d" % z], 0, wr=akeys(u, a, a + 4), cost=cg(512) + 512 * C["tti"] * C["cyc"])
         part[0] = u
         for a in (0, 8):
@@ -413,13 +432,14 @@ def build(T, topo, core, C):
     MX, MK = {}, {}
 
     def store(name, dst, src, rd, k):
-        dma("st" + name, "y", [(dst, src)], rd, [], "t%d" % k)
+        dma("st" + name, "s" if name == "yz6" else "y", [(dst, src)], rd, [], "t%d" % k)
 
     def expo(u, lev):
-        for a in range(RELU.get(u, 0), 16, 8):
-            o = T["A" + u][:, 128 * a:128 * a + 1024] if u in SCAN else slab(u, a, a + 8)
-            sact("exp%s_%d" % (u, a), o, o, Act.Exp, akeys(u, a, a + 8) + WARM, 1024, wr=akeys(u, a, a + 8), scale=-1.0 / 512,
-                 bias=0.0 if u in SCAN else T.hl[:, 2:3] if lev else T.hl[:, 1:2])
+        w = 16 if u in WHOLE else 4 if u in LAST else 8
+        for a in range(RELU.get(u, 0), 16, w):
+            o = T["A" + u][:, 128 * a:128 * (a + w)] if u in SCAN else slab(u, a, a + w)
+            sact("exp%s_%d" % (u, a), o, o, Act.Exp, akeys(u, a, a + w) + WARM, 128 * w, wr=akeys(u, a, a + w), scale=-1.0 / 512,
+                 bias=0.0 if u in SCAN else T.hl[:, 1:2] if lev else T.hl[:, 2:3])
 
     def weigh(k, a, b):
         A, us = T["A" + k], SETS[k]
@@ -485,28 +505,33 @@ def build(T, topo, core, C):
         if len(xs) == 1 and not lev:
             MX[m], MK[m] = xs[0], keys
         else:
-            MX[m], MK[m] = xs[0], list(keys)
+            MX[m], MK[m] = (xs[0], list(keys)) if m < 4 else (blk(T.ymb, m - 4), ["ym%d" % m])
             h = "sum" + u
             prs = [(T.idf[:], x) for x in xs]
             if lev:
-                x, y = {2: (0, 1), 5: (3, 4), 6: (2, 5)}[m]
-                pr = blk(T.prod, {2: 0, 5: 1, 6: 2}[m])
-                vtt("prod%d" % m, pr, MX[x], MX[y], Alu.mult, MK[x] + MK[y], 128)
-                prs.append((T.idh[:], pr))
+                prs.append((T.idh[:], blk(T.prod, (2, 5, 6).index(m))))
                 keys = keys + ["prod%d" % m, "idh"]
             op(h, "p", lambda q: [q.matmul(ps(h, 0, 128), a, b, i == 0, i == len(prs) - 1) for i, (a, b) in enumerate(prs)],
                keys + ["idf"], [h], cp(len(prs) * 512, len(prs)), acq=(h, 1))
+            if m in (1, 4, 5):
+                x, y = {1: (0, 2), 4: (3, 5), 5: (2, 6)}[m]
+                op("prod%d" % y, "v", lambda q: [q.tensor_tensor(blk(T.prod, (2, 5, 6).index(y)), ps(h, 0, 128), MX[x], Alu.mult)], [h] + MK[x],
+                   ["prod%d" % y, h], cv(128), rel=h)
             both("ym%d" % m, MX[m], None, [h], cv(128), rel=h, wr=MK[m])
-        store("ym%d" % m, blk(T.ym, m), MX[m], MK[m], m)
+        if m < 4:
+            store("ym%d" % m, blk(T.ym, m), MX[m], MK[m], m)
+        elif m == 6:
+            store("ym4", T.ym[:, 512:896], T.ymb[:], ["ym4", "ym5", "ym6"], m)
 
     def scan(u, m):
         out = blk(T.yzb, m - 4)
-        for a in (0, 8):
-            sc = blk(T.SC, a // 8, 1024)
-            op("scan%s_%d" % (u, a), "v", lambda q, a=a, sc=sc: [q.tensor_tensor_scan(sc, T.RT[:], T["A" + u][:, 128 * a:128 * a + 1024], 0.0, Alu.mult, Alu.add)],
-               akeys(u, a, a + 8) + ["RT"], ["SC%d" % a], cv(1024))
+        w = 4 if u in LAST else 8
+        for a in range(0, 16, w):
+            op("scan%s_%d" % (u, a), "v", lambda q, a=a: [q.tensor_tensor_scan(T.SC[:, 128 * a:128 * (a + w)], T.RT[:, 0:128 * w],
+                                                                               T["A" + u][:, 128 * a:128 * (a + w)], 0.0, Alu.mult, Alu.add)],
+               akeys(u, a, a + w) + ["RT"], ["SC%d" % x for x in range(a, a + w, 4)], cv(128 * w))
         op("yz%d" % m, "vs", lambda q, e: [q.tensor_scalar(out, T.SC[:, 15::16], T.hl[:, 0:1], None, Alu.mult) if e == "v" else
-                                           q.activation(out, T.SC[:, 15::16], Act.Copy, scale=T.hl[:, 0:1])], ["SC0", "SC8", "hl"], ["yz%d" % m], cv(128))
+                                           q.activation(out, T.SC[:, 15::16], Act.Copy, scale=T.hl[:, 0:1])], ["SC0", "SC4", "SC8", "SC12", "hl"], ["yz%d" % m], cv(128))
         store("yz%d" % m, blk(T.yz, m), out, ["yz%d" % m], 7 + m)
 
     def elect(m, cf, cfk):
@@ -517,7 +542,7 @@ def build(T, topo, core, C):
            [cfk, "Dm", "one16", "kio"], [h], cp(640, 2), acq=(h, 1))
         for j in range(4):
             op("%s_%d" % (h, j), "p", lambda q, j=j: [q.matmul(ps(h, i, 128, 16), slab(u, i), blk(T.BO, LEV[m], 8), False, i == 15) for i in range(4 * j, 4 * j + 4)],
-               akeys(u, 4 * j, 4 * j + 4) + ["BO%d" % LEV[m], h], [h], cp(4 * 256, 4))
+               akeys(u, 4 * j, 4 * j + 4) + ["BQ%d" % LEV[m], h], [h], cp(4 * 256, 4))
         z = ROT[m]
         rm, kp, val = blk(T.rm, z), blk(T.kp, z), blk(T.val, z)
         rk, kk, vk = "rm_%d" % z, "kp_%d" % z, "val_%d" % z
@@ -554,11 +579,11 @@ def build(T, topo, core, C):
                                         for e in range(2)], [h + "c", "pf", "pf4"], ["off%d" % m], 2 * cv(4), rel=h)
         U, keys = (T.Ut, uk(top)) if m < 5 else (T.U2, ["U2"])
         if old is None:
-            old, oldk = blk(T.old, {2: 0, 3: 1, 5: 2, 6: 3}[m]), "old%d" % m
-            column(oldk, old, None, uwin(U, top).indirect(lst), keys + [lk])
+            old, oldk = blk(T.old, m % 2), "old_%d" % (m % 2)
+            column("old%d" % m, old, None, uwin(U, top).indirect(lst), keys + [lk], wr=[oldk])
         for k in (3, 2, 1, 0):
             vtt("ext%d_%d" % (m, k), U[:, 0:SP + F + 128 * top].indirect(T.offu[:, 8 * m + 2 * k:8 * m + 2 * k + 2]), blk(old, k, 32),
-                T.BM[:, 128 * m + 32 * k:128 * m + 32 * k + 32], Alu.max, ["off%d" % m, oldk, "BM"], 0, wr=keys + ["spare"],
+                T.BM[:, 128 * m + 32 * k:128 * m + 32 * k + 32], Alu.max, ["off%d" % m, oldk, "BMa" if m < 2 else "BMb"], 0, wr=keys + ["spare"],
                 cost=C["fix"] + 32 * C["sca"] * C["cyc"])
         if m == 4:
             dma("U4", "y", [(uwin(T.U2, 3), uwin(T.Ut, 3))], uk(3), ["U2"], "cpu", 640000)
@@ -686,8 +711,7 @@ def build(T, topo, core, C):
         rem = {2: 0, 5: 1, 6: 2}.get(m)
         part[0] = "g" + u
         if m == 2:
-            both("Xe3", blk(T.XR, 12), T.Pt[:, F + 256:F + 384], ["Pc2"], cv(128))
-            dma("XR3", "y", [(blk(T.XR, 12 + j), blk(T.XR, 12)) for j in (1, 2, 3)], ["Xe3"], ["XR3"], "xr3")
+            dma("XR3", "y", [(blk(T.XQ, j), T.Pt[:, F + 256:F + 384]) for j in range(4)], ["Pc2"], ["XR3"], "xr3")
             direct(u, blk(T.rcu, 0), "rc2", 3, 3)
             continue
         if rem is not None:
@@ -939,14 +963,14 @@ def search(T, topo, core, rounds, seed0=12345):
     return best
 
 
-def improve(T, topo, core, p, rounds, seed0=777):
+def improve(T, topo, core, p, rounds, seed0, HEAT2, SOFT2, lead=2.0):
     data = []
     for j, ch in enumerate(VARY):
         C = dict(COST)
         C.update(ch)
         ops = build(T, topo, core, C)[0]
         depend(ops)
-        data.append(([o["cost"] for o in ops], [o["lag"] for o in ops], C["lat"], C["dma"], (1.0 if j else 2.0) / C["norm"] / (len(VARY) + 1)))
+        data.append(([o["cost"] for o in ops], [o["lag"] for o in ops], C["lat"], C["dma"], (1.0 if j else lead) / C["norm"] / (len(VARY) - 1 + lead)))
     n = len(ops)
     order, eng, bank = list(p[0]), list(p[4]), dict(p[1])
     pred = [[d for d, lag in o["lag"]] for o in ops]
@@ -983,11 +1007,17 @@ def improve(T, topo, core, p, rounds, seed0=777):
                 extra.setdefault(acq[y[2]][0], []).extend(rels[x[2]])
         return extra, None, on
 
-    def value(order, eng, extra):
+    def value(order, eng, extra, a=0, old=None, limit=1e30):
         v, res = 0.0, []
-        for cost, lags, lat, dma, wt in data:
-            fin, why, last = [0.0] * (n + 1), [-1] * n, dict.fromkeys(eng, -1)
-            for k in order:
+        first = dict.fromkeys(eng, -1)
+        for k in order[:a]:
+            first[eng[k]] = k
+        rest = order[a:]
+        for j, (cost, lags, lat, dma, wt) in enumerate(data):
+            if j == 1 and old and (max(res[0][0]) - max(old[0][0])) * data[0][4] > limit:
+                return None, None
+            fin, why, last = (old[j][0][:], old[j][1][:], dict(first)) if old else ([0.0] * (n + 1), [-1] * n, dict(first))
+            for k in rest:
                 w = last[eng[k]]
                 t = fin[w]
                 for d, lag in lags[k]:
@@ -1017,25 +1047,26 @@ def improve(T, topo, core, p, rounds, seed0=777):
             k = why[k]
         k = path[int(rnd() * len(path))]
         o2, e2, b2 = order, eng, bank
+        start = order.index(k)
         r = rnd()
         if ops[k]["eng"] == "vs" and r < 0.3:
             e2 = list(eng)
             e2[k] = "s" if eng[k] == "v" else "v"
-        elif ops[k]["acq"] and r < 0.3:
+        if ops[k]["acq"] and r < 0.2:
             h, w = ops[k]["acq"]
             b2 = dict(bank)
             b2[h] = int(rnd() * 8) // w * w
-        else:
+        elif e2 is eng or r < 0.2:
             j = why[k]
-            up = rnd() < 0.75
-            if j >= 0 and eng[j] == eng[k] and j not in pred[k] and rnd() < 0.5:
+            up = rnd() < 0.7
+            if e2 is eng and j >= 0 and eng[j] == eng[k] and j not in pred[k] and rnd() < 0.5:
                 k, up = j, False
             at = to = order.index(k)
             step, link = (-1, succ) if up else (1, pred)
-            hop = 1 + int(rnd() ** 3 * 8)
+            hop = 1 + int(rnd() ** 4 * HOP)
             x = at + step
             while hop and 0 <= x < n:
-                if eng[order[x]] == eng[k]:
+                if eng[order[x]] == e2[k]:
                     to = x
                     hop -= 1
                 x += step
@@ -1046,6 +1077,7 @@ def improve(T, topo, core, p, rounds, seed0=777):
             if order[to] in group:
                 continue
             a, b = min(at, to), max(at, to) + 1
+            start = a
             ins, out = [x for x in order[a:b] if x in group], [x for x in order[a:b] if x not in group]
             o2 = order[:a] + (ins + out if up else out + ins) + order[b:]
         x2, bad, on = chain(o2, b2) if b2 is not bank or (o2 is not order and not group.isdisjoint(holds)) else (extra, None, None)
@@ -1053,8 +1085,8 @@ def improve(T, topo, core, p, rounds, seed0=777):
             if x2 is not None:
                 break
             w = acq[bad][1]
-            a = [x for x in on[b2[bad]] if x[2] == bad][0]
-            fit = [b for b in range(0, 8, w) if not any(x[0] < a[1] and a[0] < x[1] and x[2] != bad for q in range(b, b + w) for x in on[q])]
+            y = [x for x in on[b2[bad]] if x[2] == bad][0]
+            fit = [b for b in range(0, 8, w) if not any(x[0] < y[1] and y[0] < x[1] and x[2] != bad for q in range(b, b + w) for x in on[q])]
             if not fit:
                 break
             b2 = dict(b2)
@@ -1062,8 +1094,13 @@ def improve(T, topo, core, p, rounds, seed0=777):
             x2, bad, on = chain(o2, b2)
         if x2 is None:
             continue
-        v, r2 = value(o2, e2, x2)
-        if v <= now or rnd() < math.exp(max(-50.0, (now - v) / (HEAT2 * (1.0 - it / rounds)))):
+        if x2 is not extra:
+            for x in set(x2) | set(extra):
+                if x2.get(x) != extra.get(x):
+                    start = min(start, o2.index(x))
+        room = -HEAT2 * (1.0 - it / rounds) * math.log(1e-9 + rnd())
+        v, r2 = value(o2, e2, x2, start, res, room + 150.0)
+        if v is not None and v <= now + room:
             cost, f0 = data[0][0], r2[0][0]
             order = sorted(o2, key=lambda k: f0[k] - cost[k])
             now, res, eng, bank, extra = v, r2, e2, b2, x2
@@ -1096,7 +1133,10 @@ def rank_program(g, core, T, topo):
     ops, bank = build(T, topo, core, COST)
     depend(ops)
     if not PLAN:
-        PLAN["p"] = improve(T, topo, core, search(T, topo, core, ROUNDS, 3)[1], MORE, 9)[1]
+        p = search(T, topo, core, ROUNDS, 8)[1]
+        for rounds, heat, soft, lead in STAGES:
+            p = improve(T, topo, core, p, rounds, 3, heat, soft, lead)[1]
+        PLAN["p"] = p
     order, banks, extra, fin, eng = PLAN["p"]
     bank.update(banks)
     Q = {"v": g.vector, "s": g.scalar, "p": g.tensor, "g": g, "y": g.sync}

import math
from concourse.bass import DstId, RemoteDMATransfer
from concourse.mybir import AluOpType as Alu, AxisListType as Ax, ActivationFunctionType as Act

F, S, W = 864, 128, 1760
SP = 32
LEV = [0, 0, 1, 0, 0, 1, 2]
TIMES = [[0], [1], [0, 1], [2], [3], [2, 3], [0, 1, 2, 3]]
TOP = [0, 1, 0, 2, 4, 3, 0]
BIG = float(2 ** 23)
MAG = float(3 * 2 ** 22)
SETS = {"E0": ["E0"], "E1": ["E1"], "E2": ["E2"], "E6": ["E6"], "E3": ["E3"], "E4": ["E4"], "E5": ["E5"], "R23": ["R2", "R3"], "R01": ["R0", "R1"]}
WIDE = {"E0": 2, "E1": 2, "E2": 4, "E6": 4, "E5": 4, "E4": 4, "E3": 4, "R23": 2}
FOLD = ["E0", "E1", "E2", "E6", "E3", "R01", "E5", "E4", "R23"]
HALVE = {"E01": 4, "E26": 3, "E35": 4, "E4": 3, "R01": 5, "R23": 4, "R56": 4}
SCAN = ["R4", "R5", "R6"]
WARM = ["hl"] if SCAN else []
RELU = {}
PART = {"R01": 14, "R23": 6}
APART = list(WIDE)
FINE = {"E0", "E1", "E3", "E4"}
EARLY = {"E0", "E1", "E3", "E4"}
GOF = {"E0": 0, "E1": 1, "E3": 3, "E4": 4, "R0": 1, "R1": 3, "R3": 4, "R4": 0, "R5": 1, "R6": 4}
ORDER01 = [0, 1, 2] + list(range(5, 16)) + [3, 4]
LAST = {"R6"}
FIXV = ("ym4", "ym5", "ym6", "yz")
UG = True
WHOLE = set()
CONV = {"Uc0", "Uc1", "Uc3"}
QUART = set()
ONS = {"X16", "gE0_0", "gE1_0"}
ROUNDS = 1
STAGES = ((95000, 170.0, 0.04, 2.0), (80000, 90.0, 0.02, 2.0))
SOFT, HEAT = 0.3, 150.0
HOP = 60
VARY = ({}, {"cyc": 0.85, "pe": 0.43, "fw": 350.0, "row": 50.0, "back": 5000.0, "gam": 1.6, "norm": 0.95},
        {"cyc": 0.85, "pe": 0.43, "dma": 3200.0, "rem": 5500.0, "lat": 150.0, "back": 6000.0, "call": 2000.0, "gam": 1.45, "sca": 3.0, "norm": 0.95})
RANK = ("E0:200 S0:180 X0:170 E1:150 X1:140 S1:130 M0:120 E2:110 S2:105 E3:100 HE0:100 M1:95 M2:90 X3:85 S3:80 HE1:80 HE2:78 E6:75 X4:70 "
        "M3:66 E5:62 E4:60 M6:55 R0:52 R1:52 S4:50 HE3:50 S5:48 S6:46 M5:45 M4:44 HE6:42 HR01:35 HE5:30 HE4:30 R2:28 R3:28 HR23:20 "
        "F:15 M:10 R4:10 R5:5")
BOOST = {x.split(":")[0]: 1000.0 * int(x.split(":")[1]) for x in RANK.split()}

f32, f16, b16, i32, u16 = "float32", "float16", "bfloat16", "int32", "uint16"
SCRATCH = {
    "Pt": ("sbuf", [128, W], i32), "Ut": ("sbuf", [128, SP + W], f32), "U2": ("sbuf", [128, SP + F + 384], f32),
    "sui": ("sbuf", [128, F], i32), "sti": ("sbuf", [128, 24], i32), "stu": ("sbuf", [128, 44], u16),
    "xsi": ("sbuf", [128, 512], i32), "X16": ("sbuf", [128, 512], f16),
    "hvb": ("sbuf", [128, 16], b16), "hrec": ("sbuf", [128, 16], f32),
    "lnh": ("sbuf", [128, 32], f32), "hl": ("sbuf", [128, 8], f32), "RT": ("sbuf", [128, 1024], f32),
    "ones": ("sbuf", [128, 128], f32), "zer": ("sbuf", [128, 128], f32), "one16": ("sbuf", [128, 128], b16),
    "cm16": ("sbuf", [128, 128], b16),
    "idf": ("sbuf", [128, 128], f32), "idh": ("sbuf", [128, 128], f32), "IDS": ("sbuf", [128, 8 * 128], b16),
    "Sel": ("sbuf", [128, 512], b16), "n32": ("sbuf", [128, 32], f32),
    "BO": ("sbuf", [128, 48], f32), "BO1": ("sbuf", [128, 8], f32), "G8": ("sbuf", [128, 8], b16),
    "BN": ("sbuf", [128, 384], b16), "nBB": ("sbuf", [128, 128], b16), "sel34": ("sbuf", [128, 256], f32),
    "mR": ("sbuf", [128, 128], f32), "posm": ("sbuf", [128, 128], b16),
    "kio": ("sbuf", [128, 256], b16), "TM": ("sbuf", [128, 256], b16), "rst": ("sbuf", [128, 384], f32),
    "QA": ("sbuf", [128, 16], f32), "QB": ("sbuf", [128, 16], f32), "QE": ("sbuf", [128, 16], b16),
    "DmA": ("sbuf", [128, 128], f32), "Dm": ("sbuf", [128, 128], f32),
    "pi": ("sbuf", [128, 8], i32), "pj": ("sbuf", [128, 8], i32), "pf": ("sbuf", [128, 8], f32), "pg": ("sbuf", [128, 64], f32),
    "lt": ("sbuf", [128, 8], u16), "TT": ("sbuf", [128, 512], f32), "XR": ("sbuf", [128, 1536], f32), "XQ": ("sbuf", [128, 512], i32),
    "stj": ("sbuf", [128, 20], i32),
    "lf": ("sbuf", [128, 40], f32), "lu": ("sbuf", [128, 40], u16), "BM": ("sbuf", [128, 896], f32),
    "cu": ("sbuf", [128, 10 * 128], u16),
    "cf": ("sbuf", [128, 4 * 144], f32),
    "rcu": ("sbuf", [128, 3 * 128], u16), "rxt": ("sbuf", [128, 3 * 128], f16),
    "snew": ("sbuf", [128, 3 * 128], i32), "nxt": ("sbuf", [128, 7 * 128], f16),
    "rm": ("sbuf", [128, 4 * 128], f32), "kp": ("sbuf", [128, 4 * 128], b16), "val": ("sbuf", [128, 4 * 128], f32),
    "M1": ("sbuf", [128, 3 * 128], f16), "A1": ("sbuf", [128, 10 * 128], f16), "A2": ("sbuf", [128, 4 * 128], f16),
    "bl": ("sbuf", [128, 7 * 10], u16), "Pb": ("sbuf", [128, 7 * 128], f16),
    "eq": ("sbuf", [128, 3 * 256], b16), "offu": ("sbuf", [128, 7 * 8], u16), "old": ("sbuf", [128, 2 * 128], f32),
    "fxu": ("sbuf", [128, 24], u16), "GX": ("sbuf", [128, 384], f16),
    "prod": ("sbuf", [128, 3 * 128], f32), "yzb": ("sbuf", [128, 3 * 128], f32), "ymb": ("sbuf", [128, 3 * 128], f32),
    "pos": ("sbuf", [128, 2 * 1024 if RELU else 16], f16), "DmB": ("sbuf", [128, 128], b16),
    "SC": ("sbuf", [128, 2048], f32), "RES": ("sbuf", [128, 128 * sum(len(SETS[_k]) * WIDE.get(_k, 1) for _k in FOLD) or 8], f32),
}
ROT = [0, 1, 2, 0, 1, 2, 3]
for _k in SETS:
    SCRATCH["A" + _k] = ("sbuf", [128, len(SETS[_k]), 2048] if _k in APART else [128, 16, len(SETS[_k]), 128], f32)
for _k in SCAN:
    SCRATCH["A" + _k] = ("sbuf", [128, 2048], f32)
for _k in sorted(set(GOF.values())):
    SCRATCH["G%d" % _k] = ("sbuf", [128, 2048], f16)
for _k in range(4):
    SCRATCH["ps%d" % _k] = ("psum", [128, 1024], f32)
SEMAPHORES = (["cv", "cs", "cp", "cg", "sent", "arr2", "arr5", "arr6", "ld0", "ld1", "ld2", "ld3", "ld4", "ld5", "cpu", "cpv", "rt", "bz", "bm", "xr0", "xr1", "xr2", "xr3"]
              + [_x + _u for _u in SETS for _x in "afb"] + ["t%d" % _u for _u in range(14)])
CSEM = {"v": "cv", "s": "cs", "p": "cp", "g": "cg"}
COST = {"norm": 1.0, "cyc": 0.96, "pe": 0.48, "pfix": 5.0, "gam": 1.85, "sca": 4.8, "fix": 60.0, "lat": 90.0, "dma": 2200.0,
        "rem": 3500.0, "gdma": 800.0, "bw": 280.0, "fw": 650.0, "row": 28.0, "back": 3500.0, "tti": 0.15, "call": 1000.0, "iss": 200.0}


def helpers(T, topo, core):
    return [c for c in topo.cores_of(core) if T.rank_of(c) is None and topo.die(c) == topo.die(core)]


def result(T, k):
    a = 128 * sum(len(SETS[x]) * WIDE.get(x, 1) for x in FOLD[:FOLD.index(k)])
    return T.RES[:, a:a + 128 * len(SETS[k]) * WIDE.get(k, 1)]


def build(T, topo, core, C):
    ops = []
    bank = {}
    part = ["C"]
    setof = {u: (k, j) for k in SETS for j, u in enumerate(SETS[k])}

    def op(name, eng, fn, rd, wr, cost, kind="c", sem=None, acq=None, rel=None, lat=None):
        ops.append({"name": name, "eng": eng, "fn": fn, "rd": list(rd), "wr": list(wr), "cost": cost, "kind": kind,
                    "sem": sem, "acq": acq, "rel": rel, "part": part[0], "lat": C["lat"] if lat is None else lat})

    def cv(n, k=1.0):
        return C["fix"] + max(64, n * k) * C["cyc"]

    def cg(n):
        return C["fix"] + n * C["gam"] * C["cyc"]

    def cp(n, calls):
        return C["fix"] + n * C["pe"] + calls * C["pfix"]

    def ps(h, a, b, st=1):
        k = bank[h]
        o = (k % 2) * 512
        return T["ps%d" % (k // 2)][:, o + a:o + b:st]

    def blk(t, m, w=128):
        return t[:, m * w:(m + 1) * w]

    def ident(k):
        return blk(T.IDS, k)

    def gi(name, out, pat, base, cm, n, fl=True):
        if fl:
            op(name, "g", lambda q: [q.iota(out, pat, base, cm, allow_small_or_imprecise_dtypes=True)], [], [name], 130 + 2 * n * C["cyc"])
        else:
            op(name, "g", lambda q: [q.iota(out, pat, base, cm)], [], [name], 130 + 2 * n * C["cyc"])

    def ga(name, out, in_, rd, pat, cmp, fill, base, cm, n, wr=None):
        op(name, "g", lambda q: [q.affine_select(out, in_, pat, cmp, fill, base, cm)], rd, [wr or name], 170 + 2 * n * C["cyc"])

    def vts(name, out, in0, s1, s2, o0, o1, rd, n, wr=None, cost=None, **kw):
        if o1 is None:
            fn = lambda q: [q.tensor_scalar(out, in0, s1, None, o0)]
        else:
            fn = lambda q: [q.tensor_scalar(out, in0, s1, s2, o0, o1)]
        op(name, "v", fn, rd, wr or [name], cost or cv(n), **kw)

    def vcp(name, out, in_, rd, n, wr=None, cost=None):
        op(name, "v", lambda q: [q.tensor_copy(out, in_)], rd, wr or [name], cost or cv(n))

    def vtt(name, out, a, b, o, rd, n, wr=None, cost=None):
        op(name, "v", lambda q: [q.tensor_tensor(out, a, b, o)], rd, wr or [name], cost or cv(n, 2))

    def vset(name, out, x, n, rd=()):
        op(name, "v", lambda q: [q.memset(out, x)], rd, [name], cv(n))

    def sact(name, out, in_, func, rd, n, wr=None, cost=None, **kw):
        op(name, "s", lambda q: [q.activation(out, in_, func, **kw)], rd, wr or [name], cost or cv(n))

    def both(name, out, in_, rd, cost, plus=None, wr=None, rel=None):
        def fn(q, e):
            b = ps(rel, 0, in_ or 128) if rel else in_
            if e == "s":
                return [q.activation(out, b, Act.Copy) if plus is None else q.activation(out, b, Act.Identity, bias=plus)]
            return [q.tensor_copy(out, b) if plus is None else q.tensor_scalar(out, b, plus, None, Alu.add)]
        if name.startswith(FIXV):
            op(name, "v", lambda q: fn(q, "v"), rd, wr or [name], cost, rel=rel)
        else:
            op(name, "vs", fn, rd, wr or [name], cost, rel=rel)

    def line(name, out, in_, a, b, rd, n):
        op(name, "vs", lambda q, e: [q.tensor_scalar(out, in_, a, b, Alu.mult, Alu.add) if e == "v" else
                                     q.activation(out, in_, Act.Identity, scale=a, bias=b)], rd, [name], cv(n))

    def dma(name, eng, pairs, rd, wr, sem, size=0):
        op(name, eng, lambda q: [q.dma_start(o, i) for o, i in pairs], rd, wr, C["iss"] * len(pairs), kind="d", sem=sem, lat=C["dma"] + size / 500.0)

    def add(name, out, in_, rd, wr, sem, size):
        op(name, "g", lambda q: [q.dma_start(out, in_, accum_op=Alu.add, max_dma_last_dim=8192)], rd, wr + [name], C["gdma"], kind="d",
           sem=sem, lat=C["dma"] / 2)
        op(name + "d", "D", len(ops) - 1, rd + [name], wr, size / C["bw"], kind="e", lat=C["dma"] / 2)

    dma("sti", "y", [(T.sti[:], T.st[:])], [], ["sti"], "ld0")
    dma("sui", "s", [(T.sui[:], T.su[:])], [], ["sui"], "ld1")
    dma("P0", "s", [(T.Pt[:, 0:F], T.th[:])], [], ["P0"], "ld2")
    dma("xsi", "y", [(T.xsi[:], T.xs[:])], [], ["xsi"], "ld3")
    dma("hvb", "y", [(T.hvb[:], T.hv[:])], [], ["hvb"], "ld4")

    vset("ones", T.ones[:], 1.0, 128)
    vset("zer", T.zer[:], 0.0, 128)
    vset("one16", T.one16[:], 1.0, 64)
    vset("cm16", T.cm16[:], -15.0 / 32, 64)
    vset("QA", T.QA[:], -4096.0, 16)
    ga("idf", T.idf[:], T.ones[:], ["ones"], [[-1, 128]], Alu.is_equal, 0.0, 0, 1, 128)
    for k, sc in enumerate([1.0, 0.5, -2.0, 0.75, 0.25, 0.125, 0.0625, -1.0]):
        if k == 2 and not RELU:
            continue
        if k in (0, 3, 4, 7):
            line("I%d" % k, ident(k), T.idf[:], sc, 0.0, ["idf"], 128)
        else:
            ga("I%d" % k, ident(k), T.zer[:], ["zer"], [[-1, 128]], Alu.not_equal, sc, 0, 1, 128)
    ga("idh", T.idh[:], T.zer[:], ["zer"], [[-1, 128]], Alu.not_equal, 0.5, 0, 1, 128)
    ga("BO1", T.BO1[:], T.ones[:, 0:8], ["ones"], [[-16, 8]], Alu.is_ge, 0.0, 0, 1, 8)
    ga("G8", T.G8[:], T.BO1[:], ["BO1"], [[16, 8]], Alu.is_ge, 0.0, 15, -1, 8)
    for l in range(3):
        ga("BP%d" % l, blk(T.BO, 3 + l, 8), T.zer[:, 0:8], ["zer"], [[16, 8]], Alu.is_gt, 16.0 * (1 << l), 0, -1, 8)
        ga("BQ%d" % l, blk(T.BO, l, 8), blk(T.BO, 3 + l, 8), ["BP%d" % l], [[16, 8]], Alu.is_ge, 0.0, 15, -1, 8)
    gi("lf0", T.lf[:, 0:32], [[1, 32]], 0, 0, 32)
    gi("lf1", T.lf[:, 32:40], [[16, 8]], 15, 0, 8)
    vcp("lu", T.lu[:], T.lf[:], ["lf0", "lf1"], 40)
    ga("nB1", T.DmB[:], T.zer[:], ["zer"], [[16, 8], [0, 16]], Alu.is_gt, -1.0, 0, -1, 128)
    ga("nBB", T.nBB[:], T.DmB[:], ["nB1"], [[16, 8], [0, 16]], Alu.is_ge, 0.0, 15, -1, 128)
    for e in range(2):
        ga("BM%d" % e, blk(T.BN, 2), T.ones[:], ["ones"], [[-32, 4], [0, 32]], Alu.is_ge, 0.0, -16 * e, 1, 128, "BNt")
        ga("BN%d" % e, blk(T.BN, e), blk(T.BN, 2), ["BNt"], [[32, 4], [0, 32]], Alu.is_ge, 0.0, 15 + 16 * e, -1, 128)
    gi("pi", T.pi[:, 0:4], [[0, 4]], 0, 1, 4, False)
    gi("pi2", T.pi[:, 4:8], [[0, 4]], 0, 128, 4, False)
    vts("pj0", T.pj[:, 0:2], T.pi[:, 0:2], 15, None, Alu.bitwise_and, None, ["pi"], 2)
    vts("pj1", T.pj[:, 2:3], T.pi[:, 2:3], 31, None, Alu.bitwise_and, None, ["pi"], 1)
    vts("pj2", T.pj[:, 3:4], T.pi[:, 4:5], 15 * 128, None, Alu.bitwise_and, None, ["pi2"], 1)
    vcp("pf", T.pf[:, 0:4], T.pj[:, 0:4], ["pj0", "pj1", "pj2"], 4)
    line("pf4", T.pf[:, 4:5], T.pf[:, 0:1], 1.0, 16.0, ["pf"], 1)
    for j, (a, b, z, base, pat) in enumerate([(0, 16, 2, 0, [[1, 2], [32, 4]]), (1, 16, 2, 128, [[1, 2], [32, 4]]), (17, 32, 2, 16, [[1, 2], [32, 4]]),
                                              (16, 32, 2, 112, [[1, 2], [32, 4]]), (16, 32, 8, 240, [[1, 2]])]):
        op("tb%d" % j, "g", lambda q, a=a, b=b, z=z, base=base, pat=pat: [q.iota(T.pg[:, a:b:z], pat, base, 0, allow_small_or_imprecise_dtypes=True)],
           [], ["tb"], 150.0)
    for k in range(4):
        ga("n32_%d" % k, T.n32[:], T.n32[:] if k else T.zer[:, 0:32], ["n32" if k else "zer"], [[-1, 32]], Alu.not_equal, -1.0, -32 * k, 1, 32, "n32")
    vtt("pm", T.pg[:, 32:64], T.pg[:, 0:32], T.n32[:], Alu.mult, ["tb", "n32"], 32)
    op("pn", "v", lambda q: [q.tensor_reduce(T.pf[:, 6:7], T.pg[:, 32:64], Ax.X, Alu.add, negate=True)], ["pm"], ["pn"], cv(32))
    vts("lt", T.lt[:], T.lf[:, 0:8], 2.0, T.pf[:, 6:7], Alu.mult, Alu.add, ["lf0", "pn"], 8)
    gi("kio", T.kio[:], [[16, 2], [0, 8], [1, 16]], 0, 0, 256)
    vts("mR", T.mR[:], blk(T.kio, 0), T.pf[:, 0:1], None, Alu.is_equal, None, ["kio", "pf"], 128)
    vts("TM", T.TM[:], T.kio[:], T.pf[:, 2:3], 4096.0, Alu.is_le, Alu.mult, ["kio", "pf"], 256)
    line("posm", T.posm[:], T.mR[:], -4096.0, 4096.0, ["mR"], 128)
    for k in range(2):
        ga("sel%d" % (3 + k), blk(T.sel34, k), T.zer[:], ["zer"], [[-16, 8], [0, 16]], Alu.not_equal, 1.0, -3 - k, 1, 128)
    ga("QB", T.QB[:], T.QA[:], ["QA"], [[0, 2], [-32, 4], [0, 2]], Alu.is_ge, 0.0, 0, 1, 16)
    ga("QA", T.QA[:], T.QB[:], ["QB"], [[0, 2], [32, 4], [0, 2]], Alu.is_ge, 0.0, 31, -1, 16)
    ga("QE", T.QE[:], T.QA[:], ["QA"], [[1, 2], [0, 4], [-1, 2]], Alu.is_equal, 0.0, 0, 0, 16)
    for k in range(3):
        ga("rst%d" % k, blk(T.rst, k), T.zer[:], ["zer"], [[0, 8], [1, 16]], Alu.not_equal, BIG, 0, 0, 128)
    ga("Dm", T.Dm[:], T.zer[:], ["zer"], [[-1, 128]], Alu.not_equal, -1.0, -1, 1, 128)
    ga("DmA", T.DmA[:], T.Dm[:], ["Dm"], [[0, 8], [-1, 16]], Alu.is_gt, 0.0, 15, 0, 128)
    ga("Dm", T.Dm[:], T.DmA[:], ["DmA"], [[-1, 128]], Alu.not_equal, 1.0, 0, 1, 128)
    gi("nm0", blk(T.U2, 1), [[1, 128]], F, 0, 128)
    op("U2", "vs", lambda q, e: [q.tensor_scalar(blk(T.U2, 0), blk(T.U2, 1), T.pf[:, 3:4], None, Alu.add) if e == "v" else
                                 q.activation(blk(T.U2, 0), blk(T.U2, 1), Act.Identity, bias=T.pf[:, 3:4])], ["nm0", "pf"], ["U2"], cv(128))
    vset("BMa", T.BM[:, 0:256], 0.0, 256)
    gi("BMb", T.BM[:, 256:896], [[0, 640]], 0, 0, 640)
    for k, ms, sem in (("BMa", (0, 1), "bz"), ("BMb", range(2, 7), "bm")):
        dma(sem, "y", [(T.BM[m::16, m * 128:(m + 1) * 128], T.U2[m::16, 0:128]) for m in ms], ["U2"], [k], sem)
    sact("lnc", T.hl[:, 1:3], T.lf[:, 1:3], Act.Ln, ["lf0"], 2, scale=1.0 / 32, cost=1400.0)
    sact("lnh", T.lnh[:, 0:16], T.hvb[:], Act.Ln, ["hvb", "lnc"], 16, scale=1.0 / 16)
    if SCAN:
        sact("hl", T.hl[:, 0:1], T.lnh[:, 15:16], Act.Exp, ["lnh"], 1, cost=1600.0)
        op("hrec", "v", lambda q: [q.reciprocal(T.hrec[:], T.hvb[:])], ["hvb"], ["hrec"], 300.0)
        gi("r160", T.RT[:, 0:1], [[0, 1]], 0, 0, 1)
        vtt("RT", T.RT[:, 1:16], T.hvb[:, 0:15], T.hrec[:, 1:16], Alu.mult, ["hvb", "hrec"], 16)
        for w in (16, 32, 64, 128, 256, 512):
            dma("RT%d" % w, "y", [(T.RT[:, w:2 * w], T.RT[:, 0:w])], ["RT", "r160"], ["RT"], "rt")
        gi("Sel", T.Sel[:], [[0, 512]], 0, 0, 512)
        for k in range(4):
            ga("Sel%d" % k, T.Sel[:], T.Sel[:], ["Sel"], [[-1, 32], [0, 16]], Alu.not_equal, -1.0, -32 * k, 1, 512, "Sel")
    if any(k in SETS for k in RELU):
        vts("lnr", T.lnh[:, 16:32], T.lnh[:, 0:16], -8.0, None, Alu.add, None, ["lnh"], 16)

    def pk(n):
        return ["P0"] + ["Pc%d" % k for k in range(n)]

    def uk(n):
        return ["U0"] + ["Uc%d" % k for k in range(n)]

    def uwin(t, top):
        return t[:, SP:SP + F + 128 * top]

    def ublk(m):
        return T.Ut[:, SP + F + 128 * m:SP + F + 128 * m + 128]

    def cfb(l):
        return T.cf[:, 144 * l:144 * l + 128]

    def column(name, out, c, win, rd, wr=None):
        if name in CONV:
            vcp(name, out, blk(T.cu, c), ["cu%d" % c], 128, wr=wr)
        else:
            both(name, out, win, rd, cg(128), wr=wr)

    vcp("stu", T.stu[:, 0:24], T.sti[:], ["sti"], 24)
    dma("stj", "y", [(T.stj[:, 10 * l + a:10 * l + a + n], T.st[:, 8 * l + 8:8 * l + 8 + n]) for l in (0, 1) for a, n in ((0, 8), (8, 2))], ["sti"], ["stj"], "ld5")
    vcp("stv", T.stu[:, 24:44], T.stj[:], ["stj"], 20)
    vcp("cu7", blk(T.cu, 7), T.sui[:].indirect(T.stu[:, 0:8]), ["sui", "stu"], 128, cost=cg(128))
    if UG:
        ga("U0", uwin(T.Ut, 0), T.sui[:], ["sui"], [[0, F]], Alu.is_equal, 0.0, 0, 0, F)
    else:
        both("U0", uwin(T.Ut, 0), T.sui[:], ["sui"], cv(F))
    both("cf0", cfb(0), T.sui[:].indirect(T.stu[:, 0:8]), ["sui", "stu"], cg(128))
    for l in (1, 2):
        both("cf%d" % l, blk(T.cf, l, 144), T.sui[:].indirect(T.stu[:, 14 + 10 * l:23 + 10 * l]), ["sui", "stv"], cg(144))
    both("X16", T.X16[:], T.xsi[:], ["xsi"], cv(512), plus=-2048.0)
    for z, m in enumerate((2, 5, 6)):
        h = "Xm%d" % z
        op(h, "p", lambda q, h=h, m=m: [q.matmul(ps(h, 0, 128), ident((0, 1, 4)[LEV[m]]), blk(T.X16, t), t == TIMES[m][0], t == TIMES[m][-1]) for t in TIMES[m]],
           ["X16", "I1", "I4"], [h], cp(128 * len(TIMES[m]), len(TIMES[m])), acq=(h, 1))
        both("Xe%d" % z, blk(T.XR, 4 * z), None, [h], cv(128), plus=2048.0, rel=h)
        dma("XR%d" % z, "y", [(blk(T.XR, 4 * z + j), blk(T.XR, 4 * z)) for j in (1, 2, 3)], ["Xe%d" % z], ["XR%d" % z], "xr%d" % z)

    def symbols(m):
        return [blk(T.X16, t) for t in TIMES[m]], "X16"
    for l in range(3):
        a = 7 + l
        vtt("M1%d" % l, blk(T.M1, l), T.sti[:, 8 * l:8 * l + 8].indirect(T.lu[:, 0:8]), T.mR[:], Alu.mult, ["sti", "lu", "mR"], 128, cost=cg(128))
        op("Ap%d" % a, "p", lambda q, l=l, a=a: [q.matmul(ps("a%d" % a, 0, 128), blk(T.M1, l), ident(0), True, True)],
           ["M1%d" % l, "I0"], ["Ap%d" % a], cp(128, 1), acq=("a%d" % a, 1))
        both("A1%d" % a, blk(T.A1, a), None, ["Ap%d" % a], cv(128), rel="a%d" % a)

    def gkeys(k, a=0, b=2048):
        return ["G%d_%d" % (k, x) for x in range(a // 512, b // 512)]

    def akeys(u, a=0, b=16):
        return ["A%s_%d" % (u, x) for x in range(a, b)]

    def slab(u, a, b=None):
        k, j = setof[u]
        if k in APART:
            return T["A" + k][:, j, 128 * a:128 * (b or a + 1)]
        return T["A" + k][:, a, j, :] if b is None else T["A" + k][:, a:b, j, :]

    def slot(k, i):
        return T["A" + k][:, :, 128 * i:128 * i + 128] if k in APART else T["A" + k][:, i, :, :]

    def slots(u):
        return ORDER01 if u in ("R0", "R1") else list(range(16))

    def turned(c, cf, cfk):
        z = c % 2
        for e in range(2):
            op("tt%d_%d" % (c, e), "v", lambda q, e=e: [q.transpose(blk(T.TT, 2 * z + e), cf[:, 16 * e:16 * e + 128])], [cfk], ["TT%d_%d" % (z, e)], cv(128))
        vcp("cu%d" % c, blk(T.cu, c), blk(T.TT, z, 256).indirect(T.lt[:]), ["TT%d_0" % z, "TT%d_1" % z, "lt"], 0, cost=cg(128))

    def direct(u, cand, ck, top, z):
        for a in range(0, 16, 4):
            vtt("g%s_%d" % (u, a), slab(u, a, a + 4), T.Pt[:, 0:F + 128 * top].indirect(cand[:, 8 * a:8 * a + 32]), blk(T.XR, z, 512) if z < 3 else T.XQ[:], Alu.subtract,
                pk(top) + [ck, "XR%d" % z], 0, wr=akeys(u, a, a + 4), cost=cg(512) + 512 * C["tti"] * C["cyc"])
        part[0] = u
        for a in (0, 8):
            sact("abs%s_%d" % (u, a), slab(u, a, a + 8), slab(u, a, a + 8), Act.Abs, akeys(u, a, a + 8), 1024, wr=akeys(u, a, a + 8))

    def gather(u, cand, ck, top):
        G = T["G%d" % GOF[u]]
        w = 512 if u in QUART else 1024
        for a in range(0, 2048, w):
            both("g%s_%d" % (u, a), G[:, a:a + w], T.Pt[:, 0:F + 128 * top].indirect(cand[:, a // 16:(a + w) // 16]), pk(top) + [ck],
                 cg(w), plus=-2048.0, wr=gkeys(GOF[u], a, a + w))

    def dist(u, lev, xts, xk):
        G = T["G%d" % GOF[u]]
        w = 4 if u in FINE else 8
        a0 = 0 if u in SCAN else RELU.get(setof[u][0], 0)
        end = 14 if u in ("R0", "R1") else 16
        for a, b in [(a, min(a + w, end)) for a in range(a0, end, w)]:
            h = "d%s_%d" % (u, a)
            n = 128 * (b - a)

            def mm(q, c0, c1, a=a, b=b, h=h):
                r = []
                if u in SCAN:
                    for c in range(c0, c1, 4):
                        o = ps(h, 128 * (c - a), 128 * (c - a) + 512)
                        r.append(q.matmul(o, ident(lev), G[:, 128 * c:128 * c + 512], True, False))
                        r.append(q.matmul(o, xts[0][8 * c:8 * c + 32, :], T.Sel[8 * c:8 * c + 32, :], False, a >= RELU.get(u, 0)))
                    return r
                for c in range(c0, c1):
                    o = ps(h, 128 * (c - a), 128 * (c - a) + 128)
                    if u not in EARLY:
                        for j, x in enumerate(xts):
                            r.append(q.matmul(o, ident(7), x, j == 0, False))
                    r.append(q.matmul(o, ident(lev), G[:, slots(u)[c]::16], False, u not in EARLY or c + 1 == b))
                return r
            if u in EARLY:
                op(h + "x", "p", lambda q, h=h: [q.matmul(ps(h, c, c + 128), ident(7), xts[0], c == 0, False) for c in range(0, 512, 128)],
                   [xk, "I7"], [h], cp(512, 4), acq=(h, 1))
                op(h, "p", lambda q, a=a, b=b, mm=mm: mm(q, a, b), gkeys(GOF[u]) + [h, "I%d" % lev], [h], cp(512, 4))
            elif u in SCAN:
                for c in range(a, b, 4):
                    op("%s_%d" % (h, c), "p", lambda q, c=c, mm=mm: mm(q, c, c + 4), gkeys(GOF[u], 128 * a, 128 * b) + ["Sel", xk, "I%d" % lev],
                       [h], cp(1024, 2), acq=(h, w // 4) if c == a else None)
            else:
                z = 4 if len(xts) == 1 else 2
                for c in range(a, b, z):
                    e = min(c + z, b)
                    op("%s_%d" % (h, c), "p", lambda q, c=c, e=e, mm=mm: mm(q, c, e), gkeys(GOF[u]) + ["I7", xk, "I%d" % lev], [h],
                       cp(128 * (e - c) * (1 + len(xts)), (e - c) * (1 + len(xts))), acq=(h, (b - a + 3) // 4) if c == a else None)
            out = T["A" + u][:, 128 * a:128 * b] if u in SCAN else slab(u, a, b)
            if u in SCAN and a < RELU.get(u, 0):
                positive(h)
                op("exp" + h, "s", lambda q, out=out, h=h: [q.activation(out, ps(h, 0, 1024), Act.Exp, scale=1.0 / 512, bias=-8.0)], [h, "hl"],
                   akeys(u, a, b), cv(n), rel=h)
            else:
                op("abs" + h, "s", lambda q, out=out, n=n, h=h: [q.activation(out, ps(h, 0, n), Act.Abs)], [h], akeys(u, a, b), cv(n), rel=h)

    turn = [0]

    def positive(h):
        z = turn[0] % 2
        turn[0] += 1
        r = blk(T.pos, z, 1024)
        op("pos" + h, "v", lambda q: [q.tensor_scalar(r, ps(h, 0, 1024), 0.0, -2048.0, Alu.max, Alu.add)], [h], ["pos%d" % z], cv(1024))
        op(h + "r", "p", lambda q: [q.matmul(ps(h, c, c + 512), ident(2), r[:, c:c + 512], False, True) for c in (0, 512)],
           ["pos%d" % z, "I2", h], [h, h + "r"], cp(1024, 2))

    def joint(k, xs):
        A, us = T["A" + k], SETS[k]
        for a in range(0, RELU.get(k, 0), 4):
            h = "j%s_%d" % (k, a)
            for c in (a, a + 2):
                def mm(q, c=c, a=a, h=h):
                    r = []
                    for i in (c, c + 1):
                        for j, u in enumerate(us):
                            o = ps(h, 256 * (i - a) + 128 * j, 256 * (i - a) + 128 * j + 128)
                            r.append(q.matmul(o, ident(7), xs[u][0], i == c and j == 0, False))
                            r.append(q.matmul(o, ident(0), T["G%d" % GOF[u]][:, slots(u)[i]::16], False, False))
                    return r
                op("%s_%d" % (h, c), "p", mm, [x for u in us for x in gkeys(GOF[u]) + [xs[u][1]]] + ["I0", "I7"], [h], cp(1024, 8),
                   acq=(h, 2) if c == a else None)
            positive(h)
            op("exp" + h, "s", lambda q, a=a, h=h: [q.activation(A[:, i, :, :], ps(h, 256 * (i - a), 256 * (i - a) + 256), Act.Exp, scale=1.0 / 512,
                                                                 bias=T.lnh[:, 16 + slots(us[0])[i]:17 + slots(us[0])[i]]) for i in range(a, a + 4)],
               [h, "lnr"] + WARM, [x for u in us for x in akeys(u, a, a + 4)], 4 * cv(256), rel=h)

    MX, MK = {}, {}

    def store(name, dst, src, rd, k):
        dma("st" + name, "s" if name == "yz6" else "y", [(dst, src)], rd, [], "t%d" % k)

    def expo(u, lev):
        w = 16 if u in WHOLE else 4 if u in LAST else 8
        for a in range(RELU.get(u, 0), 16, w):
            o = T["A" + u][:, 128 * a:128 * (a + w)] if u in SCAN else slab(u, a, a + w)
            sact("exp%s_%d" % (u, a), o, o, Act.Exp, akeys(u, a, a + w) + WARM, 128 * w, wr=akeys(u, a, a + w), scale=-1.0 / 512,
                 bias=0.0 if u in SCAN else T.hl[:, 1:2] if lev else T.hl[:, 2:3])

    def weigh(k, a, b):
        A, us = T["A" + k], SETS[k]
        keys = [x for u in us for x in akeys(u, a, b)]
        op("exp%s_%d" % (k, a), "s", lambda q: [q.activation(slot(k, i), slot(k, i), Act.Exp, scale=-1.0 / 512,
                                                             bias=T.lnh[:, slots(us[0])[i]:slots(us[0])[i] + 1]) for i in range(a, b)],
           keys + ["lnh"] + WARM, keys, (b - a) * cv(128 * len(us)))

    def total(k, steps):
        A, us = T["A" + k], SETS[k]
        if k not in FOLD:
            for j, (to, fr, n) in enumerate(steps):
                add("add%s_%d" % (k, j), A[:, to:to + n, :, :], A[:, fr:fr + n, :, :], [x for u in us for x in akeys(u, fr, fr + n)],
                    [x for u in us for x in akeys(u, to, to + n)] + ["sem" + k], "a" + k, n * len(us) * 65536)
            return
        hs = helpers(T, topo, core)
        j = FOLD.index(k) % len(hs)
        n, z = PART.get(k, 16), WIDE.get(k, 1)
        keys = [x for u in us for x in akeys(u, 0, n)]

        def fold(q):
            rid, pid = topo.addr(hs[j], core)
            e = topo.engines(core, hs[j])
            prs = ([([slab(u, i, i + z) for i in range(0, n, z)], blk(result(T, k), x, 128 * z)) for x, u in enumerate(us)] if k in APART else
                   [([slot(k, i) for i in range(n)], result(T, k))])
            w = len(e) // len(prs)
            q.remote_dma_fused([RemoteDMATransfer(dst_ids=[DstId(rid=rid, pnc=pid)], dma_engine_mask=sum(1 << y for y in e[x * w:(x + 1) * w]),
                                                  remote_sem=T.sem["f" + k], srcs=a, dsts=[b], alu_op=1) for x, (a, b) in enumerate(prs)],
                               local_sem=T.sem.sent)
            return len(e)
        op("fold" + k, "g", fold, keys, ["fold" + k, "help%d" % j], C["call"], kind="r", lat=C["dma"] / 2)
        op("fold" + k + "d", "D", len(ops) - 1, keys + ["fold" + k], ["fold" + k, "help%d" % j],
           8 * n // z * (len(us) if k in APART else 1) * C["row"] + n * len(us) * 65536 / C["fw"], kind="e", lat=C["dma"] / 2)
        op("back" + k, "h%d" % j, len(topo.engines(hs[j], core)), ["fold" + k], ["res" + k], C["back"] + 110.0 * z * len(us), kind="w", sem="b" + k)

    def summed(u):
        k, j = setof[u]
        if k in FOLD:
            z = WIDE.get(k, 1)
            return [blk(result(T, k), z * j + i) for i in range(z)], ["res" + k]
        left = max(1, 16 >> HALVE[k])
        return [slab(u, i) for i in range(left)], akeys(u, 0, left)

    def rest(k, m, w):
        h, n = "sum" + k, PART[k]
        z = 512 // w
        for a in range(n, 16, z):
            op("%s_%d" % (h, a), "p", lambda q, a=a: [q.matmul(ps(h, 0, w), T.idf[:], slot(k, i), i == n, i == 15 and not n)
                                                      for i in range(a, a + z)],
               [x for u in SETS[k] for x in akeys(u, a, a + z)] + ["idf"], [h], cp(2048, z), acq=(h, 1) if a == n else None)
        if n:
            xs = [(128 * j, x) for j, u in enumerate(SETS[k]) for x in summed(u)[0]]
            op(h + "f", "p", lambda q: [q.matmul(ps(h, a, a + 128), T.idf[:], x, False, j + 1 == len(xs)) for j, (a, x) in enumerate(xs)],
               ["res" + k, "idf"], [h], cp(512 * len(xs), len(xs)))
        out = result(T, k)[:, 0:w]
        both("yz%d" % m, out, w, [h], cv(w), rel=h, wr=["res" + k])
        store("yz%d" % m, T.yz[:, 128 * m:128 * m + w], out, ["res" + k], 7 + m)

    def mixture(m):
        u = "E%d" % m
        lev = LEV[m]
        xs, keys = summed(u)
        if len(xs) == 1 and not lev:
            MX[m], MK[m] = xs[0], keys
        else:
            MX[m], MK[m] = (xs[0], list(keys)) if m < 4 else (blk(T.ymb, m - 4), ["ym%d" % m])
            h = "sum" + u
            prs = [(T.idf[:], x) for x in xs]
            if lev:
                prs.append((T.idh[:], blk(T.prod, (2, 5, 6).index(m))))
                keys = keys + ["prod%d" % m, "idh"]
            op(h, "p", lambda q: [q.matmul(ps(h, 0, 128), a, b, i == 0, i == len(prs) - 1) for i, (a, b) in enumerate(prs)],
               keys + ["idf"], [h], cp(len(prs) * 512, len(prs)), acq=(h, 1))
            if m in (1, 4, 5):
                x, y = {1: (0, 2), 4: (3, 5), 5: (2, 6)}[m]
                op("prod%d" % y, "v", lambda q: [q.tensor_tensor(blk(T.prod, (2, 5, 6).index(y)), ps(h, 0, 128), MX[x], Alu.mult)], [h] + MK[x],
                   ["prod%d" % y, h], cv(128), rel=h)
            both("ym%d" % m, MX[m], None, [h], cv(128), rel=h, wr=MK[m])
        if m < 4:
            store("ym%d" % m, blk(T.ym, m), MX[m], MK[m], m)
        elif m == 6:
            store("ym4", T.ym[:, 512:896], T.ymb[:], ["ym4", "ym5", "ym6"], m)

    def scan(u, m):
        out = blk(T.yzb, m - 4)
        w = 4 if u in LAST else 8
        for a in range(0, 16, w):
            op("scan%s_%d" % (u, a), "v", lambda q, a=a: [q.tensor_tensor_scan(T.SC[:, 128 * a:128 * (a + w)], T.RT[:, 0:128 * w],
                                                                               T["A" + u][:, 128 * a:128 * (a + w)], 0.0, Alu.mult, Alu.add)],
               akeys(u, a, a + w) + ["RT"], ["SC%d" % x for x in range(a, a + w, 4)], cv(128 * w))
        op("yz%d" % m, "vs", lambda q, e: [q.tensor_scalar(out, T.SC[:, 15::16], T.hl[:, 0:1], None, Alu.mult) if e == "v" else
                                           q.activation(out, T.SC[:, 15::16], Act.Copy, scale=T.hl[:, 0:1])], ["SC0", "SC4", "SC8", "SC12", "hl"], ["yz%d" % m], cv(128))
        store("yz%d" % m, blk(T.yz, m), out, ["yz%d" % m], 7 + m)

    def elect(m, cf, cfk):
        u = "E%d" % m
        h = "k%d" % m
        op(h + "n", "p", lambda q: [q.matmul(ps(h, 128, 256), cf, T.Dm[:], True, True),
                                    q.matmul(ps(h, 0, 128), T.one16[0:1, :], T.kio[0:1, 0:128], True, False)],
           [cfk, "Dm", "one16", "kio"], [h], cp(640, 2), acq=(h, 1))
        for j in range(4):
            op("%s_%d" % (h, j), "p", lambda q, j=j: [q.matmul(ps(h, i, 128, 16), slab(u, i), blk(T.BO, LEV[m], 8), False, i == 15) for i in range(4 * j, 4 * j + 4)],
               akeys(u, 4 * j, 4 * j + 4) + ["BQ%d" % LEV[m], h], [h], cp(4 * 256, 4))
        z = ROT[m]
        rm, kp, val = blk(T.rm, z), blk(T.kp, z), blk(T.val, z)
        rk, kk, vk = "rm_%d" % z, "kp_%d" % z, "val_%d" % z
        op("rm%d" % m, "v", lambda q: [q.tensor_tensor_scan(rm, blk(T.rst, 0), ps(h, 0, 128), 0.0, Alu.add, Alu.min)], [h, "rst0"], [rk], cv(128))
        op("kp%d" % m, "v", lambda q: [q.tensor_tensor(kp, ps(h, 0, 128), rm, Alu.is_gt)], [h, rk], [kk], cv(128))
        op("val%d" % m, "v", lambda q: [q.tensor_tensor_scan(val, kp, ps(h, 128, 256), 0.0, Alu.mult, Alu.add)], [h, kk], [vk], cv(128))
        a1 = blk(T.A1, m)
        vtt("A1%d" % m, a1, val.indirect(T.lu[:, 32:40]), T.mR[:], Alu.mult, [vk, "lu", "mR"], 0, cost=cg(128))
        op("L%d" % m, "p", lambda q: [q.matmul(ps(h, 256, 264), a1, T.G8[:], True, True)] +
           ([q.matmul(ps(h, 264, 265), a1, T.G8[:, 0:1], True, True)] if m == 2 else []), ["A1%d" % m, "G8"], ["L%d" % m], cp(64, 1))
        n = 9 if m == 2 else 8
        op("bl%d" % m, "v", lambda q: [q.tensor_copy(T.bl[:, 10 * m:10 * m + n], ps(h, 256, 256 + n))], ["L%d" % m], ["bl%d" % m], cv(8), rel=h)
        if m < 4:
            both("A2%d" % m, blk(T.A2, m), val.indirect(T.lu[:, 32:40]), [vk, "lu"], cg(128))

    def extend(m, a, lst, lk, top, old, oldk):
        h = "x%d" % m
        a1 = blk(T.A1, a)
        own = (blk(T.M1, a - 7), T.nBB[:], ["M1%d" % (a - 7), "nBB"]) if a >= 7 else (ident(7), blk(T.A2, a), ["I7", "A2%d" % a])
        z = (0, 1, 2, 0, 1, 2, 0)[m]
        eq, ek = blk(T.eq, z, 256), "eq_%d" % z

        def mm(q):
            r = []
            for e in range(2):
                r.append(q.matmul(ps(h, 128 * e, 128 * e + 128), own[0], own[1], True, False))
                r.append(q.matmul(ps(h, 128 * e, 128 * e + 128), blk(T.BN, e), a1, False, True))
            return r
        op(h, "p", mm, ["A1%d" % a, "BN0", "BN1"] + own[2], [h], cp(512, 4), acq=(h, 1))
        op("eq%d" % m, "v", lambda q: [q.tensor_tensor(eq, ps(h, 0, 256), T.TM[:], Alu.is_equal)], [h, "TM"], [ek], cv(256))
        op(h + "c", "p", lambda q: [q.matmul(ps(h, 256, 264), a1, T.G8[:], True, False)] +
           [q.matmul(ps(h, 256, 264), blk(eq, e), blk(T.QE, e, 8), False, e == 1) for e in range(2)], [ek, "QE", "G8", "A1%d" % a], [h + "c"], cp(192, 3))
        op("off%d" % m, "v", lambda q: [q.tensor_scalar(T.offu[:, 8 * m + e:8 * m + 8:2], ps(h, 256 + e, 264, 2), float(SP), T.pf[:, 4 * e:4 * e + 1], Alu.add, Alu.max)
                                        for e in range(2)], [h + "c", "pf", "pf4"], ["off%d" % m], 2 * cv(4), rel=h)
        U, keys = (T.Ut, uk(top)) if m < 5 else (T.U2, ["U2"])
        if old is None:
            old, oldk = blk(T.old, m % 2), "old_%d" % (m % 2)
            column("old%d" % m, old, None, uwin(U, top).indirect(lst), keys + [lk], wr=[oldk])
        for k in (3, 2, 1, 0):
            vtt("ext%d_%d" % (m, k), U[:, 0:SP + F + 128 * top].indirect(T.offu[:, 8 * m + 2 * k:8 * m + 2 * k + 2]), blk(old, k, 32),
                T.BM[:, 128 * m + 32 * k:128 * m + 32 * k + 32], Alu.max, ["off%d" % m, oldk, "BMa" if m < 2 else "BMb"], 0, wr=keys + ["spare"],
                cost=C["fix"] + 32 * C["sca"] * C["cyc"])
        if m == 4:
            dma("U4", "y", [(uwin(T.U2, 3), uwin(T.Ut, 3))], uk(3), ["U2"], "cpu", 640000)
        if m == 1:
            dma("U1", "y", [(uwin(T.U2, 1), uwin(T.Ut, 1))], uk(1), ["U2"], "cpv", 510000)

    def snap(m):
        lev, top = LEV[m], TOP[m]
        h = "s%d" % m
        bl, pb = T.bl[:, 10 * m:10 * m + 8], blk(T.Pb, m)
        rem = {2: 0, 5: 1, 6: 2}.get(m)
        both("Pb%d" % m, pb, T.Pt[:, 0:F + 128 * top].indirect(bl), pk(top) + ["bl%d" % m], cg(128), plus=-2048.0)
        xts, xk = symbols(m)

        def mm(q, tr):
            o = ps(h, 128 * tr, 128 * tr + 128)
            prs = [(T.one16[0:1, :], T.cm16[0:1, :])] + [(ident(4 + lev), x) for x in xts] + [(ident(3), pb)]
            return [q.matmul(o, p[tr], p[1 - tr], j == 0, j == len(prs) - 1) for j, p in enumerate(prs)]
        tr = 1 if "R%d" % m in SCAN else 0
        n = (1 + tr) * (2 + len(xts))
        op(h, "p", lambda q: mm(q, 0) + (mm(q, 1) if tr else []), ["Pb%d" % m, xk, "one16", "cm16", "I3", "I%d" % (4 + lev)], [h],
           cp(128 * n, n), acq=(h, 1))
        new = T.Pt[:, F + 128 * m:F + 128 * m + 128] if rem is None else blk(T.snew, rem)
        nk = "Pc%d" % m if rem is None else "snew%d" % m
        op("new%d" % m, "v", lambda q: [q.tensor_scalar(new, ps(h, 0, 128), MAG, 2048.0 - MAG, Alu.add, Alu.add)], [h], [nk], cv(128), rel=h)
        if tr:
            op("nxt%d" % m, "v", lambda q: [q.tensor_scalar(blk(T.nxt, m), ps(h, 128, 256), MAG, -MAG, Alu.add, Alu.add)], [h],
               ["nxt%d" % m], cv(128), rel=h)
        elif m != 2:
            both("nxt%d" % m, blk(T.nxt, m), new, [nk], cv(128), plus=-2048.0)
        copy = m in (1, 5, 6)
        win, rd = uwin(T.U2 if copy else T.Ut, top).indirect(bl), (["U2"] if copy else uk(top)) + ["bl%d" % m]
        if m == 2:
            both("cf3", blk(T.cf, 3, 144), uwin(T.Ut, top).indirect(T.bl[:, 20:29]), rd, cg(144))
            turned(2, blk(T.cf, 3, 144), "cf3")
        else:
            vcp("cu%d" % m, blk(T.cu, m), win, rd, 0, cost=cg(128))
        if m in (0, 1, 3):
            column("Uc%d" % m, ublk(m), m, win, rd)
        if rem is None:
            return
        n = len(T.cores)
        r = T.rank_of(core)
        dst, src = T.cores[(r + lev) % n], T.cores[(r - lev) % n]
        wide = [(new, T.Pt[:, F + 128 * m:F + 128 * m + 128])] + ([(cfb(3), ublk(2))] if m == 2 else [])
        prs = [(blk(a, j, 64), blk(b, j, 64)) for a, b in wide for j in range(2)] + [(blk(T.cu, m), blk(T.rcu, rem))]
        if m != 2:
            prs.append((blk(T.nxt, m), blk(T.rxt, rem)))

        def share(k):
            w = 1
            while 2 * w * len(prs) <= k:
                w *= 2
            return w

        def send(q):
            rid, pid = topo.addr(dst, core)
            e = topo.engines(core, dst)
            w = share(len(e))
            q.remote_dma_fused([RemoteDMATransfer(dst_ids=[DstId(rid=rid, pnc=pid)], dma_engine_mask=sum(1 << x for x in e[j * w:(j + 1) * w]),
                                                  remote_sem=T.sem["arr%d" % m], src=a, dst=b) for j, (a, b) in enumerate(prs)],
                               local_sem=T.sem.sent)
            return w * len(prs)
        op("send%d" % m, "g", send, ["snew%d" % m, "cu%d" % m, "cf3" if m == 2 else "nxt%d" % m], ["sent%d" % m], 1000.0, kind="r")
        op("recv%d" % m, "n%d" % m, share(len(topo.engines(src, core))) * len(prs), ["sent%d" % m],
           ["Pc%d" % m, "rc%d" % m] + (["Uc2"] if m == 2 else []), C["rem"], kind="w", sem="arr%d" % m)

    def late():
        h = "fx"
        rows = [(3, 0), (4, 0), (4, 1)]

        def mm(q):
            r = []
            for j, (slot, c) in enumerate(rows):
                r.append(q.matmul(ps(h, 128 * j, 128 * j + 128), ident(0), T.posm[:], True, False))
                r.append(q.matmul(ps(h, 128 * j, 128 * j + 128), blk(T.sel34, slot - 3), ublk(c), False, True))
            return r
        op(h, "p", mm, ["I0", "posm", "sel3", "sel4", "Uc0", "Uc1"], [h], cp(3 * 640, 6), acq=(h, 1))
        op("fxs", "v", lambda q: [q.tensor_tensor_scan(T.TT[:, 0:384], T.rst[:], ps(h, 0, 384), 0.0, Alu.add, Alu.min)],
           [h, "rst0", "rst1", "rst2"], ["TT0_0", "TT0_1", "TT1_0"], cv(384), rel=h)
        vcp("fxu", T.fxu[:], T.TT[:, 15:384:16], ["TT0_0", "TT0_1", "TT1_0"], 24)
        both("GX", T.GX[:], T.Pt[:, 0:F + 128 * 5].indirect(T.fxu[:]), pk(5) + ["fxu"], cg(384), plus=-2048.0)
        h2 = "dl"
        src = [(blk(T.GX, 0), 0), (T["G%d" % GOF["R1"]][:, 3::16], 1), (blk(T.GX, 1), 0), (blk(T.GX, 2), 1)]

        def mm2(q):
            r = []
            for j, (x, c) in enumerate(src):
                r.append(q.matmul(ps(h2, 128 * j, 128 * j + 128), ident(7), blk(T.nxt, c), True, False))
                r.append(q.matmul(ps(h2, 128 * j, 128 * j + 128), ident(0), x, False, True))
            return r
        op(h2, "p", mm2, ["GX", "I0", "I7", "nxt0", "nxt1"] + gkeys(GOF["R1"]), [h2], cp(1024, 8), acq=(h2, 1))
        op("abs" + h2, "s", lambda q: [q.activation(T.AR01[:, 14:16, :, :], ps(h2, 0, 512), Act.Abs)], [h2],
           akeys("R0", 14, 16) + akeys("R1", 14, 16), cv(512), rel=h2)

    cand = {0: (7, cfb(0), "cf0"), 1: (0, ublk(0), "Uc0"), 2: (8, cfb(1), "cf1"), 3: (1, ublk(1), "Uc1"),
            4: (3, ublk(3), "Uc3"), 5: (2, cfb(3), "cf3"), 6: (9, cfb(2), "cf2")}
    opn = {0: (7, None, None, 0, cfb(0), "cf0"), 1: (0, None, None, 0, ublk(0), "Uc0"),
           2: (8, T.stu[:, 8:16], "stu", 0, None, None), 3: (1, T.bl[:, 10:18], "bl1", 1, None, None),
           4: (3, None, None, 2, ublk(3), "Uc3"), 5: (2, T.bl[:, 20:28], "bl2", 0, None, None),
           6: (9, T.stu[:, 16:24], "stu", 0, None, None)}
    for m in range(7):
        u = "E%d" % m
        c, cf, cfk = cand[m]
        part[0] = "g" + u
        if LEV[m]:
            if c > 7:
                turned(c, blk(T.cf, c - 7, 144), cfk)
            direct(u, blk(T.cu, c), "cu%d" % c, TOP[m], (2, 5, 6).index(m))
        else:
            gather(u, blk(T.cu, c), "cu%d" % c, TOP[m])
            part[0] = u
            dist(u, 0, *symbols(m))
        elect(m, cf, cfk)
        part[0] = "X%d" % m
        extend(m, *opn[m])
        part[0] = "S%d" % m
        snap(m)
        part[0] = "M%d" % m
        expo(u, LEV[m])
    halves = [(0, 8, 8), (0, 4, 4), (0, 2, 2), (0, 1, 1)]
    own = {}
    for m in (2, 3, 0, 1, 4, 5, 6):
        u = "R%d" % m
        rem = {2: 0, 5: 1, 6: 2}.get(m)
        part[0] = "g" + u
        if m == 2:
            dma("XR3", "y", [(blk(T.XQ, j), T.Pt[:, F + 256:F + 384]) for j in range(4)], ["Pc2"], ["XR3"], "xr3")
            direct(u, blk(T.rcu, 0), "rc2", 3, 3)
            continue
        if rem is not None:
            gather(u, blk(T.rcu, rem), "rc%d" % m, m + 1)
        elif m == 4:
            gather(u, blk(T.cu, 4), "cu4", 5)
        part[0] = u
        own[u] = (blk(T.nxt, m), "nxt%d" % m) if rem is None else (blk(T.rxt, rem), "rc%d" % m)
        dist(u, 0, [own[u][0]], own[u][1])
        if u in SCAN:
            expo(u, 0)
            scan(u, m)
    for k in FOLD + [k for k in SETS if k not in FOLD]:
        part[0] = "H" + k
        if k[0] == "R":
            joint(k, own)
            end = 14 if k == "R01" else 16
            for a in range(RELU.get(k, 0), end, 4):
                weigh(k, a, min(end, a + 4))
        if k == "R01":
            part[0] = "F"
            late()
            weigh(k, 14, 16)
            part[0] = "H" + k
        if PART.get(k, 16):
            total(k, [(0, 7, 7), (0, 4, 3), (0, 2, 2), (0, 14, 2), (0, 1, 1)] if k == "R01" else halves[:HALVE.get(k, 4)])
        if k[0] == "R":
            m, w = int(k[1]), 128 * len(SETS[k])
            if k in PART:
                rest(k, m, w)
            else:
                store("yz%d" % m, T.yz[:, 128 * m:128 * m + w], result(T, k) if k in FOLD else T["A" + k][:, 0, :, :],
                      [x for u in SETS[k] for x in summed(u)[1]], 7 + m)
    part[0] = "M"
    for m in range(7):
        mixture(m)
    return ops, bank


def depend(ops):
    lw, rs = {}, {}
    for k, o in enumerate(ops):
        d = set()
        for x in o["rd"]:
            d.add(lw[x])
        for x in o["wr"]:
            if x in lw:
                d.add(lw[x])
            d.update(rs.get(x, []))
        d.discard(k)
        same = set(x for x in d if o["eng"] == "p" and ops[x]["eng"] == "p" and o["wr"] == ops[x]["wr"])
        o["dep"] = d - same
        o["lag"] = [(x, 0.0 if x in same else ops[x]["lat"]) for x in sorted(d)]
        for x in o["rd"]:
            rs.setdefault(x, []).append(k)
        for x in o["wr"]:
            lw[x] = k
            rs[x] = []


def bundles(ops):
    n = len(ops)
    users = [[] for o in ops]
    rels = {}
    for k, o in enumerate(ops):
        for d, lag in o["lag"]:
            users[d].append(k)
        if o["rel"]:
            rels.setdefault(o["rel"], []).append(k)
    own = list(range(n))
    for k, o in enumerate(ops):
        if o["acq"]:
            last = max(rels[o["acq"][0]])
            down, up = {k}, set(rels[o["acq"][0]])
            for x in range(k + 1, last + 1):
                if any(d in down for d, lag in ops[x]["lag"]):
                    down.add(x)
            for x in range(last, k - 1, -1):
                if any(y in up for y in users[x]):
                    up.add(x)
            for x in down & up:
                own[x] = k
    members = {}
    for k in range(n):
        members.setdefault(own[k], []).append(k)
    pre = {u: set(own[d] for x in members[u] for d, lag in ops[x]["lag"]) - {u} for u in members}
    post = {u: [x for x in pre if u in pre[x]] for u in members}
    inner = {k: [(x, lag) for x in users[k] if own[x] == own[k] for d, lag in ops[x]["lag"] if d == k] for k in range(n)}
    return members, pre, post, rels, inner


def plan(ops, C, bun, key, eng):
    members, pre, post, rels, inner = bun
    n = len(ops)
    cost = [o["cost"] for o in ops]
    lags = [o["lag"] for o in ops]
    st, fin = [0.0] * n, [0.0] * n
    busy = {e: ([], []) for e in eng}
    held = [[] for b in range(8)]
    banks = {}
    wait = {u: len(pre[u]) for u in pre}
    ready = [u for u in wait if not wait[u]]

    def find(b, t):
        lo, hi = 0, len(b)
        while lo < hi:
            mid = (lo + hi) // 2
            if b[mid] <= t:
                lo = mid + 1
            else:
                hi = mid
        return lo

    def put(k, t):
        for d, lag in lags[k]:
            if fin[d] + lag > t:
                t = fin[d] + lag
        a, b = busy[eng[k]]
        c = cost[k]
        j = find(b, t)
        while j < len(a) and a[j] < t + c:
            t = b[j]
            j += 1
        a.insert(j, t)
        b.insert(j, t + c)
        st[k], fin[k] = t, t + c

    def take(k):
        a, b = busy[eng[k]]
        j = a.index(st[k])
        del a[j], b[j]
    while ready:
        u = max(ready, key=key.get)
        ready.remove(u)
        ms = members[u]
        if len(ms) == 1:
            put(u, 0.0)
        else:
            h, w = ops[u]["acq"]
            t = 0.0
            while True:
                for k in ms:
                    put(k, t)
                for k in ms[-2::-1]:
                    c = cost[k]
                    end = min([st[x] - lag for x, lag in inner[k]] or [0.0])
                    if end - c > st[k] + 1.0:
                        old = st[k]
                        take(k)
                        a, b = busy[eng[k]]
                        j = find(a, end - 1e-6)
                        while j and b[j - 1] > end - c + 1e-6:
                            end = min(end, a[j - 1])
                            j -= 1
                        put(k, max(old, end - c - 1e-6))
                s, e = st[u], max(fin[k] for k in ms) + C["lat"]
                clash = [min([y for x, y, z in held[q] if x < e and y > s] or [0.0]) for q in range(8)]
                fit = [q for q in range(0, 8, w) if not max(clash[q:q + w])]
                if fit:
                    q = fit[0] if w == 2 else max(fit, key=lambda x: (clash[x ^ 1] > 0, x))
                    banks[h] = q
                    for x in range(q, q + w):
                        held[x].append((s, e, u))
                    break
                for k in ms:
                    take(k)
                t = max(t + 1.0, min(x for x in clash if x))
        for x in post[u]:
            wait[x] -= 1
            if not wait[x]:
                ready.append(x)
    extra = {}
    for q in range(8):
        hs = sorted(held[q])
        for a, b in zip(hs, hs[1:]):
            extra.setdefault(b[2], []).extend(rels[ops[a[2]]["acq"][0]])
    return sorted(range(n), key=lambda k: (st[k], k)), banks, extra, fin, eng


def replay(ops, p, C):
    fin, free = [0.0] * len(ops), {}
    extra, eng = p[2], p[4]
    for k in p[0]:
        o = ops[k]
        t = free.get(eng[k], 0.0)
        for d, lag in o["lag"]:
            if fin[d] + lag > t:
                t = fin[d] + lag
        for d in extra.get(k, ()):
            if fin[d] + C["lat"] > t:
                t = fin[d] + C["lat"]
        fin[k] = free[eng[k]] = t + o["cost"]
    return max(fin) + C["dma"]


def search(T, topo, core, rounds, seed0=12345):
    sets = []
    for ch in VARY:
        C = dict(COST)
        C.update(ch)
        ops = build(T, topo, core, C)[0]
        depend(ops)
        sets.append((ops, C))
    ops, C = sets[0]
    n = len(ops)
    bun = bundles(ops)
    members = bun[0]
    units = sorted(members)
    parts = {}
    for u in units:
        parts.setdefault(ops[u]["part"], []).append(u)
    names = sorted(parts)
    free = [k for k in range(n) if ops[k]["eng"] == "vs"]
    tail = [0.0] * n
    for k in range(n - 1, -1, -1):
        tail[k] = max(tail[k], BOOST.get(ops[k]["part"], 0.0)) + ops[k]["cost"]
        for d, lag in ops[k]["lag"]:
            tail[d] = max(tail[d], tail[k] + lag)
    load = [o["cost"] if o["eng"] in "vsp" else 0.0 for o in ops]
    seed = [seed0]

    def rnd():
        seed[0] = (seed[0] * 1103515245 + 12345) % 2147483648
        return (seed[0] >> 8) / 8388608.0

    def value(key, eng):
        p = plan(ops, C, bun, key, eng)
        r = [replay(o, p, c) / c["norm"] for o, c in sets]
        return (r[0] + sum(r)) / (len(r) + 1) + SOFT * sum(c * f for c, f in zip(load, p[3])) / sum(load), p, r
    eng = [("s" if o["name"] in ONS else "v") if o["eng"] == "vs" else o["eng"] for o in ops]
    now = best = value({u: max(tail[x] for x in members[u]) for u in units}, eng)
    for j in range(rounds):
        fin, eng = now[1][3], list(now[1][4])
        key = {u: ops[u]["cost"] - fin[u] for u in units}
        if rnd() < 0.25:
            for z in range(1 + int(rnd() * 2)):
                k = free[int(rnd() * len(free))]
                eng[k] = "s" if eng[k] == "v" else "v"
        else:
            for z in range(1 + int(rnd() * 2)):
                d = (rnd() + rnd() - 1.0) * (1500.0, 5000.0, 15000.0)[int(rnd() * 3)]
                for u in (parts[names[int(rnd() * len(names))]] if rnd() < 0.3 else [units[int(rnd() * len(units))]]):
                    key[u] += d
        v = value(key, eng)
        if v[0] <= now[0] or rnd() < math.exp(max(-50.0, (now[0] - v[0]) / (HEAT * (1.0 - j / rounds)))):
            now = v
            if v[0] < best[0]:
                best = v
    return best


def improve(T, topo, core, p, rounds, seed0, HEAT2, SOFT2, lead=2.0):
    data = []
    for j, ch in enumerate(VARY):
        C = dict(COST)
        C.update(ch)
        ops = build(T, topo, core, C)[0]
        depend(ops)
        data.append(([o["cost"] for o in ops], [o["lag"] for o in ops], C["lat"], C["dma"], (1.0 if j else lead) / C["norm"] / (len(VARY) - 1 + lead)))
    n = len(ops)
    order, eng, bank = list(p[0]), list(p[4]), dict(p[1])
    pred = [[d for d, lag in o["lag"]] for o in ops]
    succ = [[] for o in ops]
    rels = {}
    for k, o in enumerate(ops):
        for d in pred[k]:
            succ[d].append(k)
        if o["rel"]:
            rels.setdefault(o["rel"], []).append(k)
    acq = {o["acq"][0]: (k, o["acq"][1]) for k, o in enumerate(ops) if o["acq"]}
    load = [c if o["eng"] in "vsp" else 0.0 for c, o in zip(data[0][0], ops)]
    holds = set(k for k, o in enumerate(ops) if o["acq"] or o["rel"])
    seed = [seed0]

    def rnd():
        seed[0] = (seed[0] * 1103515245 + 12345) % 2147483648
        return (seed[0] >> 8) / 8388608.0

    def chain(order, bank):
        pos = [0] * n
        for j, k in enumerate(order):
            pos[k] = j
        on = [[] for b in range(8)]
        for h, (k, w) in acq.items():
            for b in range(bank[h], bank[h] + w):
                on[b].append((pos[k], max(pos[r] for r in rels[h]), h))
        extra = {}
        for b in range(8):
            on[b].sort()
            for x, y in zip(on[b], on[b][1:]):
                if x[1] > y[0]:
                    return None, y[2], on
                extra.setdefault(acq[y[2]][0], []).extend(rels[x[2]])
        return extra, None, on

    def value(order, eng, extra, a=0, old=None, limit=1e30):
        v, res = 0.0, []
        first = dict.fromkeys(eng, -1)
        for k in order[:a]:
            first[eng[k]] = k
        rest = order[a:]
        for j, (cost, lags, lat, dma, wt) in enumerate(data):
            if j == 1 and old and (max(res[0][0]) - max(old[0][0])) * data[0][4] > limit:
                return None, None
            fin, why, last = (old[j][0][:], old[j][1][:], dict(first)) if old else ([0.0] * (n + 1), [-1] * n, dict(first))
            for k in rest:
                w = last[eng[k]]
                t = fin[w]
                for d, lag in lags[k]:
                    if fin[d] + lag > t:
                        t = fin[d] + lag
                        w = d
                if k in extra:
                    for d in extra[k]:
                        if fin[d] + lat > t:
                            t = fin[d] + lat
                            w = d
                fin[k] = t + cost[k]
                why[k] = w
                last[eng[k]] = k
            v += (max(fin) + dma) * wt
            res.append((fin, why))
        return v + SOFT2 * sum(c * f for c, f in zip(load, res[0][0])) / sum(load), res
    extra = chain(order, bank)[0]
    now, res = value(order, eng, extra)
    best = (now, order, bank, extra, res, eng)
    for it in range(rounds):
        fin, why = res[int(rnd() * len(res))]
        path = []
        k = fin.index(max(fin)) if rnd() < 0.7 else int(rnd() * n)
        while k >= 0:
            path.append(k)
            k = why[k]
        k = path[int(rnd() * len(path))]
        o2, e2, b2 = order, eng, bank
        start = order.index(k)
        r = rnd()
        if ops[k]["eng"] == "vs" and r < 0.3:
            e2 = list(eng)
            e2[k] = "s" if eng[k] == "v" else "v"
        if ops[k]["acq"] and r < 0.2:
            h, w = ops[k]["acq"]
            b2 = dict(bank)
            b2[h] = int(rnd() * 8) // w * w
        elif e2 is eng or r < 0.2:
            j = why[k]
            up = rnd() < 0.7
            if e2 is eng and j >= 0 and eng[j] == eng[k] and j not in pred[k] and rnd() < 0.5:
                k, up = j, False
            at = to = order.index(k)
            step, link = (-1, succ) if up else (1, pred)
            hop = 1 + int(rnd() ** 4 * HOP)
            x = at + step
            while hop and 0 <= x < n:
                if eng[order[x]] == e2[k]:
                    to = x
                    hop -= 1
                x += step
            group = {k}
            for x in range(at + step, to + step, step):
                if not group.isdisjoint(link[order[x]]):
                    group.add(order[x])
            if order[to] in group:
                continue
            a, b = min(at, to), max(at, to) + 1
            start = a
            ins, out = [x for x in order[a:b] if x in group], [x for x in order[a:b] if x not in group]
            o2 = order[:a] + (ins + out if up else out + ins) + order[b:]
        x2, bad, on = chain(o2, b2) if b2 is not bank or (o2 is not order and not group.isdisjoint(holds)) else (extra, None, None)
        for tries in range(3):
            if x2 is not None:
                break
            w = acq[bad][1]
            y = [x for x in on[b2[bad]] if x[2] == bad][0]
            fit = [b for b in range(0, 8, w) if not any(x[0] < y[1] and y[0] < x[1] and x[2] != bad for q in range(b, b + w) for x in on[q])]
            if not fit:
                break
            b2 = dict(b2)
            b2[bad] = fit[int(rnd() * len(fit))]
            x2, bad, on = chain(o2, b2)
        if x2 is None:
            continue
        if x2 is not extra:
            for x in set(x2) | set(extra):
                if x2.get(x) != extra.get(x):
                    start = min(start, o2.index(x))
        room = -HEAT2 * (1.0 - it / rounds) * math.log(1e-9 + rnd())
        v, r2 = value(o2, e2, x2, start, res, room + 150.0)
        if v is not None and v <= now + room:
            cost, f0 = data[0][0], r2[0][0]
            order = sorted(o2, key=lambda k: f0[k] - cost[k])
            now, res, eng, bank, extra = v, r2, e2, b2, x2
            if v < best[0]:
                best = (v, order, bank, extra, res, eng)
    return best[0], (best[1], best[2], best[3], best[4][0][0], best[5]), [max(f) + d[3] for (f, w), d in zip(best[4], data)]


PLAN = {}


def hand_back(g, core, T, topo):
    for r in T.cores:
        hs = helpers(T, topo, r)
        if core in hs:
            rid, pid = topo.addr(r, core)
            sent = 0
            for k in FOLD[hs.index(core)::len(hs)]:
                g.wait_ge(T.sem["f" + k], len(topo.engines(r, core)))
                g.remote_dma(result(T, k), result(T, k), T.sem["b" + k], T.sem.sent, pid, rid, topo.mask(core, r))
                sent += len(topo.engines(core, r))
            if sent:
                g.wait_ge(T.sem.sent, sent)


def rank_program(g, core, T, topo):
    if T.rank_of(core) is None:
        hand_back(g, core, T, topo)
        return
    ops, bank = build(T, topo, core, COST)
    depend(ops)
    if not PLAN:
        p = search(T, topo, core, ROUNDS, 8)[1]
        for rounds, heat, soft, lead in STAGES:
            p = improve(T, topo, core, p, rounds, 3, heat, soft, lead)[1]
        PLAN["p"] = p
    order, banks, extra, fin, eng = PLAN["p"]
    bank.update(banks)
    Q = {"v": g.vector, "s": g.scalar, "p": g.tensor, "g": g, "y": g.sync}
    total = {s: 0 for s in SEMAPHORES}
    mark, seen = {}, {}
    for k in order:
        o = ops[k]
        if o["kind"] == "w":
            total[o["sem"]] = o["fn"]
            mark[k] = (o["sem"], o["fn"])
            continue
        if o["kind"] == "e":
            mark[k] = mark[o["fn"]]
            continue
        q = Q[eng[k]]
        need = {}
        for d in list(o["dep"]) + extra.get(k, []):
            s, v = mark[d]
            need[s] = max(need.get(s, 0), v)
        for s, v in sorted(need.items()):
            if seen.get((eng[k], s), 0) < v:
                q.wait_ge(T.sem[s], v)
                seen[(eng[k], s)] = v
        if o["kind"] == "r":
            total["sent"] += o["fn"](q)
            mark[k] = ("sent", 0)
            continue
        s, inc = (o["sem"], 16) if o["kind"] == "d" else (CSEM[eng[k]], 1)
        for ins in (o["fn"](q, eng[k]) if o["eng"] == "vs" else o["fn"](q)):
            ins.then_inc(T.sem[s], inc)
            total[s] += inc
        mark[k] = (s, total[s])
    for s in SEMAPHORES:
        if total[s]:
            g.wait_ge(T.sem[s], total[s])
